import numpy as np, ml_dtypes
CORES = [2,3,42,43,82,83,122,123]
N = 8
BF = ml_dtypes.bfloat16
def f(rng, *shape):
    return (rng.standard_normal(shape, dtype=np.float32) * np.exp2(rng.integers(-2, 3, shape[:-1] + (1,)))).astype(BF)
def wide(rng, *shape):
    v = f(rng, *shape).astype(np.float32); k = shape[:-2] + (1, shape[-1])
    return (v * np.exp2(rng.integers(-6, 7, k)) * (rng.random(k) > 0.0625)).astype(BF)
def gentries(a):
    return np.ascontiguousarray(a.reshape(8, 16, -1).transpose(0, 2, 1)).reshape(8, -1)
def gtable(e):
    e = np.asarray(e); return np.ascontiguousarray(e.reshape(8, -1, 16).transpose(0, 2, 1)).reshape(128, -1).astype(np.int32)
L, M, S0, R = 2048, 8192, 10, 4
S = 16
def tame(v):
    u = np.minimum(np.maximum(v.astype(np.float32), np.float32(-960)), np.float32(960))
    return np.where(np.abs(u) < np.float32(2.0 ** -16), np.float32(0), u).astype(BF)
def speech(rng):
    q = 2.0 ** (-0.4 * rng.permutation(24)); ks = rng.integers(2, 7, 24); ks[np.argmax(q)] = 5
    W = [rng.permutation(S0)[:k] for k in ks]; w = np.zeros((N, 8, L), np.int64)
    for r in range(N):
        acc = np.add.accumulate(q * 2.0 ** rng.integers(-1, 2, 24))
        for g in range(8):
            i = np.minimum(np.searchsorted(acc, rng.random(L // 2) * acc[-1], side="right"), 23)
            v = np.concatenate([W[j] for j in i])[:L]; w[r, g] = np.where(rng.random(L) < 0.1, rng.integers(0, S0, L), v)
    return w
def lengths(rng):
    le = rng.integers(L // 2, L + 1, (N, 8)); le[rng.integers(0, N), rng.integers(0, 8)] = L
    return le
def plant(rng, w, le):
    r = rng.integers(0, len(w)); w[r, np.argmax(le[r]), :S0] = rng.permutation(S0)
def make(rng, w, le):
    st = np.zeros((N, 8, M), np.int32); ps = np.zeros((N, 8, L), np.int64)
    for r in range(N):
        for g in range(8):
            v = rng.permutation(np.concatenate((np.arange(S0), rng.integers(0, S0, M - S0)))); o = np.argsort(v, kind="stable")
            c = np.bincount(v, minlength=S0); first = np.add.accumulate(c) - c
            st[r, g] = v; ps[r, g] = o[first[w[r, g]] + rng.integers(0, c[w[r, g]])]
    return {"ve": tame(f(rng, N, 128, M)), "st": st, "pos": np.stack([gtable(p) for p in ps]), "le": le.reshape(N, 8, 1).astype(np.int32)}
def setup_inputs(rng):
    w, le = speech(rng), lengths(rng); plant(rng, w, le); return make(rng, w, le)
def setup_inputs_ends(rng):
    w, le = speech(rng), lengths(rng)
    for r in range(N): le[r, rng.permutation(8)[:4]] = np.array([0, 1, 2, L])
    ab = rng.permutation(S0)[:2]; v = w.reshape(N, 8, L // 2, 2); v[rng.random((N, 8, L // 2)) < 0.4] = ab; w = v.reshape(N, 8, L); w[:, :, :2] = ab
    for r in range(N):
        for g in range(8):
            if le[r, g] >= 2: w[r, g, le[r, g] - 2:le[r, g]] = ab
    plant(rng, w, le); d = make(rng, w, le)
    d["pos"][:, 8::16, 2] = 0; d["pos"][:, 9::16, 2] = M - 1; return d
def setup_inputs_ties(rng):
    w, le = speech(rng)[:N // 2], lengths(rng)[:N // 2]; plant(rng, w, le)
    return make(rng, np.concatenate((w, w ^ 1)), np.concatenate((le, le)))
def setup_inputs_few(rng):
    w = speech(rng); le = rng.integers(0, 2, (N, 8)); r, q = rng.permutation(N)[:2]; g = rng.integers(0, 8); le[q] = 0; le[q, (g + 3) % 8] = 1; le[r, g] = S0 + 2
    p = 1 + rng.permutation(S0 - 1); w[r, g, :S0 + 2] = np.concatenate((p[:1], [0], p[1:], [0], p[:1])); return make(rng, w, le)
def setup_inputs_loop(rng):
    W = [rng.permutation(S0)[:k] for k in range(2, 8)]; le = lengths(rng); w = np.zeros((N, 8, L), np.int64)
    for r in range(N):
        for g, i in enumerate(rng.permutation(np.array([0, 1, 2, 2, 3, 4, 5, 5]))): w[r, g] = W[i][(np.arange(L) + rng.integers(0, 8)) % len(W[i])]
    plant(rng, w, le); return make(rng, w, le)
def setup_inputs_spread(rng):
    w = np.stack([np.stack([np.repeat(rng.integers(0, S0, L), rng.integers(1, 40, L))[:L] for g in range(8)]) for r in range(N)])
    le = np.maximum(np.floor(L * rng.random((N, 8)) ** 4).astype(np.int64), 1); le[np.arange(N), rng.integers(0, 8, N)] = L
    plant(rng, w, le); d = make(rng, w, le); d["ve"] = tame(wide(rng, N, 128, M)); return d
def rounds(st, pos, le):
    s, pl = [], []
    for r in range(N):
        P = gentries(pos[r]).astype(np.int64)
        for g in range(8):
            p = P[g, :int(le[r, g, 0])]; pl.append(p); s.append(st[r, g][p].astype(np.int64))
    mg = np.zeros((R, 3), np.float32)
    for t in range(R):
        h = np.zeros(S * S, np.int64)
        for v in s: h += np.bincount((v[:-1] * S + v[1:])[v[:-1] != v[1:]], minlength=S * S)
        k = int(np.argmax(h)); a = k // S; b = k - S * a; mg[t] = a, b, h[k]
        for i in range(len(s)):
            v = s[i]; hit = np.zeros(v.size, bool); hit[:-1] = (v[:-1] == a) & (v[1:] == b)
            keep = np.ones(v.size, bool); keep[1:] = ~hit[:-1]
            s[i] = np.where(hit, S0 + t, v)[keep]; pl[i] = pl[i][keep]
    return s, pl, mg
def check_inputs(d):
    try:
        bad = []
        if not np.isfinite(d["ve"].astype(np.float32)).all(): bad.append("ve is finite")
        if d["st"].min() < 0 or d["st"].max() >= S0: bad.append("st is 0 to S0 - 1")
        if d["pos"].min() < 0 or d["pos"].max() >= M: bad.append("pos is 0 to M - 1")
        if d["le"].min() < 0 or d["le"].max() > L: bad.append("le is 0 to L")
        if not bad and rounds(d["st"], d["pos"], d["le"])[2][:, 2].min() < 1: bad.append("a pair is left in every round")
        return bad
    except Exception:
        return ["shapes"]
def reference(ve, st, pos, le):
    s, pl, mg = rounds(st, pos, le)
    y = np.zeros((N, 128, L), BF); fs = np.full((N, 8, L), -1, np.float32); fl = np.zeros((N, 8, 1), np.float32)
    for r in range(N):
        for g in range(8):
            v, p = s[8 * r + g], pl[8 * r + g]; fl[r, g, 0] = v.size; fs[r, g, :v.size] = v
            y[r, 16 * g:16 * g + 16, :v.size] = ve[r, 16 * g:16 * g + 16][:, p]
    return {"y": y, "fs": fs, "fl": fl, "mg": np.tile(mg, (N, 1, 1))}

@@ -1,0 +1,358 @@
+from concourse.bass import DstId, RemoteDMATransfer
+from concourse.mybir import AluOpType as A, AxisListType as AX, ActivationFunctionType as AF
+
+W = 152
+PITCH = 136
+R = 4
+S0 = 10
+NR = 8
+M31 = 1.5 * 2.0 ** 31
+M23 = 1.5 * 2.0 ** 23
+
+f32, bf, f16, i32, u16 = "float32", "bfloat16", "float16", "int32", "uint16"
+SCRATCH = {
+    "posi": ("sbuf", [128, 128], i32), "stw": ("sbuf", [128, 512], i32), "lei": ("sbuf", [128, 4], i32),
+    "vew": ("sbuf", [128, 8192], bf), "tmpi": ("sbuf", [128, 256], i32),
+    "hiu": ("sbuf", [128, 128], u16), "lou": ("sbuf", [128, 128], u16), "pou": ("sbuf", [128, 128], u16),
+    "offu": ("sbuf", [128, 128], u16),
+    "pin": ("sbuf", [128, 8], i32), "pf": ("sbuf", [128, 16], f32), "lef": ("sbuf", [128, 4], f32),
+    "nid": ("sbuf", [128, W], f32), "n15": ("sbuf", [128, 128], bf), "n7": ("sbuf", [128, 128], bf),
+    "n3": ("sbuf", [128, 128], bf), "n4": ("sbuf", [128, 128], bf),
+    "tm": ("sbuf", [128, 16], bf), "big": ("sbuf", [128, 144], bf), "idn": ("sbuf", [128, 144], bf),
+    "sel": ("sbuf", [128, 16], f16), "rep": ("sbuf", [128, 128], f16), "cst": ("sbuf", [128, 16], f16),
+    "dm": ("sbuf", [128, 128], bf), "dm2": ("sbuf", [128, 128], bf), "g8": ("sbuf", [128, 128], f32),
+    "tri": ("sbuf", [128, 128], f32), "tri2": ("sbuf", [128, 128], f32), "gsel": ("sbuf", [128, 8], f32),
+    "jj": ("sbuf", [128, W], f32), "jt": ("sbuf", [128, W], f32), "inv": ("sbuf", [128, W], bf),
+    "val": ("sbuf", [128, 128], bf), "tt": ("sbuf", [128, 128], f32),
+    "mk": ("sbuf", [128, 2048], bf), "xx": ("sbuf", [128, 2072], bf), "oh": ("sbuf", [128, 13 * PITCH + 8], bf),
+    "mm": ("sbuf", [128, 128], f16), "pay": ("sbuf", [128, 16 * R], f16), "land": ("sbuf", [128, 16 * NR * R], f16),
+    "neg": ("sbuf", [128, 128], bf), "low": ("sbuf", [128, 48], f32),
+    "sc": ("sbuf", [128, 48], f32), "tr": ("sbuf", [128, 32], f32),
+    "kk": ("sbuf", [128, 4], f32), "rr": ("sbuf", [128, 4], f32),
+    "fo": ("sbuf", [128, W], bf), "fm": ("sbuf", [128, W], bf), "m1": ("sbuf", [128, W], bf),
+    "alv": ("sbuf", [128, W], bf), "ded": ("sbuf", [128, W], bf), "t16": ("sbuf", [128, W], bf),
+    "cd": ("sbuf", [128, W], bf), "d1": ("sbuf", [128, W], bf),
+    "pc": ("sbuf", [128, 2 * W], bf), "ne": ("sbuf", [128, 2 * W], bf),
+    "av": ("sbuf", [128, 128], bf), "aa": ("sbuf", [128, 128], bf), "ss": ("sbuf", [128, 128], f32),
+    "mt": ("sbuf", [128, 128], f32), "zz": ("sbuf", [128, 128], f32),
+    "y0": ("sbuf", [128, 2048], bf), "yw": ("sbuf", [128, 4096], bf),
+    "v0": ("sbuf", [128, 2048], f32), "fw": ("sbuf", [128, 4096], f32),
+    "ft": ("sbuf", [128, 128], f32), "fa": ("sbuf", [128, 128], f32), "fb": ("sbuf", [128, 128], f32),
+    "fc": ("sbuf", [128, 128], f32),
+    "mgs": ("sbuf", [128, 12], f32), "mt4": ("sbuf", [128, 16], f32), "fls": ("sbuf", [128, 4], f32),
+    "p1": ("psum", [128, 512], f32), "p2": ("psum", [128, 512], f32), "p3": ("psum", [128, 512], f32),
+    "pb": ("psum", [128, 512], f32), "e0": ("psum", [128, 512], f32), "e1": ("psum", [128, 512], f32),
+    "e2": ("psum", [128, 512], f32), "e3": ("psum", [128, 512], f32),
+}
+PSUM = ("p1", "p2", "p3", "pb", "e0", "e1", "e2", "e3")
+SEMAPHORES = (["cv", "ca", "cp", "cg", "dpos", "dst", "dle", "dve", "dft", "dout", "dout2", "sent"]
+              + ["ar%d_%d" % (t, s) for t in range(R) for s in range(NR)])
+
+
+def rank_program(g, core, T, topo):
+    rank = T.rank_of(core)
+    if rank is None:
+        return
+    Q = {"v": g.vector, "a": g.scalar, "p": g.tensor, "g": g, "s": g.sync}
+    CS = {"v": "cv", "a": "ca", "p": "cp", "g": "cg"}
+    count = {k: 0 for k in SEMAPHORES}
+    seen = {e: {} for e in Q}
+    wrote, read = {}, {}
+
+    def need(e, toks):
+        top = {}
+        for s, n in toks:
+            if n > top.get(s, 0):
+                top[s] = n
+        for s, n in top.items():
+            if e == "p" and s == "cp":
+                continue
+            if seen[e].get(s, 0) < n:
+                Q[e].wait_ge(T.sem[s], n)
+                seen[e][s] = n
+
+    def order(e, r, w):
+        toks = [wrote[k] for k in list(r) + list(w) if k in wrote]
+        for k in w:
+            toks += read.get(k, [])
+        for k in r:
+            if k in PSUM:
+                toks += [x for x in read.get(k, []) if x[0] != CS.get(e)]
+        need(e, toks)
+
+    def note(tok, r, w):
+        for k in r:
+            read.setdefault(k, []).append(tok)
+        for k in w:
+            wrote[k] = tok
+            read[k] = []
+
+    def op(e, fn, r, w):
+        order(e, r, w)
+        s = CS[e]
+        fn().then_inc(T.sem[s], 1)
+        count[s] += 1
+        note((s, count[s]), r, w)
+
+    def dma(e, sem, out, in_, r, w):
+        order(e, r, w)
+        Q[e].dma_start(out, in_).then_inc(T.sem[sem], 16)
+        count[sem] += 16
+        note((sem, count[sem]), r, w)
+
+    V, S, P = g.vector, g.scalar, g.tensor
+
+    def ts(out, in0, s1, s2, o0, o1, r, w):
+        if o1 is None:
+            op("v", lambda: V.tensor_scalar(out, in0, s1, None, o0), r, w)
+        else:
+            op("v", lambda: V.tensor_scalar(out, in0, s1, s2, o0, o1), r, w)
+
+    def tt(out, in0, in1, o, r, w):
+        op("v", lambda: V.tensor_tensor(out, in0, in1, o), r, w)
+
+    def cp(out, in_, r, w):
+        op("v", lambda: V.tensor_copy(out, in_), r, w)
+
+    def ms(out, c, w):
+        op("v", lambda: V.memset(out, c), [], w)
+
+    def scan(out, d0, d1, init, o0, o1, r, w):
+        op("v", lambda: V.tensor_tensor_scan(out, d0, d1, init, o0, o1), r, w)
+
+    def mm(out, l, rh, st, sp, r, w):
+        op("p", lambda: P.matmul(out, l, rh, st, sp), r, w)
+
+    def io(out, pat, cm, w, small=True):
+        if small:
+            op("g", lambda: g.iota(out, pat, 0, cm, allow_small_or_imprecise_dtypes=True), [], w)
+        else:
+            op("g", lambda: g.iota(out, pat, 0, cm), [], w)
+
+    dma("s", "dpos", T.posi[:], T.pos[:], [], ["posi"])
+    dma("a", "dst", T.stw[:], T.st[:], [], ["stw"])
+    dma("s", "dle", T.lei[0:8, 0:1], T.le[:], [], ["lei"])
+    dma("s", "dve", T.vew[:], T.ve[:], [], ["vew"])
+
+    io(T.pin[:, 0:1], [[0, 1]], 1, ["pin0"], small=False)
+    io(T.nid[:], [[1, W]], 0, ["nid"])
+    io(T.n4[:], [[1, 8], [0, 16]], 0, ["n4"])
+    io(T.n15[:], [[0, 8], [1, 16]], 0, ["n15"])
+    io(T.n7[:], [[0, 16], [1, 8]], 0, ["n7"])
+    io(T.n3[:], [[1, 16], [0, 8]], 0, ["n3"])
+    OH = ["oh%d" % x for x in range(13)]
+    ms(T.oh[:], 0.0, OH)
+    ms(T.xx[:, 0:8], 0.0, ["xpad0"])
+    ms(T.xx[:, 2056:2072], 0.0, ["xpad1"])
+    p0 = T.pin[:, 0:1]
+    ts(T.pin[:, 1:2], p0, 15, None, A.bitwise_and, None, ["pin0"], ["pin1"])
+    ts(T.pin[:, 2:3], p0, 4, None, A.arith_shift_right, None, ["pin0"], ["pin2"])
+    ts(T.pin[:, 3:4], p0, 3, None, A.arith_shift_right, None, ["pin0"], ["pin3"])
+    ts(T.pin[:, 4:5], p0, 7, None, A.bitwise_and, None, ["pin0"], ["pin4"])
+    ts(T.pin[:, 5:6], p0, 112, None, A.bitwise_and, None, ["pin0"], ["pin5"])
+    cp(T.pf[:, 0:6], T.pin[:, 0:6], ["pin%d" % i for i in range(6)], ["pf"])
+    fP, fR, fG, fP3, fP7, fG16 = [T.pf[:, i:i + 1] for i in range(6)]
+    ts(T.tm[:], T.nid[:, 0:16], fR, None, A.is_equal, None, ["nid", "pf"], ["tm"])
+    ts(T.big[:], T.nid[:, 0:144], -15.0, fG16, A.add, A.is_equal, ["nid", "pf"], ["big"])
+    ts(T.pf[:, 6:7], fR, 128.0, None, A.mult, None, ["pf"], ["pf6"])
+    ts(T.g8[0:8, :], T.n4[0:8, :], T.pf[0:8, 0:1], None, A.is_equal, None, ["n4", "pf"], ["g8"])
+    ts(T.jj[:], T.nid[:], T.pf[:, 6:7], -8.0, A.add, A.add, ["nid", "pf6"], ["jj"])
+    ts(T.pf[:, 7:8], fP3, 156.0, -1.0 / 2048, A.add, A.mult, ["pf"], ["pf7"])
+    ts(T.jt[:], T.jj[:], 0.0, 8192.0, A.is_lt, A.mult, ["jj"], ["jt"])
+    tt(T.jt[:], T.jt[:], T.jj[:], A.add, ["jt", "jj"], ["jt"])
+
+    ts(T.tmpi[:, 0:128], T.posi[:], 9, None, A.arith_shift_right, None, ["posi"], ["tmp0"])
+    ts(T.tmpi[:, 128:256], T.posi[:], 511, None, A.bitwise_and, None, ["posi"], ["tmp1"])
+    cp(T.hiu[:], T.tmpi[:, 0:128], ["tmp0"], ["hiu"])
+    cp(T.lou[:], T.tmpi[:, 128:256], ["tmp1"], ["lou"])
+    NC = 8
+    CW = 2048 // NC
+    for i in range(NC):
+        op("a", lambda: S.activation(T.mk[:, CW * i:CW * (i + 1)],
+                                     T.tm[:, 0:16].indirect(T.hiu[:, CW // 16 * i:CW // 16 * (i + 1)]), AF.Copy),
+           ["tm", "hiu"], ["mk%d" % i])
+    cp(T.lef[0:8, 0:1], T.lei[0:8, 0:1], ["lei"], ["lef"])
+    mm(T.pb[:, 0:1], T.g8[0:8, :], T.lef[0:8, 0:1], True, True, ["g8", "lef"], ["pb"])
+    ts(T.sel[:], T.nid[:, 0:16], fP3, None, A.is_equal, None, ["nid", "pf"], ["sel"])
+    ts(T.cst[:], T.nid[:, 0:16], -16.0 / 2048, T.pf[:, 7:8], A.mult, A.add, ["nid", "pf7"], ["cst"])
+    done_r = 0
+    for i in range(NC):
+        tt(T.xx[:, 8 + CW * i:8 + CW * (i + 1)],
+           T.stw[:, 0:512].indirect(T.lou[:, CW // 16 * i:CW // 16 * (i + 1)]),
+           T.mk[:, CW * i:CW * (i + 1)], A.mult, ["stw", "lou", "mk%d" % i], ["x%d" % i])
+        while done_r < 16 and (i == NC - 1 or 128 * done_r + 144 <= CW * (i + 1)):
+            r = done_r
+            mm(T.e0[:, 0:W], T.big[:, 15 - r:143 - r], T.xx[:, 128 * r:128 * r + W], r == 0, r == 15,
+               ["big", "xpad0", "xpad1"] + ["x%d" % k for k in range(i + 1)], ["e0"])
+            done_r += 1
+    ts(T.inv[:], T.jt[:], T.pb[:, 0:1], 15.0, A.is_ge, A.mult, ["jt", "pb"], ["inv"])
+    ts(T.dm[:], T.n7[:], fP7, None, A.is_equal, None, ["n7", "pf"], ["dm"])
+    ts(T.dm2[:], T.n3[:], fP3, None, A.not_equal, None, ["n3", "pf"], ["dm2"])
+    tt(T.fo[:], T.e0[:, 0:W], T.inv[:], A.max, ["e0", "inv"], ["fo"])
+
+    cores = list(T.cores)
+    chips = []
+    for c in cores:
+        if topo.chip(c) not in chips:
+            chips.append(topo.chip(c))
+    on = {ch: [c for c in cores if topo.chip(c) == ch] for ch in chips}
+
+    def far_of(c):
+        i = chips.index(topo.chip(c))
+        m = on[topo.chip(c)].index(c)
+        out = []
+        for d in range(1, len(chips)):
+            row = on[chips[(i + d) % len(chips)]]
+            out += [row[(m + k) % len(row)] for k in range(len(row))]
+        return out
+
+    far = far_of(core)
+    near = [c for c in on[topo.chip(core)] if c != core]
+    far_eng = [e for e in topo.engines(core, far[0]) if all(e in topo.engines(core, c) for c in far)]
+    near_eng = [e for e in topo.engines(core, near[0]) if e not in far_eng][0:4:2]
+    senders = [(c, len(near_eng)) for c in near]
+    senders += [(c, len(far_eng)) for c in sorted(far, key=lambda c: far_of(c).index(core))]
+
+    def did(c):
+        a = topo.addr(c)
+        return DstId(rid=a[0], pnc=a[1])
+
+    off = 0
+    for t in range(R):
+        NS = S0 + t
+        n8 = 8 * NS
+        for x in range(NS):
+            ts(T.oh[:, PITCH * x:PITCH * x + 129], T.fo[:, 7:136], float(x - off), None, A.is_equal, None,
+               ["fo"], ["oh%d" % x])
+        span = 17 * (n8 - 1) + 1
+        for k in range(17):
+            mm(T.p1[0:n8, 0:n8], T.oh[:, k:k + span:17], T.oh[:, k + 1:k + 1 + span:17], k == 0, k == 16, OH, ["p1"])
+        if t == 0:
+            tt(T.dm[:], T.dm[:], T.dm2[:], A.mult, ["dm", "dm2"], ["dm"])
+            ms(T.p2[:, 0:16], 0.0, ["p2"])
+            ms(T.p3[:, 16:48], -1.0e9, ["p3"])
+            ms(T.low[:], -1.0e9, ["low"])
+            ms(T.pc[:], 200.0, ["pcl", "pcr"])
+            cp(T.pou[:], T.posi[:], ["posi"], ["pou"])
+            ts(T.rep[:], T.n15[:], fP3, 256.0, A.is_equal, A.mult, ["n15", "pf"], ["rep"])
+        elif t == 1:
+            cp(T.alv[:], T.ne[:, 0:W], ["ne"], ["alv"])
+        else:
+            tt(T.alv[:], T.alv[:], T.ne[:, 0:W], A.mult, ["alv", "ne"], ["alv"])
+        ts(T.t16[:], T.fo[:], -16.0, 100.0 - 17 * off, A.mult, A.add, ["fo"], ["t16"])
+        if t > 0:
+            ts(T.ded[:], T.alv[:], -1.0, 1.0, A.mult, A.add, ["alv"], ["ded"])
+            tt(T.cd[:, 1:W], T.t16[:, 0:W - 1], T.fo[:, 1:W], A.subtract, ["t16", "fo"], ["cd"])
+            tt(T.d1[:, 1:W], T.cd[:, 1:W], T.alv[:, 1:W], A.mult, ["cd", "alv"], ["d1"])
+
+        tt(T.mm[0:n8, 0:n8], T.p1[0:n8, 0:n8], T.dm[0:n8, 0:n8], A.mult, ["p1", "dm"], ["mm"])
+        mm(T.p2[0:n8, 0:16], T.mm[0:n8, 0:n8], T.sel[0:n8, :], True, True, ["mm", "sel"], ["p2"])
+        pay = T.pay[:, 16 * t:16 * t + 16]
+        cp(pay, T.p2[:, 0:16], ["p2"], ["pay%d" % t])
+        slot = T.land[:, 16 * (NR * t + rank):16 * (NR * t + rank) + 16]
+        order("g", ["pay%d" % t], [])
+        sem = T.sem["ar%d_%d" % (t, rank)]
+        g.remote_dma_fused([
+            RemoteDMATransfer(dst_ids=[did(c) for c in far], dma_engine_mask=sum(1 << e for e in far_eng),
+                              remote_sem=sem, srcs=[pay], dsts=[slot for c in far]),
+            RemoteDMATransfer(dst_ids=[did(c) for c in near], dma_engine_mask=sum(1 << e for e in near_eng),
+                              remote_sem=sem, srcs=[pay], dsts=[slot for c in near]),
+        ], local_sem=T.sem.sent)
+        count["sent"] += len(far_eng) + len(near_eng)
+
+        if t == 0:
+            tt(T.pc[:, 1:W], T.t16[:, 0:W - 1], T.fo[:, 1:W], A.subtract, ["t16", "fo"], ["pcl"])
+            tt(T.pc[:, W:2 * W - 1], T.t16[:, 0:W - 1], T.fo[:, 1:W], A.subtract, ["t16", "fo"], ["pcr"])
+        else:
+            scan(T.pc[:, 2 * W - 2:W - 1:-1], T.ded[:, W - 1:0:-1], T.d1[:, W - 1:0:-1], 0.0, A.mult, A.add,
+                 ["ded", "d1"], ["pcr"])
+            scan(T.pc[:, 1:W], T.ded[:, 1:W], T.d1[:, 1:W], 0.0, A.mult, A.add, ["ded", "d1"], ["pcl"])
+        if t < R - 1:
+            ts(T.fm[:], T.fo[:], float(off - NS), None, A.add, None, ["fo"], ["fm"])
+        if t == 0:
+            ts(T.val[:], T.jt[:, 8:136], T.pb[:, 0:1], None, A.is_lt, None, ["jt", "pb"], ["val"])
+            ts(T.idn[:], T.nid[:, 0:144], fP, None, A.is_equal, None, ["nid", "pf"], ["idn"])
+            ts(T.tt[:], T.jj[:, 8:136], -1.0, 4096.0, A.mult, A.add, ["jj"], ["tt"])
+            ms(T.neg[:], -1.0, ["neg"])
+            for r in range(16):
+                op("a", lambda: S.activation(T.y0[:, r:2048:16], T.vew[:, 0:8192].indirect(T.pou[:, 8 * r:8 * r + 8]),
+                                             AF.Copy), ["vew", "pou"], ["y0_%d" % r])
+            op("a", lambda: S.activation(T.fw[:], T.vew[:, 0:4096], AF.Silu, scale=0.0), ["vew"], ["fw"])
+            op("a", lambda: S.activation(T.yw[:], T.vew[:, 0:4096], AF.Copy, scale=0.0), ["vew"], ["yw"])
+        if t == 1:
+            ts(T.tri[:], T.n4[:], fG, None, A.is_equal, None, ["n4", "pf"], ["tri"])
+            ts(T.tri2[:], T.nid[:, 0:128], fP, None, A.is_gt, None, ["nid", "pf"], ["tri2"])
+            ts(T.gsel[:], T.nid[:, 0:8], fG, None, A.is_equal, None, ["nid", "pf"], ["gsel"])
+            ts(T.pf[:, 8:9], T.tt[:, 127:128], -1.0, 1.0, A.mult, A.add, ["tt"], ["pf8"])
+            tt(T.tri[:], T.tri[:], T.tri2[:], A.mult, ["tri", "tri2"], ["tri"])
+        if t == R - 1:
+            tt(T.av[:], T.alv[:, 8:136], T.val[:], A.mult, ["alv", "val"], ["av"])
+            for b in range(4):
+                bank = "e%d" % b
+                for q in range(4):
+                    r = 4 * b + q
+                    mm(T[bank][:, 128 * q:128 * q + 128], T.idn[:, r:r + 128], T.pc[:, W + 8:W + 136], True, True,
+                       ["idn", "pcr"], [bank])
+                for q in range(4):
+                    r = 4 * b + q
+                    op("a", lambda: S.activation(T.v0[:, r:2048:16], T[bank][:, 128 * q:128 * q + 128], AF.Identity,
+                                                 bias=164.0, scale=-1.0), [bank], ["v0_%d" % r])
+            mm(T.pb[:, 1:2], T.tri[:], T.pf[:, 8:9], True, False, ["tri", "pf8"], ["pb"])
+
+        mm(T.p3[:, 0:16], T.rep[:], T.cst[:], True, False, ["rep", "cst"], ["p3"])
+        mm(T.p3[:, 0:16], T.rep[0:n8, :], T.pay[0:n8, 16 * t:16 * t + 16], False, False, ["pay%d" % t], ["p3"])
+        for i, (c, n) in enumerate(senders):
+            s = T.rank_of(c)
+            need("p", [("ar%d_%d" % (t, s), n)])
+            mm(T.p3[:, 0:16], T.rep[0:n8, :], T.land[0:n8, 16 * (NR * t + s):16 * (NR * t + s) + 16],
+               False, i == len(senders) - 1, [], ["p3"])
+        K, RK = T.kk[:, t:t + 1], T.rr[:, t:t + 1]
+        scan(T.sc[:], T.p3[:, 0:48], T.low[:], -1.0e9, A.max, A.max, ["p3", "low"], ["sc"])
+        op("v", lambda: V.transpose(T.tr[:], T.sc[:, 16:48]), ["sc"], ["tr"])
+        op("v", lambda: V.tensor_reduce(K, T.tr[:], AX.X, A.max), ["tr"], ["kk%d" % t])
+        ts(RK, K, M31, M31, A.add, A.subtract, ["kk%d" % t], ["rr%d" % t])
+        if t < R - 1:
+            ts(T.ne[:], T.pc[:], RK, K, A.add, A.not_equal, ["pcl", "pcr", "kk%d" % t, "rr%d" % t], ["ne"])
+            tt(T.m1[:], T.fm[:], T.ne[:, 0:W], A.mult, ["fm", "ne"], ["m1"])
+            tt(T.fo[:], T.m1[:], T.ne[:, W:2 * W], A.mult, ["m1", "ne"], ["fo"])
+            off = NS
+
+    K, RK = T.kk[:, 3:4], T.rr[:, 3:4]
+    ts(T.ne[:, 0:128], T.pc[:, 8:136], RK, K, A.add, A.not_equal, ["pcl", "kk3", "rr3"], ["ne"])
+    tt(T.aa[:], T.av[:], T.ne[:, 0:128], A.mult, ["av", "ne"], ["aa"])
+    scan(T.ss[:], T.aa[:], T.neg[:], T.tt[:, 0:1], A.add, A.add, ["aa", "neg", "tt"], ["ss"])
+    mm(T.pb[:, 1:2], T.tri[:], T.ss[:, 127:128], False, True, ["tri", "ss"], ["pb"])
+    tt(T.mt[:], T.aa[:], T.tt[:], A.mult, ["aa", "tt"], ["mt"])
+    tt(T.zz[:], T.ss[:], T.mt[:], A.subtract, ["ss", "mt"], ["zz"])
+    ts(T.offu[:], T.zz[:], T.pb[:, 1:2], None, A.add, None, ["zz", "pb"], ["offu"])
+    op("a", lambda: S.activation(T.fw[:, 0:4096].indirect(T.offu[:, 0:128]), T.v0[:], AF.Silu),
+       ["offu"] + ["v0_%d" % r for r in range(16)], ["fw"])
+    cp(T.yw[:, 0:4096].indirect(T.offu[:, 0:128]), T.y0[:], ["offu"] + ["y0_%d" % r for r in range(16)], ["yw"])
+    mm(T.pb[0:8, 2:3], T.gsel[:], T.ss[:, 127:128], True, True, ["gsel", "ss"], ["pb"])
+    dma("a", "dft", T.ft[:], T.fw[0:128:16, 0:2048], ["fw"], ["ft"])
+    dma("s", "dout", T.y[:], T.yw[:, 0:2048], ["yw"], [])
+
+    KR = ["kk%d" % t for t in range(R)] + ["rr%d" % t for t in range(R)]
+    tt(T.mt4[:, 0:4], T.kk[:], T.rr[:], A.subtract, KR, ["kr"])
+    ts(T.fls[0:8, 0:1], T.pb[0:8, 2:3], -48128.0, None, A.add, None, ["pb"], ["fls"])
+    ts(T.mgs[0:1, 2:12:3], T.rr[0:1, :], 1.0 / 256, 1.0, A.mult, A.add, KR, ["mg2"])
+    ts(T.mt4[0:1, 4:8], T.mt4[0:1, 0:4], -1.0 / 16, 92.5 / 16, A.mult, A.add, ["kr"], ["ma"])
+    ts(T.mt4[:, 12:13], T.mt4[:, 3:4], -1.0, 164.0, A.mult, A.add, ["kr"], ["c3"])
+    ts(T.mgs[0:1, 0:12:3], T.mt4[0:1, 4:8], M23, M23, A.add, A.subtract, ["ma"], ["mg0"])
+    ts(T.mt4[0:1, 8:12], T.mgs[0:1, 0:12:3], -16.0, 100.0, A.mult, A.add, ["mg0"], ["mb"])
+    tt(T.mgs[0:1, 1:12:3], T.mt4[0:1, 8:12], T.mt4[0:1, 0:4], A.subtract, ["mb", "kr"], ["mg1"])
+    dma("s", "dout", T.fl[:], T.fls[0:8, 0:1], ["fls"], [])
+    dma("s", "dout", T.mg[:], T.mgs[0:1, 0:12], ["mg0", "mg1", "mg2"], [])
+
+    ts(T.fa[:], T.ft[:], 1.0 / 16, 1.0 - 71.5 / 16, A.mult, A.add, ["ft"], ["fa"])
+    ts(T.fb[:], T.ft[:], M23, M23, A.add, A.subtract, ["ft"], ["fb"])
+    ts(T.fa[:], T.fa[:], M23, M23, A.add, A.subtract, ["fa"], ["fa"])
+    ts(T.fb[:], T.fb[:], T.mt4[:, 12:13], 14.0, A.is_equal, A.mult, ["fb", "c3"], ["fb"])
+    tt(T.fc[:], T.fa[:], T.fb[:], A.max, ["fa", "fb"], ["fc"])
+    ts(T.fc[:], T.fc[:], -1.0, None, A.add, None, ["fc"], ["fc"])
+    dma("a", "dout2", T.fs[:], T.fc[:], ["fc"], [])
+
+    need("s", [("dout", count["dout"])])
+    need("a", [("dout2", count["dout2"]), ("ca", count["ca"])])
+    need("v", [("cv", count["cv"]), ("cp", count["cp"])])
+    need("g", [("sent", count["sent"]), ("cg", count["cg"])])

@@ -6,6 +6,8 @@ PITCH = 136
 R = 4
 S0 = 10
 NR = 8
+WIN = 6144
+LOW = -16000000
 M31 = 1.5 * 2.0 ** 31
 M23 = 1.5 * 2.0 ** 23
 
@@ -15,28 +17,36 @@ SCRATCH = {
     "vew": ("sbuf", [128, 8192], bf), "tmpi": ("sbuf", [128, 256], i32),
     "hiu": ("sbuf", [128, 128], u16), "lou": ("sbuf", [128, 128], u16), "pou": ("sbuf", [128, 128], u16),
     "offu": ("sbuf", [128, 128], u16),
-    "pin": ("sbuf", [128, 8], i32), "pf": ("sbuf", [128, 16], f32), "lef": ("sbuf", [128, 4], f32),
+    "pin": ("sbuf", [128, 8], i32), "pf": ("sbuf", [128, 24], f32), "lef": ("sbuf", [128, 4], f32),
     "nid": ("sbuf", [128, W], f32), "n15": ("sbuf", [128, 128], bf), "n7": ("sbuf", [128, 128], bf),
-    "n3": ("sbuf", [128, 128], bf), "n4": ("sbuf", [128, 128], bf),
+    "n3": ("sbuf", [128, 128], bf), "n4": ("sbuf", [128, 128], bf), "n31": ("sbuf", [128, 128], bf),
     "tm": ("sbuf", [128, 16], bf), "big": ("sbuf", [128, 144], bf), "idn": ("sbuf", [128, 144], bf),
-    "sel": ("sbuf", [128, 16], f16), "rep": ("sbuf", [128, 128], f16), "cst": ("sbuf", [128, 16], f16),
+    "sel": ("sbuf", [128, 16], f16), "sel2": ("sbuf", [128, 16], f16), "sa": ("sbuf", [128, 32], bf),
+    "rep": ("sbuf", [128, 128], f16), "cst": ("sbuf", [128, 16], f16),
     "dm": ("sbuf", [128, 128], bf), "dm2": ("sbuf", [128, 128], bf), "g8": ("sbuf", [128, 128], f32),
-    "tri": ("sbuf", [128, 128], f32), "tri2": ("sbuf", [128, 128], f32), "gsel": ("sbuf", [128, 8], f32),
-    "jj": ("sbuf", [128, W], f32), "jt": ("sbuf", [128, W], f32), "inv": ("sbuf", [128, W], bf),
+    "onef": ("sbuf", [128, 128], f32), "oneb": ("sbuf", [128, 144], bf), "ec": ("sbuf", [128, 384], bf),
+    "tri": ("sbuf", [128, 128], f32), "gsel": ("sbuf", [128, 8], f32),
+    "idf": ("sbuf", [128, 128], f32), "hs": ("sbuf", [128, 16], f32), "ht": ("sbuf", [128, 16], f32),
+    "kb": ("sbuf", [128, 48], f32), "t2": ("sbuf", [128, 32], f32),
+    "lab": ("sbuf", [128, 256], f16), "lc": ("sbuf", [128, 256], bf), "ld": ("sbuf", [128, 256], bf),
+    "cb": ("sbuf", [128, 4 * PITCH + 8], bf), "eb": ("sbuf", [128, 4 * PITCH + 8], bf),
+    "w4": ("sbuf", [128, W], bf), "nq": ("sbuf", [128, W], bf),
+    "jj": ("sbuf", [128, W], f32), "jt": ("sbuf", [128, 8], f32), "inv": ("sbuf", [128, W], bf),
     "val": ("sbuf", [128, 128], bf), "tt": ("sbuf", [128, 128], f32),
     "mk": ("sbuf", [128, 2048], bf), "xx": ("sbuf", [128, 2072], bf), "oh": ("sbuf", [128, 13 * PITCH + 8], bf),
     "mm": ("sbuf", [128, 128], f16), "pay": ("sbuf", [128, 16 * R], f16), "land": ("sbuf", [128, 16 * NR * R], f16),
     "neg": ("sbuf", [128, 128], bf), "low": ("sbuf", [128, 48], f32),
     "sc": ("sbuf", [128, 48], f32), "tr": ("sbuf", [128, 32], f32),
     "kk": ("sbuf", [128, 4], f32), "rr": ("sbuf", [128, 4], f32),
-    "fo": ("sbuf", [128, W], bf), "fm": ("sbuf", [128, W], bf), "m1": ("sbuf", [128, W], bf),
+    "fo": ("sbuf", [128, W], bf),
     "alv": ("sbuf", [128, W], bf), "ded": ("sbuf", [128, W], bf), "t16": ("sbuf", [128, W], bf),
     "cd": ("sbuf", [128, W], bf), "d1": ("sbuf", [128, W], bf),
     "pc": ("sbuf", [128, 2 * W], bf), "ne": ("sbuf", [128, 2 * W], bf),
-    "av": ("sbuf", [128, 128], bf), "aa": ("sbuf", [128, 128], bf), "ss": ("sbuf", [128, 128], f32),
+    "av": ("sbuf", [128, 128], bf), "pcd": ("sbuf", [128, 128], bf), "ee": ("sbuf", [128, 136], bf),
+    "ss": ("sbuf", [128, 132], f32), "nd": ("sbuf", [128, 132], f32),
     "mt": ("sbuf", [128, 128], f32), "zz": ("sbuf", [128, 128], f32),
-    "y0": ("sbuf", [128, 2048], bf), "yw": ("sbuf", [128, 4096], bf),
-    "v0": ("sbuf", [128, 2048], f32), "fw": ("sbuf", [128, 4096], f32),
+    "y0": ("sbuf", [128, 2048], bf), "yw": ("sbuf", [128, WIN], bf),
+    "v0": ("sbuf", [128, 2048], f32), "fw": ("sbuf", [128, WIN], f32),
     "ft": ("sbuf", [128, 128], f32), "fa": ("sbuf", [128, 128], f32), "fb": ("sbuf", [128, 128], f32),
     "fc": ("sbuf", [128, 128], f32),
     "mgs": ("sbuf", [128, 12], f32), "mt4": ("sbuf", [128, 16], f32), "fls": ("sbuf", [128, 4], f32),
@@ -123,72 +133,81 @@ def rank_program(g, core, T, topo):
     def mm(out, l, rh, st, sp, r, w):
         op("p", lambda: P.matmul(out, l, rh, st, sp), r, w)
 
-    def io(out, pat, cm, w, small=True):
-        if small:
-            op("g", lambda: g.iota(out, pat, 0, cm, allow_small_or_imprecise_dtypes=True), [], w)
-        else:
-            op("g", lambda: g.iota(out, pat, 0, cm), [], w)
+    def act(out, in_, bias, scale, r, w, fn=AF.Identity):
+        op("a", lambda: S.activation(out, in_, fn, bias=bias, scale=scale), r, w)
+
+    def io(out, pat, cm, w, base=0):
+        op("g", lambda: g.iota(out, pat, base, cm, allow_small_or_imprecise_dtypes=True), [], w)
+
+    def pick(out, in_, pat, cmp, base, cm, r, w):
+        op("g", lambda: g.affine_select(out, in_, pat, cmp, 0.0, base, cm), r, w)
 
     dma("s", "dpos", T.posi[:], T.pos[:], [], ["posi"])
     dma("a", "dst", T.stw[:], T.st[:], [], ["stw"])
     dma("s", "dle", T.lei[0:8, 0:1], T.le[:], [], ["lei"])
     dma("s", "dve", T.vew[:], T.ve[:], [], ["vew"])
 
-    io(T.pin[:, 0:1], [[0, 1]], 1, ["pin0"], small=False)
+    CB = ["cb0", "cb1", "cb2", "cb3"]
+    op("g", lambda: g.iota(T.pin[:, 0:1], [[0, 1]], 0, 1), [], ["pin0"])
     io(T.nid[:], [[1, W]], 0, ["nid"])
-    io(T.n4[:], [[1, 8], [0, 16]], 0, ["n4"])
-    io(T.n15[:], [[0, 8], [1, 16]], 0, ["n15"])
+    io(T.n4[0:8, :], [[1, 8], [0, 16]], 0, ["n4"])
     io(T.n7[:], [[0, 16], [1, 8]], 0, ["n7"])
     io(T.n3[:], [[1, 16], [0, 8]], 0, ["n3"])
+    io(T.n15[:], [[0, 8], [1, 16]], 0, ["n15"])
+    io(T.pc[:], [[0, 2 * W]], 0, ["pcl", "pcr"], base=200)
+    io(T.cb[:], [[0, 4 * PITCH + 8]], 0, CB, base=200)
+    io(T.low[:], [[0, 48]], 0, ["low"], base=LOW)
+    io(T.kb[:], [[0, 48]], 0, ["kb"], base=LOW)
+    io(T.onef[:], [[0, 128]], 0, ["onef"], base=1)
+    io(T.oneb[:], [[0, 144]], 0, ["oneb"], base=1)
+    io(T.n31[0:32, :], [[0, 4], [1, 32]], 0, ["n31"])
     OH = ["oh%d" % x for x in range(13)]
     ms(T.oh[:], 0.0, OH)
     ms(T.xx[:, 0:8], 0.0, ["xpad0"])
     ms(T.xx[:, 2056:2072], 0.0, ["xpad1"])
     p0 = T.pin[:, 0:1]
     ts(T.pin[:, 1:2], p0, 15, None, A.bitwise_and, None, ["pin0"], ["pin1"])
-    ts(T.pin[:, 2:3], p0, 4, None, A.arith_shift_right, None, ["pin0"], ["pin2"])
+    ts(T.pin[:, 2:3], p0, 16, None, A.bitwise_and, None, ["pin0"], ["pin2"])
     ts(T.pin[:, 3:4], p0, 3, None, A.arith_shift_right, None, ["pin0"], ["pin3"])
     ts(T.pin[:, 4:5], p0, 7, None, A.bitwise_and, None, ["pin0"], ["pin4"])
     ts(T.pin[:, 5:6], p0, 112, None, A.bitwise_and, None, ["pin0"], ["pin5"])
     cp(T.pf[:, 0:6], T.pin[:, 0:6], ["pin%d" % i for i in range(6)], ["pf"])
-    fP, fR, fG, fP3, fP7, fG16 = [T.pf[:, i:i + 1] for i in range(6)]
+    fP, fR, fH, fP3, fP7, fG16 = [T.pf[:, i:i + 1] for i in range(6)]
     ts(T.tm[:], T.nid[:, 0:16], fR, None, A.is_equal, None, ["nid", "pf"], ["tm"])
     ts(T.big[:], T.nid[:, 0:144], -15.0, fG16, A.add, A.is_equal, ["nid", "pf"], ["big"])
-    ts(T.pf[:, 6:7], fR, 128.0, None, A.mult, None, ["pf"], ["pf6"])
+    ts(T.pf[:, 9:10], fR, 128.0, None, A.mult, None, ["pf"], ["pf9"])
     ts(T.g8[0:8, :], T.n4[0:8, :], T.pf[0:8, 0:1], None, A.is_equal, None, ["n4", "pf"], ["g8"])
-    ts(T.jj[:], T.nid[:], T.pf[:, 6:7], -8.0, A.add, A.add, ["nid", "pf6"], ["jj"])
-    ts(T.pf[:, 7:8], fP3, 156.0, -1.0 / 2048, A.add, A.mult, ["pf"], ["pf7"])
-    ts(T.jt[:], T.jj[:], 0.0, 8192.0, A.is_lt, A.mult, ["jj"], ["jt"])
-    tt(T.jt[:], T.jt[:], T.jj[:], A.add, ["jt", "jj"], ["jt"])
 
     ts(T.tmpi[:, 0:128], T.posi[:], 9, None, A.arith_shift_right, None, ["posi"], ["tmp0"])
-    ts(T.tmpi[:, 128:256], T.posi[:], 511, None, A.bitwise_and, None, ["posi"], ["tmp1"])
     cp(T.hiu[:], T.tmpi[:, 0:128], ["tmp0"], ["hiu"])
-    cp(T.lou[:], T.tmpi[:, 128:256], ["tmp1"], ["lou"])
-    NC = 8
-    CW = 2048 // NC
+    ts(T.tmpi[:, 128:256], T.posi[:], 511, None, A.bitwise_and, None, ["posi"], ["tmp1"])
+    cuts = [0, 128] + list(range(384, 2048, 256)) + [2048]
+    NC = len(cuts) - 1
     for i in range(NC):
-        op("a", lambda: S.activation(T.mk[:, CW * i:CW * (i + 1)],
-                                     T.tm[:, 0:16].indirect(T.hiu[:, CW // 16 * i:CW // 16 * (i + 1)]), AF.Copy),
+        a, b = cuts[i], cuts[i + 1]
+        op("a", lambda: S.activation(T.mk[:, a:b], T.tm[:, 0:16].indirect(T.hiu[:, a // 16:b // 16]), AF.Copy),
            ["tm", "hiu"], ["mk%d" % i])
-    cp(T.lef[0:8, 0:1], T.lei[0:8, 0:1], ["lei"], ["lef"])
-    mm(T.pb[:, 0:1], T.g8[0:8, :], T.lef[0:8, 0:1], True, True, ["g8", "lef"], ["pb"])
-    ts(T.sel[:], T.nid[:, 0:16], fP3, None, A.is_equal, None, ["nid", "pf"], ["sel"])
-    ts(T.cst[:], T.nid[:, 0:16], -16.0 / 2048, T.pf[:, 7:8], A.mult, A.add, ["nid", "pf7"], ["cst"])
+    act(T.fw[:, 0:2048], T.mk[:], 0.0, 0.0, ["mk%d" % i for i in range(NC)], ["fw"], fn=AF.Silu)
+    ts(T.jj[:], T.nid[:], T.pf[:, 9:10], -8.0, A.add, A.add, ["nid", "pf9"], ["jj"])
+    cp(T.lou[:], T.tmpi[:, 128:256], ["tmp1"], ["lou"])
     done_r = 0
     for i in range(NC):
-        tt(T.xx[:, 8 + CW * i:8 + CW * (i + 1)],
-           T.stw[:, 0:512].indirect(T.lou[:, CW // 16 * i:CW // 16 * (i + 1)]),
-           T.mk[:, CW * i:CW * (i + 1)], A.mult, ["stw", "lou", "mk%d" % i], ["x%d" % i])
-        while done_r < 16 and (i == NC - 1 or 128 * done_r + 144 <= CW * (i + 1)):
+        a, b = cuts[i], cuts[i + 1]
+        tt(T.xx[:, 8 + a:8 + b], T.stw[:, 0:512].indirect(T.lou[:, a // 16:b // 16]), T.mk[:, a:b], A.mult,
+           ["stw", "lou", "mk%d" % i], ["x%d" % i])
+        if i == 0:
+            cp(T.lef[0:8, 0:1], T.lei[0:8, 0:1], ["lei"], ["lef"])
+            mm(T.pb[:, 0:1], T.g8[0:8, :], T.lef[0:8, 0:1], True, True, ["g8", "lef"], ["pb"])
+            ts(T.jt[:], T.jj[:, 0:8], 0.0, 8192.0, A.is_lt, A.mult, ["jj"], ["jt"])
+        while done_r < 16 and (i == NC - 1 or 128 * done_r + 144 <= b):
             r = done_r
             mm(T.e0[:, 0:W], T.big[:, 15 - r:143 - r], T.xx[:, 128 * r:128 * r + W], r == 0, r == 15,
                ["big", "xpad0", "xpad1"] + ["x%d" % k for k in range(i + 1)], ["e0"])
             done_r += 1
-    ts(T.inv[:], T.jt[:], T.pb[:, 0:1], 15.0, A.is_ge, A.mult, ["jt", "pb"], ["inv"])
-    ts(T.dm[:], T.n7[:], fP7, None, A.is_equal, None, ["n7", "pf"], ["dm"])
-    ts(T.dm2[:], T.n3[:], fP3, None, A.not_equal, None, ["n3", "pf"], ["dm2"])
-    tt(T.fo[:], T.e0[:, 0:W], T.inv[:], A.max, ["e0", "inv"], ["fo"])
+    tt(T.jt[:], T.jt[:], T.jj[:, 0:8], A.add, ["jt", "jj"], ["jt"])
+    ts(T.inv[:, 8:W], T.jj[:, 8:W], T.pb[:, 0:1], 15.0, A.is_ge, A.mult, ["jj", "pb"], ["inv1"])
+    ts(T.inv[:, 0:8], T.jt[:], T.pb[:, 0:1], 15.0, A.is_ge, A.mult, ["jt", "pb"], ["inv0"])
+    tt(T.fo[:], T.e0[:, 0:W], T.inv[:], A.max, ["e0", "inv0", "inv1"], ["fo"])
 
     cores = list(T.cores)
     chips = []
@@ -217,36 +236,87 @@ def rank_program(g, core, T, topo):
         a = topo.addr(c)
         return DstId(rid=a[0], pnc=a[1])
 
+    def codes_out(banks):
+        for b in banks:
+            bank = "e%d" % b
+            for q in range(4):
+                r = 4 * b + q
+                mm(T[bank][:, 128 * q:128 * q + 128], T.idn[:, r:r + 128], T.pc[:, W + 8:W + 136], True, True,
+                   ["idn", "pcr"], [bank])
+            for q in range(4):
+                r = 4 * b + q
+                act(T.v0[:, r:2048:16], T[bank][:, 128 * q:128 * q + 128], 116.0, -1.0, [bank], ["v0_%d" % r])
+
+    FM, M1 = T.e1[:, 0:W], T.e1[:, 256:256 + W]
+    PCL, PCR = 0, W
+    sA, sB1, sB2, sLow = T.pf[:, 12:13], T.pf[:, 13:14], T.pf[:, 14:15], T.pf[:, 15:16]
     off = 0
     for t in range(R):
         NS = S0 + t
-        n8 = 8 * NS
-        for x in range(NS):
-            ts(T.oh[:, PITCH * x:PITCH * x + 129], T.fo[:, 7:136], float(x - off), None, A.is_equal, None,
-               ["fo"], ["oh%d" % x])
-        span = 17 * (n8 - 1) + 1
-        for k in range(17):
-            mm(T.p1[0:n8, 0:n8], T.oh[:, k:k + span:17], T.oh[:, k + 1:k + 1 + span:17], k == 0, k == 16, OH, ["p1"])
+        last = t == R - 1
         if t == 0:
-            tt(T.dm[:], T.dm[:], T.dm2[:], A.mult, ["dm", "dm2"], ["dm"])
-            ms(T.p2[:, 0:16], 0.0, ["p2"])
-            ms(T.p3[:, 16:48], -1.0e9, ["p3"])
-            ms(T.low[:], -1.0e9, ["low"])
-            ms(T.pc[:], 200.0, ["pcl", "pcr"])
+            n8, nm, nsel, sel, sk = 8 * NS, 8 * NS, 16, T.sel, "sel"
+            for x in range(NS):
+                ts(T.oh[:, PITCH * x:PITCH * x + 129], T.fo[:, 7:136], float(x), None, A.is_equal, None,
+                   ["fo"], ["oh%d" % x])
+            span = 17 * (n8 - 1) + 1
+            for k in range(17):
+                mm(T.p1[0:n8, 0:n8], T.oh[:, k:k + span:17], T.oh[:, k + 1:k + 1 + span:17], k == 0, k == 16, OH, ["p1"])
             cp(T.pou[:], T.posi[:], ["posi"], ["pou"])
+            ts(T.dm[:], T.n7[:], fP7, None, A.is_equal, None, ["n7", "pf"], ["dm"])
+            ts(T.dm2[:], T.n3[:], fP3, None, A.not_equal, None, ["n3", "pf"], ["dm2"])
+            ts(T.sel[:], T.nid[:, 0:16], fP3, None, A.is_equal, None, ["nid", "pf"], ["sel"])
+            ms(T.p2[:, 0:16], 0.0, ["p2"])
+            tt(T.dm2[:], T.dm[:], T.dm2[:], A.mult, ["dm", "dm2"], ["dm2"])
+            ts(T.pf[:, 7:8], fP3, 156.0, -1.0 / 2048, A.add, A.mult, ["pf"], ["pf7"])
             ts(T.rep[:], T.n15[:], fP3, 256.0, A.is_equal, A.mult, ["n15", "pf"], ["rep"])
-        elif t == 1:
-            cp(T.alv[:], T.ne[:, 0:W], ["ne"], ["alv"])
+            ts(T.cst[:], T.nid[:, 0:16], -16.0 / 2048, T.pf[:, 7:8], A.mult, A.add, ["nid", "pf7"], ["cst"])
+            ts(T.t16[:], T.fo[:], -16.0, 100.0, A.mult, A.add, ["fo"], ["t16"])
+            for r in range(16):
+                op("a", lambda: S.activation(T.y0[:, r:2048:16], T.vew[:, 0:8192].indirect(T.pou[:, 8 * r:8 * r + 8]),
+                                             AF.Copy), ["vew", "pou"], ["y0_%d" % r])
+            mask, mk_ = T.dm2, "dm2"
         else:
-            tt(T.alv[:], T.alv[:], T.ne[:, 0:W], A.mult, ["alv", "ne"], ["alv"])
-        ts(T.t16[:], T.fo[:], -16.0, 100.0 - 17 * off, A.mult, A.add, ["fo"], ["t16"])
-        if t > 0:
-            ts(T.ded[:], T.alv[:], -1.0, 1.0, A.mult, A.add, ["alv"], ["ded"])
+            nm = 32
+            if t == 1:
+                n8, nsel, sel, sk = 8 * (NS - 1), 16, T.sel, "sel"
+            else:
+                n8, nsel, sel, sk = 8 * NS, NS - 1, T.sel2, "sel2"
+            u = t - 1
+            K, RK, KR = T.kk[:, u:u + 1], T.rr[:, u:u + 1], ["kk%d" % u, "rr%d" % u]
+            ts(T.eb[:], T.cb[:], RK, K, A.add, A.is_equal, CB + KR, ["eb"])
+            for k in range(17):
+                mm(T.p1[0:n8, 0:32], T.oh[:, k + 1:k + 2 + 17 * (n8 - 1):17], T.eb[:, k + 1:k + 2 + 17 * 31:17],
+                   k == 0, k == 16, OH + ["eb"], ["p1"])
+            ts(T.ne[:], T.pc[:], RK, K, A.add, A.not_equal, ["pcl", "pcr"] + KR, ["ne"])
+            tt(M1, FM, T.ne[:, 0:W], A.mult, ["e1", "ne"], ["e1"])
+            if t == 1:
+                cp(T.alv[:], T.ne[:, 0:W], ["ne"], ["alv"])
+            else:
+                tt(T.alv[:], T.alv[:], T.ne[:, 0:W], A.mult, ["alv", "ne"], ["alv"])
+            tt(T.fo[:], M1, T.ne[:, W:2 * W], A.mult, ["e1", "ne"], ["fo"])
+            off = NS - 1
+            act(T.ded[:], T.alv[:], 1.0, -1.0, ["alv"], ["ded"])
+            ts(T.t16[:], T.fo[:], -16.0, 100.0 - 17 * off, A.mult, A.add, ["fo"], ["t16"])
+            tt(T.mt4[:, u:u + 1], K, RK, A.subtract, KR, ["kr%d" % u])
             tt(T.cd[:, 1:W], T.t16[:, 0:W - 1], T.fo[:, 1:W], A.subtract, ["t16", "fo"], ["cd"])
-            tt(T.d1[:, 1:W], T.cd[:, 1:W], T.alv[:, 1:W], A.mult, ["cd", "alv"], ["d1"])
+            act(T.mt4[:, 6:7], RK, 256.0, 1.0, KR, ["r256"])
+            act(T.lc[0:32, 0:128], T.ec[0:32, 128 * u:128 * u + 128], 0.0, T.pf[0:32, 12:13], ["ec", "sA"], ["lc0"])
+            act(T.lc[0:32, 128:256], T.ec[0:32, 128 * u:128 * u + 128], 0.0, T.pf[0:32, 13:14], ["ec", "sB1"], ["lc1"])
+            if last:
+                act(T.pcd[:], T.alv[:, 8:136], 200.0, -200.0, ["alv"], ["pcd"])
+            else:
+                act(T.w4[:], T.alv[:], 400.0, -400.0, ["alv"], ["w4"])
+                act(FM, T.fo[:], float(off - NS), 1.0, ["fo"], ["e1"])
+                for x in range(0 if t == 1 else 1, NS + 1):
+                    act(T.oh[:, PITCH * x:PITCH * x + 129], T.fo[:, 7:136], off - x + 0.5, 1.0, ["fo"], ["oh%d" % x],
+                        fn=AF.Sign)
+            mask, mk_ = T.dm, "dm"
 
-        tt(T.mm[0:n8, 0:n8], T.p1[0:n8, 0:n8], T.dm[0:n8, 0:n8], A.mult, ["p1", "dm"], ["mm"])
-        mm(T.p2[0:n8, 0:16], T.mm[0:n8, 0:n8], T.sel[0:n8, :], True, True, ["mm", "sel"], ["p2"])
+        tt(T.mm[0:n8, 0:nm], T.p1[0:n8, 0:nm], mask[0:n8, 0:nm], A.mult, ["p1", mk_], ["mm"])
+        mm(T.p2[0:nm, 0:nsel], T.mm[0:n8, 0:nm], sel[0:n8, 0:nsel], True, True, ["mm", sk], ["p2"])
+        if t > 0:
+            ts(T.mt4[:, 4:5], T.mt4[:, u:u + 1], -1.0 / 16, 92.5 / 16, A.mult, A.add, ["kr%d" % u], ["ma"])
         pay = T.pay[:, 16 * t:16 * t + 16]
         cp(pay, T.p2[:, 0:16], ["p2"], ["pay%d" % t])
         slot = T.land[:, 16 * (NR * t + rank):16 * (NR * t + rank) + 16]
@@ -261,95 +331,144 @@ def rank_program(g, core, T, topo):
         count["sent"] += len(far_eng) + len(near_eng)
 
         if t == 0:
+            for k in range(R - 1):
+                pick(T.ec[0:32, 128 * k:128 * k + 128], T.oneb[0:32, 0:128], [[0, 4], [1, 32]], A.is_equal, -(S0 + k), 0,
+                     ["oneb"], ["ec"])
+            pick(T.idf[:], T.onef[:], [[-1, 128]], A.is_equal, 0, 1, ["onef"], ["idf"])
+            ms(T.p3[:, 16:48], -1.0e9, ["p3"])
             tt(T.pc[:, 1:W], T.t16[:, 0:W - 1], T.fo[:, 1:W], A.subtract, ["t16", "fo"], ["pcl"])
             tt(T.pc[:, W:2 * W - 1], T.t16[:, 0:W - 1], T.fo[:, 1:W], A.subtract, ["t16", "fo"], ["pcr"])
+            ts(FM, T.fo[:], float(-NS), None, A.add, None, ["fo"], ["e1"])
+            cp(T.cb[:, PITCH + 1:PITCH + 129], T.pc[:, PCL + 7:PCL + 135], ["pcl"], ["cb1"])
+            cp(T.cb[:, 0:129], T.pc[:, PCR + 8:PCR + 137], ["pcr"], ["cb0"])
         else:
+            if t == 1:
+                pick(T.idn[:], T.oneb[:], [[-1, 144]], A.is_equal, 0, 1, ["oneb"], ["idn"])
+                pick(T.tri[:], T.onef[:], [[1, 128]], A.is_gt, 0, -1, ["onef"], ["tri"])
+                pick(T.tri[:], T.tri[:], [[-16, 8], [0, 16]], A.is_ge, 0, 1, ["tri"], ["tri"])
+            if t == 2:
+                pick(T.gsel[:], T.onef[:, 0:8], [[-16, 8]], A.is_ge, 0, 1, ["onef"], ["gsel"])
+                pick(T.gsel[:], T.gsel[:], [[16, 8]], A.is_ge, 15, -1, ["gsel"], ["gsel"])
+                io(T.neg[:], [[0, 128]], 0, ["neg"], base=-1)
+                io(T.ee[:, 128:136], [[0, 8]], 0, ["eepad"])
+            tt(T.d1[:, 1:W], T.cd[:, 1:W], T.alv[:, 1:W], A.mult, ["cd", "alv"], ["d1"])
+            ts(T.mgs[:, 3 * u:3 * u + 1], T.mt4[:, 4:5], M23, M23, A.add, A.subtract, ["ma"], ["a%d" % u])
             scan(T.pc[:, 2 * W - 2:W - 1:-1], T.ded[:, W - 1:0:-1], T.d1[:, W - 1:0:-1], 0.0, A.mult, A.add,
                  ["ded", "d1"], ["pcr"])
-            scan(T.pc[:, 1:W], T.ded[:, 1:W], T.d1[:, 1:W], 0.0, A.mult, A.add, ["ded", "d1"], ["pcl"])
-        if t < R - 1:
-            ts(T.fm[:], T.fo[:], float(off - NS), None, A.add, None, ["fo"], ["fm"])
+            if last:
+                codes_out([0, 2])
+            ts(T.mt4[:, 5:6], T.mgs[:, 3 * u:3 * u + 1], -16.0, 100.0, A.mult, A.add, ["a%d" % u], ["mb"])
+            ts(T.ld[0:32, 0:128], T.n31[0:32, :], T.mgs[0:32, 3 * u:3 * u + 1], T.pf[0:32, 12:13], A.is_equal, A.mult,
+               ["n31", "sA", "a%d" % u], ["ld0"])
+            tt(T.mgs[:, 3 * u + 1:3 * u + 2], T.mt4[:, 5:6], T.mt4[:, u:u + 1], A.subtract, ["mb", "kr%d" % u], ["b%d" % u])
+            if t == 1:
+                ts(T.kb[:, 0:16], T.p3[:, 0:16], sLow, None, A.add, None, ["p3", "sLow"], ["kb"])
+            if not last:
+                scan(T.pc[:, 1:W], T.ded[:, 1:W], T.d1[:, 1:W], 0.0, A.mult, A.add, ["ded", "d1"], ["pcl"])
+            ts(T.ld[0:32, 128:256], T.n31[0:32, :], T.mgs[0:32, 3 * u + 1:3 * u + 2], T.pf[0:32, 14:15], A.is_equal, A.mult,
+               ["n31", "sB2", "b%d" % u], ["ld1"])
+            ts(T.ht[:], T.kb[:, 0:16], K, T.mt4[:, 6:7], A.is_equal, A.mult, ["kb", "r256"] + KR, ["ht"])
+            tt(T.lab[0:32, :], T.lc[0:32, :], T.ld[0:32, :], A.subtract, ["lc0", "ld0", "lc1", "ld1"], ["lab"])
+            tt(T.hs[:], T.kb[:, 0:16], T.ht[:], A.subtract, ["kb", "ht"], ["hs"])
+            if not last:
+                tt(T.cb[:, 0:129], T.pc[:, PCR + 8:PCR + 137], T.w4[:, 8:137], A.add, ["pcr", "w4"], ["cb0"])
+                tt(T.cb[:, PITCH + 1:PITCH + 129], T.pc[:, PCL + 7:PCL + 135], T.w4[:, 8:136], A.add, ["pcl", "w4"], ["cb1"])
+        if not last:
+            tt(T.nq[:, 7:136], T.pc[:, PCL + 7:PCL + 136], T.cb[:, 0:129], A.not_equal, ["pcl", "cb0"], ["nq"])
+            ts(T.nq[:, 7:136], T.nq[:, 7:136], 400.0, None, A.mult, None, ["nq"], ["nq"])
+            tt(T.cb[:, 2 * PITCH + 1:2 * PITCH + 129], T.nq[:, 8:136], T.pc[:, PCL + 8:PCL + 136], A.add, ["nq", "pcl"], ["cb2"])
+            tt(T.cb[:, 3 * PITCH + 1:3 * PITCH + 129], T.nq[:, 7:135], T.pc[:, PCL + 7:PCL + 135], A.add, ["nq", "pcl"], ["cb3"])
         if t == 0:
-            ts(T.val[:], T.jt[:, 8:136], T.pb[:, 0:1], None, A.is_lt, None, ["jt", "pb"], ["val"])
-            ts(T.idn[:], T.nid[:, 0:144], fP, None, A.is_equal, None, ["nid", "pf"], ["idn"])
-            ts(T.tt[:], T.jj[:, 8:136], -1.0, 4096.0, A.mult, A.add, ["jj"], ["tt"])
-            ms(T.neg[:], -1.0, ["neg"])
-            for r in range(16):
-                op("a", lambda: S.activation(T.y0[:, r:2048:16], T.vew[:, 0:8192].indirect(T.pou[:, 8 * r:8 * r + 8]),
-                                             AF.Copy), ["vew", "pou"], ["y0_%d" % r])
-            op("a", lambda: S.activation(T.fw[:], T.vew[:, 0:4096], AF.Silu, scale=0.0), ["vew"], ["fw"])
-            op("a", lambda: S.activation(T.yw[:], T.vew[:, 0:4096], AF.Copy, scale=0.0), ["vew"], ["yw"])
+            ms(T.pb[:, 48:64], 0.0, ["pb"])
+            ts(T.pf[:, 10:11], fP3, 0.0, 256.0, A.is_equal, A.mult, ["pf"], ["s0"])
+            ts(T.pf[:, 11:12], fP3, 2.0, 256.0, A.is_equal, A.mult, ["pf"], ["s2"])
+            ts(sB2, fP3, 1.0, 256.0, A.is_equal, A.mult, ["pf"], ["sB2"])
+            ts(T.pf[:, 16:17], fP3, 3.0, 256.0, A.is_equal, A.mult, ["pf"], ["s3"])
+            ts(sLow, fH, -1.0e8, None, A.mult, None, ["pf"], ["sLow"])
+            tt(sA, T.pf[:, 10:11], T.pf[:, 11:12], A.subtract, ["s0", "s2"], ["sA"])
+            tt(sB1, sB2, T.pf[:, 16:17], A.subtract, ["sB2", "s3"], ["sB1"])
+            ts(T.sa[:, 0:16], T.nid[:, 0:16], fP3, 0.5, A.is_equal, A.mult, ["nid", "pf"], ["sa0"])
+            ts(T.sa[:, 16:32], T.nid[:, 1:17], fP3, 0.5, A.is_equal, A.mult, ["nid", "pf"], ["sa1"])
+            ts(T.val[:], T.jj[:, 8:136], T.pb[:, 0:1], None, A.is_lt, None, ["jj", "pb"], ["val"])
+            tt(T.sel2[:], T.sa[:, 0:16], T.sa[:, 16:32], A.subtract, ["sa0", "sa1"], ["sel2"])
+            ms(T.yw[:, 0:1024], 0.0, ["yw"])
         if t == 1:
-            ts(T.tri[:], T.n4[:], fG, None, A.is_equal, None, ["n4", "pf"], ["tri"])
-            ts(T.tri2[:], T.nid[:, 0:128], fP, None, A.is_gt, None, ["nid", "pf"], ["tri2"])
-            ts(T.gsel[:], T.nid[:, 0:8], fG, None, A.is_equal, None, ["nid", "pf"], ["gsel"])
-            ts(T.pf[:, 8:9], T.tt[:, 127:128], -1.0, 1.0, A.mult, A.add, ["tt"], ["pf8"])
-            tt(T.tri[:], T.tri[:], T.tri2[:], A.mult, ["tri", "tri2"], ["tri"])
-        if t == R - 1:
+            ms(T.yw[:, 1024:2048], 0.0, ["yw2"])
+        if t == 2:
+            act(T.tt[:], T.jj[:, 8:136], 4096.0, -1.0, ["jj"], ["tt"])
+            act(T.pf[:, 8:9], T.jj[:, 135:136], 4095.0, -1.0, ["jj"], ["pf8"])
+        if last:
             tt(T.av[:], T.alv[:, 8:136], T.val[:], A.mult, ["alv", "val"], ["av"])
-            for b in range(4):
-                bank = "e%d" % b
-                for q in range(4):
-                    r = 4 * b + q
-                    mm(T[bank][:, 128 * q:128 * q + 128], T.idn[:, r:r + 128], T.pc[:, W + 8:W + 136], True, True,
-                       ["idn", "pcr"], [bank])
-                for q in range(4):
-                    r = 4 * b + q
-                    op("a", lambda: S.activation(T.v0[:, r:2048:16], T[bank][:, 128 * q:128 * q + 128], AF.Identity,
-                                                 bias=164.0, scale=-1.0), [bank], ["v0_%d" % r])
-            mm(T.pb[:, 1:2], T.tri[:], T.pf[:, 8:9], True, False, ["tri", "pf8"], ["pb"])
+            tt(T.pcd[:], T.pcd[:], T.d1[:, 8:136], A.add, ["pcd", "d1"], ["pcd"])
+            scan(T.ss[:, 0:128], T.av[:], T.neg[:], T.tt[:, 0:1], A.add, A.add, ["av", "neg", "tt"], ["ss"])
+            tt(T.p2[:, 128:256], T.av[:], T.tt[:], A.mult, ["av", "tt"], ["p2"])
+            tt(T.zz[:], T.ss[:, 0:128], T.p2[:, 128:256], A.subtract, ["ss", "p2"], ["zz"])
+            ts(T.nd[:, 128:129], T.p2[:, 255:256], -1.0, T.pf[:, 8:9], A.mult, A.add, ["p2", "pf8"], ["nd2"])
+            tt(T.nd[:, 1:128], T.zz[:, 0:127], T.zz[:, 1:128], A.subtract, ["zz"], ["nd1"])
+            ts(T.nd[:, 0:1], T.zz[:, 0:1], -1.0, None, A.mult, None, ["zz"], ["nd0"])
 
-        mm(T.p3[:, 0:16], T.rep[:], T.cst[:], True, False, ["rep", "cst"], ["p3"])
-        mm(T.p3[:, 0:16], T.rep[0:n8, :], T.pay[0:n8, 16 * t:16 * t + 16], False, False, ["pay%d" % t], ["p3"])
-        for i, (c, n) in enumerate(senders):
+        srcs = [(T.pay[0:nm, 16 * t:16 * t + 16], None)]
+        for c, n in senders:
             s = T.rank_of(c)
-            need("p", [("ar%d_%d" % (t, s), n)])
-            mm(T.p3[:, 0:16], T.rep[0:n8, :], T.land[0:n8, 16 * (NR * t + s):16 * (NR * t + s) + 16],
-               False, i == len(senders) - 1, [], ["p3"])
+            srcs.append((T.land[0:nm, 16 * (NR * t + s):16 * (NR * t + s) + 16], ("ar%d_%d" % (t, s), n)))
+        if t == 0:
+            mm(T.p3[:, 0:16], T.rep[:], T.cst[:], True, False, ["rep", "cst"], ["p3"])
+        else:
+            mm(T.p3[:, 0:16], T.idf[:], T.hs[:], True, False, ["idf", "hs"], ["p3"])
+        for i, (src, tok) in enumerate(srcs):
+            end = i == len(srcs) - 1
+            if tok:
+                need("p", [tok])
+            if t == 0:
+                mm(T.p3[:, 0:16], T.rep[0:nm, :], src, False, end, ["pay0"], ["p3"])
+            else:
+                mm(T.pb[:, 32:48], T.lab[0:32, 128:256], src, i == 0, end, ["lab", "pay%d" % t], ["pb"])
+                mm(T.p3[:, 0:16], T.lab[0:32, 0:128], src, False, end, ["lab"], ["p3"])
+        if last:
+            codes_out([1, 3])
         K, RK = T.kk[:, t:t + 1], T.rr[:, t:t + 1]
-        scan(T.sc[:], T.p3[:, 0:48], T.low[:], -1.0e9, A.max, A.max, ["p3", "low"], ["sc"])
+        if t == 0:
+            scan(T.sc[:], T.p3[:, 0:48], T.low[:], -1.0e9, A.max, A.max, ["p3", "low"], ["sc"])
+        else:
+            op("v", lambda: V.transpose(T.t2[:], T.pb[:, 32:64]), ["pb"], ["t2"])
+            tt(T.kb[:, 0:16], T.p3[:, 0:16], T.t2[:, 0:16], A.add, ["p3", "t2"], ["kb"])
+            scan(T.sc[:], T.kb[:], T.low[:], -1.0e9, A.max, A.max, ["kb", "low"], ["sc"])
         op("v", lambda: V.transpose(T.tr[:], T.sc[:, 16:48]), ["sc"], ["tr"])
         op("v", lambda: V.tensor_reduce(K, T.tr[:], AX.X, A.max), ["tr"], ["kk%d" % t])
         ts(RK, K, M31, M31, A.add, A.subtract, ["kk%d" % t], ["rr%d" % t])
-        if t < R - 1:
-            ts(T.ne[:], T.pc[:], RK, K, A.add, A.not_equal, ["pcl", "pcr", "kk%d" % t, "rr%d" % t], ["ne"])
-            tt(T.m1[:], T.fm[:], T.ne[:, 0:W], A.mult, ["fm", "ne"], ["m1"])
-            tt(T.fo[:], T.m1[:], T.ne[:, W:2 * W], A.mult, ["m1", "ne"], ["fo"])
-            off = NS
 
     K, RK = T.kk[:, 3:4], T.rr[:, 3:4]
-    ts(T.ne[:, 0:128], T.pc[:, 8:136], RK, K, A.add, A.not_equal, ["pcl", "kk3", "rr3"], ["ne"])
-    tt(T.aa[:], T.av[:], T.ne[:, 0:128], A.mult, ["av", "ne"], ["aa"])
-    scan(T.ss[:], T.aa[:], T.neg[:], T.tt[:, 0:1], A.add, A.add, ["aa", "neg", "tt"], ["ss"])
-    mm(T.pb[:, 1:2], T.tri[:], T.ss[:, 127:128], False, True, ["tri", "ss"], ["pb"])
-    tt(T.mt[:], T.aa[:], T.tt[:], A.mult, ["aa", "tt"], ["mt"])
-    tt(T.zz[:], T.ss[:], T.mt[:], A.subtract, ["ss", "mt"], ["zz"])
-    ts(T.offu[:], T.zz[:], T.pb[:, 1:2], None, A.add, None, ["zz", "pb"], ["offu"])
-    op("a", lambda: S.activation(T.fw[:, 0:4096].indirect(T.offu[:, 0:128]), T.v0[:], AF.Silu),
+    ts(T.ee[:, 0:128], T.pcd[:], RK, K, A.add, A.is_equal, ["pcd", "kk3", "rr3"], ["ee"])
+    scan(T.ss[:, 0:129], T.ee[:, 0:129], T.nd[:, 0:129], 0.0, A.add, A.add, ["ee", "eepad", "nd0", "nd1", "nd2"], ["ss"])
+    mm(T.pb[:, 1:2], T.tri[:], T.ss[:, 128:129], True, True, ["tri", "ss"], ["pb"])
+    ts(T.p2[:, 128:256], T.ee[:, 0:128], 4096.0, None, A.mult, None, ["ee"], ["p2"])
+    tt(T.zz[:], T.p2[:, 128:256], T.ss[:, 0:128], A.subtract, ["p2", "ss"], ["zz"])
+    ts(T.offu[:], T.zz[:], T.pb[:, 1:2], None, A.subtract, None, ["zz", "pb"], ["offu"])
+    op("a", lambda: S.activation(T.fw[:, 0:WIN].indirect(T.offu[:, 0:128]), T.v0[:], AF.Silu),
        ["offu"] + ["v0_%d" % r for r in range(16)], ["fw"])
-    cp(T.yw[:, 0:4096].indirect(T.offu[:, 0:128]), T.y0[:], ["offu"] + ["y0_%d" % r for r in range(16)], ["yw"])
-    mm(T.pb[0:8, 2:3], T.gsel[:], T.ss[:, 127:128], True, True, ["gsel", "ss"], ["pb"])
+    cp(T.yw[:, 0:WIN].indirect(T.offu[:, 0:128]), T.y0[:], ["offu"] + ["y0_%d" % r for r in range(16)], ["yw", "yw2"])
     dma("a", "dft", T.ft[:], T.fw[0:128:16, 0:2048], ["fw"], ["ft"])
     dma("s", "dout", T.y[:], T.yw[:, 0:2048], ["yw"], [])
 
     KR = ["kk%d" % t for t in range(R)] + ["rr%d" % t for t in range(R)]
-    tt(T.mt4[:, 0:4], T.kk[:], T.rr[:], A.subtract, KR, ["kr"])
-    ts(T.fls[0:8, 0:1], T.pb[0:8, 2:3], -48128.0, None, A.add, None, ["pb"], ["fls"])
+    mm(T.pb[0:8, 2:3], T.gsel[:], T.ss[:, 128:129], True, True, ["gsel", "ss"], ["pb"])
+    tt(T.mt4[:, 3:4], K, RK, A.subtract, KR, ["kr3"])
     ts(T.mgs[0:1, 2:12:3], T.rr[0:1, :], 1.0 / 256, 1.0, A.mult, A.add, KR, ["mg2"])
-    ts(T.mt4[0:1, 4:8], T.mt4[0:1, 0:4], -1.0 / 16, 92.5 / 16, A.mult, A.add, ["kr"], ["ma"])
-    ts(T.mt4[:, 12:13], T.mt4[:, 3:4], -1.0, 164.0, A.mult, A.add, ["kr"], ["c3"])
-    ts(T.mgs[0:1, 0:12:3], T.mt4[0:1, 4:8], M23, M23, A.add, A.subtract, ["ma"], ["mg0"])
-    ts(T.mt4[0:1, 8:12], T.mgs[0:1, 0:12:3], -16.0, 100.0, A.mult, A.add, ["mg0"], ["mb"])
-    tt(T.mgs[0:1, 1:12:3], T.mt4[0:1, 8:12], T.mt4[0:1, 0:4], A.subtract, ["mb", "kr"], ["mg1"])
+    ts(T.mt4[:, 4:5], T.mt4[:, 3:4], -1.0 / 16, 92.5 / 16, A.mult, A.add, ["kr3"], ["ma"])
+    ts(T.mt4[:, 12:13], T.mt4[:, 3:4], -1.0, 116.0, A.mult, A.add, ["kr3"], ["c3"])
+    ts(T.mgs[:, 9:10], T.mt4[:, 4:5], M23, M23, A.add, A.subtract, ["ma"], ["a3"])
+    ts(T.fls[0:8, 0:1], T.pb[0:8, 2:3], -1.0, None, A.mult, None, ["pb"], ["fls"])
+    ts(T.mt4[:, 5:6], T.mgs[:, 9:10], -16.0, 100.0, A.mult, A.add, ["a3"], ["mb"])
+    ts(T.mt4[:, 13:14], T.mgs[:, 9:10], -1.0, float(S0 + R - 1), A.mult, A.add, ["a3"], ["c4"])
+    tt(T.mgs[:, 10:11], T.mt4[:, 5:6], T.mt4[:, 3:4], A.subtract, ["mb", "kr3"], ["b3"])
     dma("s", "dout", T.fl[:], T.fls[0:8, 0:1], ["fls"], [])
-    dma("s", "dout", T.mg[:], T.mgs[0:1, 0:12], ["mg0", "mg1", "mg2"], [])
+    dma("s", "dout", T.mg[:], T.mgs[0:1, 0:12], ["mg2"] + ["a%d" % t for t in range(R)] + ["b%d" % t for t in range(R)], [])
 
-    ts(T.fa[:], T.ft[:], 1.0 / 16, 1.0 - 71.5 / 16, A.mult, A.add, ["ft"], ["fa"])
+    act(T.fa[:], T.ft[:], -23.5 / 16, 1.0 / 16, ["ft"], ["fa"])
     ts(T.fb[:], T.ft[:], M23, M23, A.add, A.subtract, ["ft"], ["fb"])
+    ts(T.p2[:, 256:384], T.fb[:], T.mt4[:, 12:13], T.mt4[:, 13:14], A.is_equal, A.mult, ["fb", "c3", "c4"], ["p2"])
     ts(T.fa[:], T.fa[:], M23, M23, A.add, A.subtract, ["fa"], ["fa"])
-    ts(T.fb[:], T.fb[:], T.mt4[:, 12:13], 14.0, A.is_equal, A.mult, ["fb", "c3"], ["fb"])
-    tt(T.fc[:], T.fa[:], T.fb[:], A.max, ["fa", "fb"], ["fc"])
-    ts(T.fc[:], T.fc[:], -1.0, None, A.add, None, ["fc"], ["fc"])
+    tt(T.fc[:], T.p2[:, 256:384], T.fa[:], A.add, ["fa", "p2"], ["fc"])
     dma("a", "dout2", T.fs[:], T.fc[:], ["fc"], [])
 
     need("s", [("dout", count["dout"])])

@@ -8,6 +8,7 @@ S0 = 10
 NR = 8
 WIN = 6144
 LOW = -16000000
+WID = (10, 10, 12, 12)
 M31 = 1.5 * 2.0 ** 31
 M23 = 1.5 * 2.0 ** 23
 
@@ -19,7 +20,7 @@ SCRATCH = {
     "offu": ("sbuf", [128, 128], u16),
     "pin": ("sbuf", [128, 8], i32), "pf": ("sbuf", [128, 24], f32), "lef": ("sbuf", [128, 4], f32),
     "nid": ("sbuf", [128, W], f32), "n15": ("sbuf", [128, 128], bf), "n7": ("sbuf", [128, 128], bf),
-    "n3": ("sbuf", [128, 128], bf), "n4": ("sbuf", [128, 128], bf), "n31": ("sbuf", [128, 128], bf),
+    "n3": ("sbuf", [128, 128], bf), "n31": ("sbuf", [128, 128], bf),
     "tm": ("sbuf", [128, 16], bf), "big": ("sbuf", [128, 144], bf), "idn": ("sbuf", [128, 144], bf),
     "sel": ("sbuf", [128, 16], f16), "sel2": ("sbuf", [128, 16], f16), "sa": ("sbuf", [128, 32], bf),
     "rep": ("sbuf", [128, 128], f16), "cst": ("sbuf", [128, 16], f16),
@@ -44,7 +45,7 @@ SCRATCH = {
     "pc": ("sbuf", [128, 2 * W], bf), "ne": ("sbuf", [128, 2 * W], bf),
     "av": ("sbuf", [128, 128], bf), "pcd": ("sbuf", [128, 128], bf), "ee": ("sbuf", [128, 136], bf),
     "ss": ("sbuf", [128, 132], f32), "nd": ("sbuf", [128, 132], f32),
-    "mt": ("sbuf", [128, 128], f32), "zz": ("sbuf", [128, 128], f32),
+    "zz": ("sbuf", [128, 128], f32),
     "y0": ("sbuf", [128, 2048], bf), "yw": ("sbuf", [128, WIN], bf),
     "v0": ("sbuf", [128, 2048], f32), "fw": ("sbuf", [128, WIN], f32),
     "ft": ("sbuf", [128, 128], f32), "fa": ("sbuf", [128, 128], f32), "fb": ("sbuf", [128, 128], f32),
@@ -150,7 +151,8 @@ def rank_program(g, core, T, topo):
     CB = ["cb0", "cb1", "cb2", "cb3"]
     op("g", lambda: g.iota(T.pin[:, 0:1], [[0, 1]], 0, 1), [], ["pin0"])
     io(T.nid[:], [[1, W]], 0, ["nid"])
-    io(T.n4[0:8, :], [[1, 8], [0, 16]], 0, ["n4"])
+    io(T.onef[:], [[0, 128]], 0, ["onef"], base=1)
+    pick(T.g8[0:8, :], T.onef[0:8, :], [[-1, 8], [0, 16]], A.is_equal, 0, 1, ["onef"], ["g8"])
     io(T.n7[:], [[0, 16], [1, 8]], 0, ["n7"])
     io(T.n3[:], [[1, 16], [0, 8]], 0, ["n3"])
     io(T.n15[:], [[0, 8], [1, 16]], 0, ["n15"])
@@ -158,7 +160,6 @@ def rank_program(g, core, T, topo):
     io(T.cb[:], [[0, 4 * PITCH + 8]], 0, CB, base=200)
     io(T.low[:], [[0, 48]], 0, ["low"], base=LOW)
     io(T.kb[:], [[0, 48]], 0, ["kb"], base=LOW)
-    io(T.onef[:], [[0, 128]], 0, ["onef"], base=1)
     io(T.oneb[:], [[0, 144]], 0, ["oneb"], base=1)
     io(T.n31[0:32, :], [[0, 4], [1, 32]], 0, ["n31"])
     OH = ["oh%d" % x for x in range(13)]
@@ -174,9 +175,6 @@ def rank_program(g, core, T, topo):
     cp(T.pf[:, 0:6], T.pin[:, 0:6], ["pin%d" % i for i in range(6)], ["pf"])
     fP, fR, fH, fP3, fP7, fG16 = [T.pf[:, i:i + 1] for i in range(6)]
     ts(T.tm[:], T.nid[:, 0:16], fR, None, A.is_equal, None, ["nid", "pf"], ["tm"])
-    ts(T.big[:], T.nid[:, 0:144], -15.0, fG16, A.add, A.is_equal, ["nid", "pf"], ["big"])
-    ts(T.pf[:, 9:10], fR, 128.0, None, A.mult, None, ["pf"], ["pf9"])
-    ts(T.g8[0:8, :], T.n4[0:8, :], T.pf[0:8, 0:1], None, A.is_equal, None, ["n4", "pf"], ["g8"])
 
     ts(T.tmpi[:, 0:128], T.posi[:], 9, None, A.arith_shift_right, None, ["posi"], ["tmp0"])
     cp(T.hiu[:], T.tmpi[:, 0:128], ["tmp0"], ["hiu"])
@@ -188,7 +186,7 @@ def rank_program(g, core, T, topo):
         op("a", lambda: S.activation(T.mk[:, a:b], T.tm[:, 0:16].indirect(T.hiu[:, a // 16:b // 16]), AF.Copy),
            ["tm", "hiu"], ["mk%d" % i])
     act(T.fw[:, 0:2048], T.mk[:], 0.0, 0.0, ["mk%d" % i for i in range(NC)], ["fw"], fn=AF.Silu)
-    ts(T.jj[:], T.nid[:], T.pf[:, 9:10], -8.0, A.add, A.add, ["nid", "pf9"], ["jj"])
+    ts(T.big[:], T.nid[:, 0:144], -15.0, fG16, A.add, A.is_equal, ["nid", "pf"], ["big"])
     cp(T.lou[:], T.tmpi[:, 128:256], ["tmp1"], ["lou"])
     done_r = 0
     for i in range(NC):
@@ -197,16 +195,20 @@ def rank_program(g, core, T, topo):
            ["stw", "lou", "mk%d" % i], ["x%d" % i])
         if i == 0:
             cp(T.lef[0:8, 0:1], T.lei[0:8, 0:1], ["lei"], ["lef"])
+            ts(T.pf[:, 9:10], fR, 128.0, -8.0, A.mult, A.add, ["pf"], ["pf9"])
+        if i == 1:
+            ts(T.jj[:], T.nid[:], T.pf[:, 9:10], None, A.add, None, ["nid", "pf9"], ["jj"])
+        if i == NC - 2:
             mm(T.pb[:, 0:1], T.g8[0:8, :], T.lef[0:8, 0:1], True, True, ["g8", "lef"], ["pb"])
-            ts(T.jt[:], T.jj[:, 0:8], 0.0, 8192.0, A.is_lt, A.mult, ["jj"], ["jt"])
         while done_r < 16 and (i == NC - 1 or 128 * done_r + 144 <= b):
             r = done_r
             mm(T.e0[:, 0:W], T.big[:, 15 - r:143 - r], T.xx[:, 128 * r:128 * r + W], r == 0, r == 15,
                ["big", "xpad0", "xpad1"] + ["x%d" % k for k in range(i + 1)], ["e0"])
             done_r += 1
-    tt(T.jt[:], T.jt[:], T.jj[:, 0:8], A.add, ["jt", "jj"], ["jt"])
+    ts(T.inv[:, 0:8], T.jj[:, 0:8], 0.0, 15.0, A.is_lt, A.mult, ["jj"], ["inv0"])
+    ts(T.jt[:], T.jj[:, 0:8], T.pb[:, 0:1], 15.0, A.is_ge, A.mult, ["jj", "pb"], ["jt"])
     ts(T.inv[:, 8:W], T.jj[:, 8:W], T.pb[:, 0:1], 15.0, A.is_ge, A.mult, ["jj", "pb"], ["inv1"])
-    ts(T.inv[:, 0:8], T.jt[:], T.pb[:, 0:1], 15.0, A.is_ge, A.mult, ["jt", "pb"], ["inv0"])
+    tt(T.inv[:, 0:8], T.inv[:, 0:8], T.jt[:], A.max, ["jt", "inv0"], ["inv0"])
     tt(T.fo[:], T.e0[:, 0:W], T.inv[:], A.max, ["e0", "inv0", "inv1"], ["fo"])
 
     cores = list(T.cores)
@@ -223,7 +225,7 @@ def rank_program(g, core, T, topo):
         for d in range(1, len(chips)):
             row = on[chips[(i + d) % len(chips)]]
             out += [row[(m + k) % len(row)] for k in range(len(row))]
-        return out
+        return sorted(out, key=lambda x: topo.same_plane(topo.chip(c), topo.chip(x)) or topo.mates(topo.chip(c), topo.chip(x)))
 
     far = far_of(core)
     near = [c for c in on[topo.chip(core)] if c != core]
@@ -235,6 +237,11 @@ def rank_program(g, core, T, topo):
     def did(c):
         a = topo.addr(c)
         return DstId(rid=a[0], pnc=a[1])
+
+    def vectors(rs):
+        for r in rs:
+            op("a", lambda: S.activation(T.y0[:, r:2048:16], T.vew[:, 0:8192].indirect(T.pou[:, 8 * r:8 * r + 8]),
+                                         AF.Copy), ["vew", "pou"], ["y0_%d" % r])
 
     def codes_out(banks):
         for b in banks:
@@ -254,6 +261,7 @@ def rank_program(g, core, T, topo):
     for t in range(R):
         NS = S0 + t
         last = t == R - 1
+        wd = WID[t]
         if t == 0:
             n8, nm, nsel, sel, sk = 8 * NS, 8 * NS, 16, T.sel, "sel"
             for x in range(NS):
@@ -272,9 +280,7 @@ def rank_program(g, core, T, topo):
             ts(T.rep[:], T.n15[:], fP3, 256.0, A.is_equal, A.mult, ["n15", "pf"], ["rep"])
             ts(T.cst[:], T.nid[:, 0:16], -16.0 / 2048, T.pf[:, 7:8], A.mult, A.add, ["nid", "pf7"], ["cst"])
             ts(T.t16[:], T.fo[:], -16.0, 100.0, A.mult, A.add, ["fo"], ["t16"])
-            for r in range(16):
-                op("a", lambda: S.activation(T.y0[:, r:2048:16], T.vew[:, 0:8192].indirect(T.pou[:, 8 * r:8 * r + 8]),
-                                             AF.Copy), ["vew", "pou"], ["y0_%d" % r])
+            vectors(range(0, 10))
             mask, mk_ = T.dm2, "dm2"
         else:
             nm = 32
@@ -296,13 +302,14 @@ def rank_program(g, core, T, topo):
                 tt(T.alv[:], T.alv[:], T.ne[:, 0:W], A.mult, ["alv", "ne"], ["alv"])
             tt(T.fo[:], M1, T.ne[:, W:2 * W], A.mult, ["e1", "ne"], ["fo"])
             off = NS - 1
-            act(T.ded[:], T.alv[:], 1.0, -1.0, ["alv"], ["ded"])
-            ts(T.t16[:], T.fo[:], -16.0, 100.0 - 17 * off, A.mult, A.add, ["fo"], ["t16"])
-            tt(T.mt4[:, u:u + 1], K, RK, A.subtract, KR, ["kr%d" % u])
-            tt(T.cd[:, 1:W], T.t16[:, 0:W - 1], T.fo[:, 1:W], A.subtract, ["t16", "fo"], ["cd"])
+            act(T.mt4[:, u:u + 1], RK, K, -1.0, KR, ["kr%d" % u])
             act(T.mt4[:, 6:7], RK, 256.0, 1.0, KR, ["r256"])
+            act(T.mt4[:, 4:5], T.mt4[:, u:u + 1], 92.5 / 16, -1.0 / 16, ["kr%d" % u], ["ma"])
             act(T.lc[0:32, 0:128], T.ec[0:32, 128 * u:128 * u + 128], 0.0, T.pf[0:32, 12:13], ["ec", "sA"], ["lc0"])
             act(T.lc[0:32, 128:256], T.ec[0:32, 128 * u:128 * u + 128], 0.0, T.pf[0:32, 13:14], ["ec", "sB1"], ["lc1"])
+            act(T.ded[:], T.alv[:], 1.0, -1.0, ["alv"], ["ded"])
+            ts(T.t16[:], T.fo[:], -16.0, 100.0 - 17 * off, A.mult, A.add, ["fo"], ["t16"])
+            tt(T.cd[:, 1:W], T.t16[:, 0:W - 1], T.fo[:, 1:W], A.subtract, ["t16", "fo"], ["cd"])
             if last:
                 act(T.pcd[:], T.alv[:, 8:136], 200.0, -200.0, ["alv"], ["pcd"])
             else:
@@ -311,15 +318,16 @@ def rank_program(g, core, T, topo):
                 for x in range(0 if t == 1 else 1, NS + 1):
                     act(T.oh[:, PITCH * x:PITCH * x + 129], T.fo[:, 7:136], off - x + 0.5, 1.0, ["fo"], ["oh%d" % x],
                         fn=AF.Sign)
+                vectors(range(7 + 3 * t, 10 + 3 * t))
             mask, mk_ = T.dm, "dm"
 
         tt(T.mm[0:n8, 0:nm], T.p1[0:n8, 0:nm], mask[0:n8, 0:nm], A.mult, ["p1", mk_], ["mm"])
         mm(T.p2[0:nm, 0:nsel], T.mm[0:n8, 0:nm], sel[0:n8, 0:nsel], True, True, ["mm", sk], ["p2"])
         if t > 0:
-            ts(T.mt4[:, 4:5], T.mt4[:, u:u + 1], -1.0 / 16, 92.5 / 16, A.mult, A.add, ["kr%d" % u], ["ma"])
-        pay = T.pay[:, 16 * t:16 * t + 16]
-        cp(pay, T.p2[:, 0:16], ["p2"], ["pay%d" % t])
-        slot = T.land[:, 16 * (NR * t + rank):16 * (NR * t + rank) + 16]
+            tt(T.d1[:, 1:W], T.cd[:, 1:W], T.alv[:, 1:W], A.mult, ["cd", "alv"], ["d1"])
+        pay = T.pay[:, 16 * t:16 * t + wd]
+        cp(pay, T.p2[:, 0:wd], ["p2"], ["pay%d" % t])
+        slot = T.land[:, 16 * (NR * t + rank):16 * (NR * t + rank) + wd]
         order("g", ["pay%d" % t], [])
         sem = T.sem["ar%d_%d" % (t, rank)]
         g.remote_dma_fused([
@@ -345,18 +353,20 @@ def rank_program(g, core, T, topo):
             if t == 1:
                 pick(T.idn[:], T.oneb[:], [[-1, 144]], A.is_equal, 0, 1, ["oneb"], ["idn"])
                 pick(T.tri[:], T.onef[:], [[1, 128]], A.is_gt, 0, -1, ["onef"], ["tri"])
-                pick(T.tri[:], T.tri[:], [[-16, 8], [0, 16]], A.is_ge, 0, 1, ["tri"], ["tri"])
             if t == 2:
-                pick(T.gsel[:], T.onef[:, 0:8], [[-16, 8]], A.is_ge, 0, 1, ["onef"], ["gsel"])
-                pick(T.gsel[:], T.gsel[:], [[16, 8]], A.is_ge, 15, -1, ["gsel"], ["gsel"])
                 io(T.neg[:], [[0, 128]], 0, ["neg"], base=-1)
                 io(T.ee[:, 128:136], [[0, 8]], 0, ["eepad"])
-            tt(T.d1[:, 1:W], T.cd[:, 1:W], T.alv[:, 1:W], A.mult, ["cd", "alv"], ["d1"])
-            ts(T.mgs[:, 3 * u:3 * u + 1], T.mt4[:, 4:5], M23, M23, A.add, A.subtract, ["ma"], ["a%d" % u])
+            if last:
+                pick(T.tri[:], T.tri[:], [[-16, 8], [0, 16]], A.is_ge, 0, 1, ["tri"], ["tri"])
+                pick(T.gsel[:], T.onef[:, 0:8], [[-16, 8]], A.is_ge, 0, 1, ["onef"], ["gsel"])
+                pick(T.gsel[:], T.gsel[:], [[16, 8]], A.is_ge, 15, -1, ["gsel"], ["gsel"])
             scan(T.pc[:, 2 * W - 2:W - 1:-1], T.ded[:, W - 1:0:-1], T.d1[:, W - 1:0:-1], 0.0, A.mult, A.add,
                  ["ded", "d1"], ["pcr"])
+            ts(T.mgs[:, 3 * u:3 * u + 1], T.mt4[:, 4:5], M23, M23, A.add, A.subtract, ["ma"], ["a%d" % u])
             if last:
-                codes_out([0, 2])
+                codes_out([0, 2, 3, 1])
+            if not last:
+                scan(T.pc[:, 1:W], T.ded[:, 1:W], T.d1[:, 1:W], 0.0, A.mult, A.add, ["ded", "d1"], ["pcl"])
             ts(T.mt4[:, 5:6], T.mgs[:, 3 * u:3 * u + 1], -16.0, 100.0, A.mult, A.add, ["a%d" % u], ["mb"])
             ts(T.ld[0:32, 0:128], T.n31[0:32, :], T.mgs[0:32, 3 * u:3 * u + 1], T.pf[0:32, 12:13], A.is_equal, A.mult,
                ["n31", "sA", "a%d" % u], ["ld0"])
@@ -364,14 +374,13 @@ def rank_program(g, core, T, topo):
             if t == 1:
                 ts(T.kb[:, 0:16], T.p3[:, 0:16], sLow, None, A.add, None, ["p3", "sLow"], ["kb"])
             if not last:
-                scan(T.pc[:, 1:W], T.ded[:, 1:W], T.d1[:, 1:W], 0.0, A.mult, A.add, ["ded", "d1"], ["pcl"])
+                tt(T.cb[:, 0:129], T.pc[:, PCR + 8:PCR + 137], T.w4[:, 8:137], A.add, ["pcr", "w4"], ["cb0"])
             ts(T.ld[0:32, 128:256], T.n31[0:32, :], T.mgs[0:32, 3 * u + 1:3 * u + 2], T.pf[0:32, 14:15], A.is_equal, A.mult,
                ["n31", "sB2", "b%d" % u], ["ld1"])
             ts(T.ht[:], T.kb[:, 0:16], K, T.mt4[:, 6:7], A.is_equal, A.mult, ["kb", "r256"] + KR, ["ht"])
             tt(T.lab[0:32, :], T.lc[0:32, :], T.ld[0:32, :], A.subtract, ["lc0", "ld0", "lc1", "ld1"], ["lab"])
             tt(T.hs[:], T.kb[:, 0:16], T.ht[:], A.subtract, ["kb", "ht"], ["hs"])
             if not last:
-                tt(T.cb[:, 0:129], T.pc[:, PCR + 8:PCR + 137], T.w4[:, 8:137], A.add, ["pcr", "w4"], ["cb0"])
                 tt(T.cb[:, PITCH + 1:PITCH + 129], T.pc[:, PCL + 7:PCL + 135], T.w4[:, 8:136], A.add, ["pcl", "w4"], ["cb1"])
         if not last:
             tt(T.nq[:, 7:136], T.pc[:, PCL + 7:PCL + 136], T.cb[:, 0:129], A.not_equal, ["pcl", "cb0"], ["nq"])
@@ -379,7 +388,7 @@ def rank_program(g, core, T, topo):
             tt(T.cb[:, 2 * PITCH + 1:2 * PITCH + 129], T.nq[:, 8:136], T.pc[:, PCL + 8:PCL + 136], A.add, ["nq", "pcl"], ["cb2"])
             tt(T.cb[:, 3 * PITCH + 1:3 * PITCH + 129], T.nq[:, 7:135], T.pc[:, PCL + 7:PCL + 135], A.add, ["nq", "pcl"], ["cb3"])
         if t == 0:
-            ms(T.pb[:, 48:64], 0.0, ["pb"])
+            ms(T.pb[:, 32:64], 0.0, ["pb"])
             ts(T.pf[:, 10:11], fP3, 0.0, 256.0, A.is_equal, A.mult, ["pf"], ["s0"])
             ts(T.pf[:, 11:12], fP3, 2.0, 256.0, A.is_equal, A.mult, ["pf"], ["s2"])
             ts(sB2, fP3, 1.0, 256.0, A.is_equal, A.mult, ["pf"], ["sB2"])
@@ -391,12 +400,12 @@ def rank_program(g, core, T, topo):
             ts(T.sa[:, 16:32], T.nid[:, 1:17], fP3, 0.5, A.is_equal, A.mult, ["nid", "pf"], ["sa1"])
             ts(T.val[:], T.jj[:, 8:136], T.pb[:, 0:1], None, A.is_lt, None, ["jj", "pb"], ["val"])
             tt(T.sel2[:], T.sa[:, 0:16], T.sa[:, 16:32], A.subtract, ["sa0", "sa1"], ["sel2"])
-            ms(T.yw[:, 0:1024], 0.0, ["yw"])
         if t == 1:
-            ms(T.yw[:, 1024:2048], 0.0, ["yw2"])
-        if t == 2:
+            io(T.yw[:, 0:1024], [[0, 1024]], 0, ["yw"])
             act(T.tt[:], T.jj[:, 8:136], 4096.0, -1.0, ["jj"], ["tt"])
             act(T.pf[:, 8:9], T.jj[:, 135:136], 4095.0, -1.0, ["jj"], ["pf8"])
+        if t == 2:
+            io(T.yw[:, 1024:2048], [[0, 1024]], 0, ["yw2"])
         if last:
             tt(T.av[:], T.alv[:, 8:136], T.val[:], A.mult, ["alv", "val"], ["av"])
             tt(T.pcd[:], T.pcd[:], T.d1[:, 8:136], A.add, ["pcd", "d1"], ["pcd"])
@@ -407,10 +416,10 @@ def rank_program(g, core, T, topo):
             tt(T.nd[:, 1:128], T.zz[:, 0:127], T.zz[:, 1:128], A.subtract, ["zz"], ["nd1"])
             ts(T.nd[:, 0:1], T.zz[:, 0:1], -1.0, None, A.mult, None, ["zz"], ["nd0"])
 
-        srcs = [(T.pay[0:nm, 16 * t:16 * t + 16], None)]
+        srcs = [(T.pay[0:nm, 16 * t:16 * t + wd], None)]
         for c, n in senders:
             s = T.rank_of(c)
-            srcs.append((T.land[0:nm, 16 * (NR * t + s):16 * (NR * t + s) + 16], ("ar%d_%d" % (t, s), n)))
+            srcs.append((T.land[0:nm, 16 * (NR * t + s):16 * (NR * t + s) + wd], ("ar%d_%d" % (t, s), n)))
         if t == 0:
             mm(T.p3[:, 0:16], T.rep[:], T.cst[:], True, False, ["rep", "cst"], ["p3"])
         else:
@@ -420,12 +429,10 @@ def rank_program(g, core, T, topo):
             if tok:
                 need("p", [tok])
             if t == 0:
-                mm(T.p3[:, 0:16], T.rep[0:nm, :], src, False, end, ["pay0"], ["p3"])
+                mm(T.p3[:, 0:wd], T.rep[0:nm, :], src, False, end, ["pay0"], ["p3"])
             else:
-                mm(T.pb[:, 32:48], T.lab[0:32, 128:256], src, i == 0, end, ["lab", "pay%d" % t], ["pb"])
-                mm(T.p3[:, 0:16], T.lab[0:32, 0:128], src, False, end, ["lab"], ["p3"])
-        if last:
-            codes_out([1, 3])
+                mm(T.pb[:, 32:32 + wd], T.lab[0:32, 128:256], src, i == 0, end, ["lab", "pay%d" % t], ["pb"])
+                mm(T.p3[:, 0:wd], T.lab[0:32, 0:128], src, False, end, ["lab"], ["p3"])
         K, RK = T.kk[:, t:t + 1], T.rr[:, t:t + 1]
         if t == 0:
             scan(T.sc[:], T.p3[:, 0:48], T.low[:], -1.0e9, A.max, A.max, ["p3", "low"], ["sc"])
@@ -447,8 +454,8 @@ def rank_program(g, core, T, topo):
     op("a", lambda: S.activation(T.fw[:, 0:WIN].indirect(T.offu[:, 0:128]), T.v0[:], AF.Silu),
        ["offu"] + ["v0_%d" % r for r in range(16)], ["fw"])
     cp(T.yw[:, 0:WIN].indirect(T.offu[:, 0:128]), T.y0[:], ["offu"] + ["y0_%d" % r for r in range(16)], ["yw", "yw2"])
-    dma("a", "dft", T.ft[:], T.fw[0:128:16, 0:2048], ["fw"], ["ft"])
-    dma("s", "dout", T.y[:], T.yw[:, 0:2048], ["yw"], [])
+    dma("s", "dft", T.ft[:], T.fw[0:128:16, 0:2048], ["fw"], ["ft"])
+    dma("a", "dout2", T.y[:], T.yw[:, 0:2048], ["yw", "fw"], [])
 
     KR = ["kk%d" % t for t in range(R)] + ["rr%d" % t for t in range(R)]
     mm(T.pb[0:8, 2:3], T.gsel[:], T.ss[:, 128:129], True, True, ["gsel", "ss"], ["pb"])
@@ -461,15 +468,15 @@ def rank_program(g, core, T, topo):
     ts(T.mt4[:, 5:6], T.mgs[:, 9:10], -16.0, 100.0, A.mult, A.add, ["a3"], ["mb"])
     ts(T.mt4[:, 13:14], T.mgs[:, 9:10], -1.0, float(S0 + R - 1), A.mult, A.add, ["a3"], ["c4"])
     tt(T.mgs[:, 10:11], T.mt4[:, 5:6], T.mt4[:, 3:4], A.subtract, ["mb", "kr3"], ["b3"])
-    dma("s", "dout", T.fl[:], T.fls[0:8, 0:1], ["fls"], [])
-    dma("s", "dout", T.mg[:], T.mgs[0:1, 0:12], ["mg2"] + ["a%d" % t for t in range(R)] + ["b%d" % t for t in range(R)], [])
 
     act(T.fa[:], T.ft[:], -23.5 / 16, 1.0 / 16, ["ft"], ["fa"])
+    dma("a", "dout2", T.fl[:], T.fls[0:8, 0:1], ["fls"], [])
+    dma("a", "dout2", T.mg[:], T.mgs[0:1, 0:12], ["mg2"] + ["a%d" % t for t in range(R)] + ["b%d" % t for t in range(R)], [])
     ts(T.fb[:], T.ft[:], M23, M23, A.add, A.subtract, ["ft"], ["fb"])
     ts(T.p2[:, 256:384], T.fb[:], T.mt4[:, 12:13], T.mt4[:, 13:14], A.is_equal, A.mult, ["fb", "c3", "c4"], ["p2"])
     ts(T.fa[:], T.fa[:], M23, M23, A.add, A.subtract, ["fa"], ["fa"])
     tt(T.fc[:], T.p2[:, 256:384], T.fa[:], A.add, ["fa", "p2"], ["fc"])
-    dma("a", "dout2", T.fs[:], T.fc[:], ["fc"], [])
+    dma("s", "dout", T.fs[:], T.fc[:], ["fc"], [])
 
     need("s", [("dout", count["dout"])])
     need("a", [("dout2", count["dout2"]), ("ca", count["ca"])])

@@ -296,20 +296,19 @@ def rank_program(g, core, T, topo):
                    k == 0, k == 16, OH + ["eb"], ["p1"])
             ts(T.ne[:], T.pc[:], RK, K, A.add, A.not_equal, ["pcl", "pcr"] + KR, ["ne"])
             tt(M1, FM, T.ne[:, 0:W], A.mult, ["e1", "ne"], ["e1"])
+            tt(T.fo[:], M1, T.ne[:, W:2 * W], A.mult, ["e1", "ne"], ["fo"])
             if t == 1:
                 cp(T.alv[:], T.ne[:, 0:W], ["ne"], ["alv"])
             else:
                 tt(T.alv[:], T.alv[:], T.ne[:, 0:W], A.mult, ["alv", "ne"], ["alv"])
-            tt(T.fo[:], M1, T.ne[:, W:2 * W], A.mult, ["e1", "ne"], ["fo"])
             off = NS - 1
             act(T.mt4[:, u:u + 1], RK, K, -1.0, KR, ["kr%d" % u])
             act(T.mt4[:, 6:7], RK, 256.0, 1.0, KR, ["r256"])
             act(T.mt4[:, 4:5], T.mt4[:, u:u + 1], 92.5 / 16, -1.0 / 16, ["kr%d" % u], ["ma"])
             act(T.lc[0:32, 0:128], T.ec[0:32, 128 * u:128 * u + 128], 0.0, T.pf[0:32, 12:13], ["ec", "sA"], ["lc0"])
-            act(T.lc[0:32, 128:256], T.ec[0:32, 128 * u:128 * u + 128], 0.0, T.pf[0:32, 13:14], ["ec", "sB1"], ["lc1"])
+            act(T.lc[0:32, 128:144], T.ec[0:32, 128 * u:128 * u + 16], 0.0, T.pf[0:32, 13:14], ["ec", "sB1"], ["lc1"])
             act(T.ded[:], T.alv[:], 1.0, -1.0, ["alv"], ["ded"])
             ts(T.t16[:], T.fo[:], -16.0, 100.0 - 17 * off, A.mult, A.add, ["fo"], ["t16"])
-            tt(T.cd[:, 1:W], T.t16[:, 0:W - 1], T.fo[:, 1:W], A.subtract, ["t16", "fo"], ["cd"])
             if last:
                 act(T.pcd[:], T.alv[:, 8:136], 200.0, -200.0, ["alv"], ["pcd"])
             else:
@@ -324,10 +323,13 @@ def rank_program(g, core, T, topo):
         tt(T.mm[0:n8, 0:nm], T.p1[0:n8, 0:nm], mask[0:n8, 0:nm], A.mult, ["p1", mk_], ["mm"])
         mm(T.p2[0:nm, 0:nsel], T.mm[0:n8, 0:nm], sel[0:n8, 0:nsel], True, True, ["mm", sk], ["p2"])
         if t > 0:
-            tt(T.d1[:, 1:W], T.cd[:, 1:W], T.alv[:, 1:W], A.mult, ["cd", "alv"], ["d1"])
+            ts(T.mgs[:, 3 * u:3 * u + 1], T.mt4[:, 4:5], M23, M23, A.add, A.subtract, ["ma"], ["a%d" % u])
         pay = T.pay[:, 16 * t:16 * t + wd]
         cp(pay, T.p2[:, 0:wd], ["p2"], ["pay%d" % t])
         slot = T.land[:, 16 * (NR * t + rank):16 * (NR * t + rank) + wd]
+        if t > 0:
+            tt(T.cd[:, 1:W], T.t16[:, 0:W - 1], T.fo[:, 1:W], A.subtract, ["t16", "fo"], ["cd"])
+            tt(T.d1[:, 1:W], T.cd[:, 1:W], T.alv[:, 1:W], A.mult, ["cd", "alv"], ["d1"])
         order("g", ["pay%d" % t], [])
         sem = T.sem["ar%d_%d" % (t, rank)]
         g.remote_dma_fused([
@@ -362,7 +364,6 @@ def rank_program(g, core, T, topo):
                 pick(T.gsel[:], T.gsel[:], [[16, 8]], A.is_ge, 15, -1, ["gsel"], ["gsel"])
             scan(T.pc[:, 2 * W - 2:W - 1:-1], T.ded[:, W - 1:0:-1], T.d1[:, W - 1:0:-1], 0.0, A.mult, A.add,
                  ["ded", "d1"], ["pcr"])
-            ts(T.mgs[:, 3 * u:3 * u + 1], T.mt4[:, 4:5], M23, M23, A.add, A.subtract, ["ma"], ["a%d" % u])
             if last:
                 codes_out([0, 2, 3, 1])
             if not last:
@@ -375,11 +376,12 @@ def rank_program(g, core, T, topo):
                 ts(T.kb[:, 0:16], T.p3[:, 0:16], sLow, None, A.add, None, ["p3", "sLow"], ["kb"])
             if not last:
                 tt(T.cb[:, 0:129], T.pc[:, PCR + 8:PCR + 137], T.w4[:, 8:137], A.add, ["pcr", "w4"], ["cb0"])
-            ts(T.ld[0:32, 128:256], T.n31[0:32, :], T.mgs[0:32, 3 * u + 1:3 * u + 2], T.pf[0:32, 14:15], A.is_equal, A.mult,
+            ts(T.ld[0:32, 128:144], T.n31[0:32, 0:16], T.mgs[0:32, 3 * u + 1:3 * u + 2], T.pf[0:32, 14:15], A.is_equal, A.mult,
                ["n31", "sB2", "b%d" % u], ["ld1"])
-            ts(T.ht[:], T.kb[:, 0:16], K, T.mt4[:, 6:7], A.is_equal, A.mult, ["kb", "r256"] + KR, ["ht"])
-            tt(T.lab[0:32, :], T.lc[0:32, :], T.ld[0:32, :], A.subtract, ["lc0", "ld0", "lc1", "ld1"], ["lab"])
-            tt(T.hs[:], T.kb[:, 0:16], T.ht[:], A.subtract, ["kb", "ht"], ["hs"])
+            keys, kn = (T.kb[:, 0:16], "kb") if t == 1 else (T.p3[:, 0:16], "p3")
+            ts(T.ht[:], keys, K, T.mt4[:, 6:7], A.is_equal, A.mult, [kn, "r256"] + KR, ["ht"])
+            tt(T.lab[0:32, 0:144], T.lc[0:32, 0:144], T.ld[0:32, 0:144], A.subtract, ["lc0", "ld0", "lc1", "ld1"], ["lab"])
+            tt(T.hs[:], keys, T.ht[:], A.subtract, [kn, "ht"], ["hs"])
             if not last:
                 tt(T.cb[:, PITCH + 1:PITCH + 129], T.pc[:, PCL + 7:PCL + 135], T.w4[:, 8:136], A.add, ["pcl", "w4"], ["cb1"])
         if not last:
@@ -388,7 +390,6 @@ def rank_program(g, core, T, topo):
             tt(T.cb[:, 2 * PITCH + 1:2 * PITCH + 129], T.nq[:, 8:136], T.pc[:, PCL + 8:PCL + 136], A.add, ["nq", "pcl"], ["cb2"])
             tt(T.cb[:, 3 * PITCH + 1:3 * PITCH + 129], T.nq[:, 7:135], T.pc[:, PCL + 7:PCL + 135], A.add, ["nq", "pcl"], ["cb3"])
         if t == 0:
-            ms(T.pb[:, 32:64], 0.0, ["pb"])
             ts(T.pf[:, 10:11], fP3, 0.0, 256.0, A.is_equal, A.mult, ["pf"], ["s0"])
             ts(T.pf[:, 11:12], fP3, 2.0, 256.0, A.is_equal, A.mult, ["pf"], ["s2"])
             ts(sB2, fP3, 1.0, 256.0, A.is_equal, A.mult, ["pf"], ["sB2"])
@@ -431,15 +432,11 @@ def rank_program(g, core, T, topo):
             if t == 0:
                 mm(T.p3[:, 0:wd], T.rep[0:nm, :], src, False, end, ["pay0"], ["p3"])
             else:
-                mm(T.pb[:, 32:32 + wd], T.lab[0:32, 128:256], src, i == 0, end, ["lab", "pay%d" % t], ["pb"])
+                for q in range(0, 128, 32):
+                    mm(T.p3[q:q + wd, 0:16], src, T.lab[0:32, 128:144], False, False, ["lab", "pay%d" % t], ["p3"])
                 mm(T.p3[:, 0:wd], T.lab[0:32, 0:128], src, False, end, ["lab"], ["p3"])
         K, RK = T.kk[:, t:t + 1], T.rr[:, t:t + 1]
-        if t == 0:
-            scan(T.sc[:], T.p3[:, 0:48], T.low[:], -1.0e9, A.max, A.max, ["p3", "low"], ["sc"])
-        else:
-            op("v", lambda: V.transpose(T.t2[:], T.pb[:, 32:64]), ["pb"], ["t2"])
-            tt(T.kb[:, 0:16], T.p3[:, 0:16], T.t2[:, 0:16], A.add, ["p3", "t2"], ["kb"])
-            scan(T.sc[:], T.kb[:], T.low[:], -1.0e9, A.max, A.max, ["kb", "low"], ["sc"])
+        scan(T.sc[:], T.p3[:, 0:48], T.low[:], -1.0e9, A.max, A.max, ["p3", "low"], ["sc"])
         op("v", lambda: V.transpose(T.tr[:], T.sc[:, 16:48]), ["sc"], ["tr"])
         op("v", lambda: V.tensor_reduce(K, T.tr[:], AX.X, A.max), ["tr"], ["kk%d" % t])
         ts(RK, K, M31, M31, A.add, A.subtract, ["kk%d" % t], ["rr%d" % t])

@@ -1,56 +1,59 @@
 from concourse.bass import DstId, RemoteDMATransfer
-from concourse.mybir import AluOpType as A, AxisListType as AX, ActivationFunctionType as AF
+from concourse.mybir import AluOpType as A, ActivationFunctionType as AF
 
 W = 152
-PITCH = 136
 R = 4
 S0 = 10
 NR = 8
 WIN = 6144
 LOW = -16000000
+BASE = 102
 WID = (10, 10, 12, 12)
+SLOT = {1: (10, 12, 11), 2: (11, 11, 12), 3: (12, 10, 13)}
+PA, PB = 132, 130
 M31 = 1.5 * 2.0 ** 31
 M23 = 1.5 * 2.0 ** 23
+AOFF = 192
+BOFF = BASE + 16 * AOFF
 
 f32, bf, f16, i32, u16 = "float32", "bfloat16", "float16", "int32", "uint16"
 SCRATCH = {
     "posi": ("sbuf", [128, 128], i32), "stw": ("sbuf", [128, 512], i32), "lei": ("sbuf", [128, 4], i32),
-    "vew": ("sbuf", [128, 8192], bf), "tmpi": ("sbuf", [128, 256], i32),
+    "vew": ("sbuf", [128, 8192], bf), "tmpi": ("sbuf", [128, 128], i32),
     "hiu": ("sbuf", [128, 128], u16), "lou": ("sbuf", [128, 128], u16), "pou": ("sbuf", [128, 128], u16),
     "offu": ("sbuf", [128, 128], u16),
     "pin": ("sbuf", [128, 8], i32), "pf": ("sbuf", [128, 24], f32), "lef": ("sbuf", [128, 4], f32),
-    "nid": ("sbuf", [128, W], f32), "n15": ("sbuf", [128, 128], bf), "n7": ("sbuf", [128, 128], bf),
-    "n3": ("sbuf", [128, 128], bf), "n31": ("sbuf", [128, 128], bf),
+    "nid": ("sbuf", [128, W], f32), "n31": ("sbuf", [128, 128], bf), "n16": ("sbuf", [128, 16], f32),
     "tm": ("sbuf", [128, 16], bf), "big": ("sbuf", [128, 144], bf), "idn": ("sbuf", [128, 144], bf),
-    "sel": ("sbuf", [128, 16], f16), "sel2": ("sbuf", [128, 16], f16), "sa": ("sbuf", [128, 32], bf),
-    "rep": ("sbuf", [128, 128], f16), "cst": ("sbuf", [128, 16], f16),
-    "dm": ("sbuf", [128, 128], bf), "dm2": ("sbuf", [128, 128], bf), "g8": ("sbuf", [128, 128], f32),
+    "sel": ("sbuf", [128, 48], bf), "rows": ("sbuf", [128, 12], f32), "slb": ("sbuf", [128, 4], bf), "aa": ("sbuf", [128, 384], bf),
+    "rep": ("sbuf", [128, 128], f16), "repf": ("sbuf", [128, 128], f32),
+    "dm": ("sbuf", [128, 144], bf), "g8": ("sbuf", [128, 128], f32),
     "onef": ("sbuf", [128, 128], f32), "oneb": ("sbuf", [128, 144], bf), "ec": ("sbuf", [128, 384], bf),
     "tri": ("sbuf", [128, 128], f32), "gsel": ("sbuf", [128, 8], f32),
-    "idf": ("sbuf", [128, 128], f32), "hs": ("sbuf", [128, 16], f32), "ht": ("sbuf", [128, 16], f32),
-    "kb": ("sbuf", [128, 48], f32), "t2": ("sbuf", [128, 32], f32),
-    "lab": ("sbuf", [128, 256], f16), "lc": ("sbuf", [128, 256], bf), "ld": ("sbuf", [128, 256], bf),
-    "cb": ("sbuf", [128, 4 * PITCH + 8], bf), "eb": ("sbuf", [128, 4 * PITCH + 8], bf),
-    "w4": ("sbuf", [128, W], bf), "nq": ("sbuf", [128, W], bf),
+    "hs": ("sbuf", [128, 16], f32), "ht": ("sbuf", [128, 16], f32),
+    "lab": ("sbuf", [128, 144], f16), "lc": ("sbuf", [128, 432], bf), "ld": ("sbuf", [128, 144], bf),
+    "cb": ("sbuf", [128, 3 * PA + 8], bf), "cc": ("sbuf", [128, 3 * PB + 8], bf), "eb": ("sbuf", [128, 3 * PA], bf),
+    "nq": ("sbuf", [128, 136], bf), "fst": ("sbuf", [128, W], bf), "alx": ("sbuf", [128, W], bf),
     "jj": ("sbuf", [128, W], f32), "jt": ("sbuf", [128, 8], f32), "inv": ("sbuf", [128, W], bf),
-    "val": ("sbuf", [128, 128], bf), "tt": ("sbuf", [128, 128], f32),
-    "mk": ("sbuf", [128, 2048], bf), "xx": ("sbuf", [128, 2072], bf), "oh": ("sbuf", [128, 13 * PITCH + 8], bf),
-    "mm": ("sbuf", [128, 128], f16), "pay": ("sbuf", [128, 16 * R], f16), "land": ("sbuf", [128, 16 * NR * R], f16),
+    "tt": ("sbuf", [128, 128], f32),
+    "mk": ("sbuf", [128, 2048], bf), "xx": ("sbuf", [128, 2072], bf),
+    "oh": ("sbuf", [128, 11 * PA + 8], bf), "oi": ("sbuf", [128, 12 * PB + 8], bf),
+    "mm": ("sbuf", [128, 48], f16), "pay": ("sbuf", [128, 16 * R], f16), "land": ("sbuf", [128, 16 * NR * R], f16),
     "neg": ("sbuf", [128, 128], bf), "low": ("sbuf", [128, 48], f32),
-    "sc": ("sbuf", [128, 48], f32), "tr": ("sbuf", [128, 32], f32),
-    "kk": ("sbuf", [128, 4], f32), "rr": ("sbuf", [128, 4], f32),
-    "fo": ("sbuf", [128, W], bf),
-    "alv": ("sbuf", [128, W], bf), "ded": ("sbuf", [128, W], bf), "t16": ("sbuf", [128, W], bf),
+    "sc": ("sbuf", [128, 48], f32), "tr": ("sbuf", [128, 36], f32), "rnd": ("sbuf", [128, 36], f32),
+    "kk": ("sbuf", [128, 36 * R], f32),
+    "fo": ("sbuf", [128, W], bf), "ded": ("sbuf", [128, W], bf),
     "cd": ("sbuf", [128, W], bf), "d1": ("sbuf", [128, W], bf),
     "pc": ("sbuf", [128, 2 * W], bf), "ne": ("sbuf", [128, 2 * W], bf),
-    "av": ("sbuf", [128, 128], bf), "pcd": ("sbuf", [128, 128], bf), "ee": ("sbuf", [128, 136], bf),
+    "ee": ("sbuf", [128, 136], bf),
     "ss": ("sbuf", [128, 132], f32), "nd": ("sbuf", [128, 132], f32),
     "zz": ("sbuf", [128, 128], f32),
     "y0": ("sbuf", [128, 2048], bf), "yw": ("sbuf", [128, WIN], bf),
     "v0": ("sbuf", [128, 2048], f32), "fw": ("sbuf", [128, WIN], f32),
     "ft": ("sbuf", [128, 128], f32), "fa": ("sbuf", [128, 128], f32), "fb": ("sbuf", [128, 128], f32),
     "fc": ("sbuf", [128, 128], f32),
-    "mgs": ("sbuf", [128, 12], f32), "mt4": ("sbuf", [128, 16], f32), "fls": ("sbuf", [128, 4], f32),
+    "mgs": ("sbuf", [128, 12], f32), "nk": ("sbuf", [128, 4], f32), "wa": ("sbuf", [128, 4], bf),
+    "wb": ("sbuf", [128, 4], f32), "mt4": ("sbuf", [128, 8], f32), "fls": ("sbuf", [128, 4], f32),
     "p1": ("psum", [128, 512], f32), "p2": ("psum", [128, 512], f32), "p3": ("psum", [128, 512], f32),
     "pb": ("psum", [128, 512], f32), "e0": ("psum", [128, 512], f32), "e1": ("psum", [128, 512], f32),
     "e2": ("psum", [128, 512], f32), "e3": ("psum", [128, 512], f32),
@@ -140,54 +143,96 @@ def rank_program(g, core, T, topo):
     def io(out, pat, cm, w, base=0):
         op("g", lambda: g.iota(out, pat, base, cm, allow_small_or_imprecise_dtypes=True), [], w)
 
-    def pick(out, in_, pat, cmp, base, cm, r, w):
-        op("g", lambda: g.affine_select(out, in_, pat, cmp, 0.0, base, cm), r, w)
+    def pick(out, in_, pat, cmp, base, cm, r, w, fill=0.0):
+        op("g", lambda: g.affine_select(out, in_, pat, cmp, fill, base, cm), r, w)
 
     dma("s", "dpos", T.posi[:], T.pos[:], [], ["posi"])
     dma("a", "dst", T.stw[:], T.st[:], [], ["stw"])
     dma("s", "dle", T.lei[0:8, 0:1], T.le[:], [], ["lei"])
     dma("s", "dve", T.vew[:], T.ve[:], [], ["vew"])
 
-    CB = ["cb0", "cb1", "cb2", "cb3"]
+    def slot_tables(t):
+        np_, ns, _ = SLOT[t]
+        u, k = t - 1, "%d" % t
+        sel, sk = T.sel[:, 16 * u:16 * u + WID[t]], ["sel" + k]
+        pat, neg, one = [[-ns, WID[t]]], [[ns, WID[t]]], [[0, 1]]
+        scale = 256 if t == 1 else 128
+        sL, sA, sR = [T.rows[:, 4 * u + i:4 * u + i + 1] for i in range(3)]
+        if t == 1:
+            sels = [lambda: pick(sel, T.oneb[:, 0:WID[t]], pat, A.is_ge, 0, 1, ["oneb"], sk),
+                    lambda: pick(sel, sel, neg, A.is_ge, ns - 1, -1, sk, sk)]
+        else:
+            top = T.sel[:, 16 * u + np_ - 1:16 * u + np_]
+            sels = [lambda: io(sel, [[0, WID[t]]], 0, sk, base=-1),
+                    lambda: pick(sel, sel, pat, A.is_ge, -ns, 1, sk, sk, fill=1.0),
+                    lambda: pick(sel, sel, pat, A.is_ge, 0, 1, sk, sk),
+                    lambda: pick(sel, sel, neg, A.is_ge, 2 * ns - 1, -1, sk, sk),
+                    lambda: pick(top, top, one, A.is_ge, -ns, 1, sk, sk, fill=1.0)]
+        rest = [lambda: io(T.rows[:, 4 * u:4 * u + 3], [[0, 3]], 0, ["sL" + k, "sA" + k, "sR" + k], base=scale),
+                lambda: pick(T.aa[0:ns, 128 * u:128 * u + np_ * ns], T.oneb[0:ns, 0:np_ * ns], [[0, np_], [-1, ns]],
+                             A.is_equal, 0, 1, ["oneb"], ["aa" + k]),
+                lambda: pick(sL, sL, one, A.is_ge, ns - 1, -1, ["sL" + k], ["sL" + k]),
+                lambda: pick(sR, sR, one, A.is_ge, -ns, 1, ["sR" + k], ["sR" + k]),
+                lambda: pick(T.ec[0:64, 128 * u:128 * u + 128], T.oneb[0:64, 0:128], [[0, 4], [1, 32]], A.is_equal,
+                             -(S0 + u), 0, ["oneb"], ["ec" + k]),
+                lambda: pick(sA, sL, one, A.is_ge, 2 * ns - 1, -1, ["sL" + k], ["sA" + k], fill=float(-scale)),
+                lambda: pick(sR, sR, one, A.is_ge, 2 * ns - 1, -1, ["sR" + k], ["sR" + k]),
+                lambda: pick(T.slb[:, u:u + 1], sL, one, A.is_ge, 0, 0, ["sL" + k], ["sB" + k])]
+        for i, call in enumerate(rest):
+            if i < len(sels):
+                sels[i]()
+            call()
+
+    def slot_masks(t):
+        np_, ns, _ = SLOT[t]
+        u, k = t - 1, "%d" % t
+        mm(T.e0[0:np_ * ns, 0:3 * ns], T.aa[0:ns, 128 * u:128 * u + np_ * ns], T.aa[0:ns, 128 * u:128 * u + 3 * ns],
+           True, True, ["aa" + k], ["e0"])
+        act(T.dm[0:np_ * ns, 48 * u:48 * u + 3 * ns], T.e0[0:np_ * ns, 0:3 * ns], 0.0, 1.0, ["e0"], ["dm" + k])
+        act(T.lc[0:64, 144 * u:144 * u + 128], T.ec[0:64, 128 * u:128 * u + 128], 0.0, T.rows[0:64, 4 * u + 1:4 * u + 2],
+            ["ec" + k, "sA" + k], ["lc" + k])
+        act(T.lc[0:64, 144 * u + 128:144 * u + 144], T.ec[0:64, 128 * u:128 * u + 16], 0.0, T.rows[0:64, 4 * u + 2:4 * u + 3],
+            ["ec" + k, "sR" + k], ["lr" + k])
+
     op("g", lambda: g.iota(T.pin[:, 0:1], [[0, 1]], 0, 1), [], ["pin0"])
     io(T.nid[:], [[1, W]], 0, ["nid"])
     io(T.onef[:], [[0, 128]], 0, ["onef"], base=1)
     pick(T.g8[0:8, :], T.onef[0:8, :], [[-1, 8], [0, 16]], A.is_equal, 0, 1, ["onef"], ["g8"])
-    io(T.n7[:], [[0, 16], [1, 8]], 0, ["n7"])
-    io(T.n3[:], [[1, 16], [0, 8]], 0, ["n3"])
-    io(T.n15[:], [[0, 8], [1, 16]], 0, ["n15"])
-    io(T.pc[:], [[0, 2 * W]], 0, ["pcl", "pcr"], base=200)
-    io(T.cb[:], [[0, 4 * PITCH + 8]], 0, CB, base=200)
-    io(T.low[:], [[0, 48]], 0, ["low"], base=LOW)
-    io(T.kb[:], [[0, 48]], 0, ["kb"], base=LOW)
+    io(T.n31[:], [[0, 4], [1, 32]], 0, ["n31"], base=AOFF)
     io(T.oneb[:], [[0, 144]], 0, ["oneb"], base=1)
-    io(T.n31[0:32, :], [[0, 4], [1, 32]], 0, ["n31"])
-    OH = ["oh%d" % x for x in range(13)]
+    io(T.hs[0:32, :], [[-16, 16]], -1, ["hs"], base=BASE - 256)
+    pick(T.repf[0:32, :], T.onef[0:32, :], [[0, 4], [-1, 32]], A.is_equal, 0, 1, ["onef"], ["repf"])
+    pick(T.hs[0:32, :], T.hs[0:32, :], [[-1, 16]], A.not_equal, 0, 1, ["hs"], ["hs"], fill=-1.0e9)
+    io(T.low[:], [[0, 48]], 0, ["low"], base=LOW)
+    io(T.n16[0:64, :], [[1, 16]], 0, ["n16"], base=-BOFF)
+    slot_tables(1)
+    OH = ["oh%d" % x for x in range(12)]
+    OI = ["oi%d" % x for x in range(12)]
     ms(T.oh[:], 0.0, OH)
     ms(T.xx[:, 0:8], 0.0, ["xpad0"])
     ms(T.xx[:, 2056:2072], 0.0, ["xpad1"])
     p0 = T.pin[:, 0:1]
     ts(T.pin[:, 1:2], p0, 15, None, A.bitwise_and, None, ["pin0"], ["pin1"])
-    ts(T.pin[:, 2:3], p0, 16, None, A.bitwise_and, None, ["pin0"], ["pin2"])
-    ts(T.pin[:, 3:4], p0, 3, None, A.arith_shift_right, None, ["pin0"], ["pin3"])
-    ts(T.pin[:, 4:5], p0, 7, None, A.bitwise_and, None, ["pin0"], ["pin4"])
-    ts(T.pin[:, 5:6], p0, 112, None, A.bitwise_and, None, ["pin0"], ["pin5"])
-    cp(T.pf[:, 0:6], T.pin[:, 0:6], ["pin%d" % i for i in range(6)], ["pf"])
-    fP, fR, fH, fP3, fP7, fG16 = [T.pf[:, i:i + 1] for i in range(6)]
+    ts(T.pin[:, 2:3], p0, 31, None, A.bitwise_and, None, ["pin0"], ["pin2"])
+    ts(T.pin[:, 3:4], p0, 112, None, A.bitwise_and, None, ["pin0"], ["pin3"])
+    ms(T.p1[:, 0:16], 0.0, ["p1"])
+    cp(T.pf[:, 0:4], T.pin[:, 0:4], ["pin%d" % i for i in range(4)], ["pf"])
+    fR, f31, fG16 = [T.pf[:, i:i + 1] for i in range(1, 4)]
+    ms(T.p2[:, 0:16], 0.0, ["p2"])
     ts(T.tm[:], T.nid[:, 0:16], fR, None, A.is_equal, None, ["nid", "pf"], ["tm"])
+    ts(T.big[:], T.nid[:, 0:144], -15.0, fG16, A.add, A.is_equal, ["nid", "pf"], ["big"])
+    ts(T.pf[:, 9:10], fR, 128.0, -8.0, A.mult, A.add, ["pf"], ["pf9"])
 
-    ts(T.tmpi[:, 0:128], T.posi[:], 9, None, A.arith_shift_right, None, ["posi"], ["tmp0"])
-    cp(T.hiu[:], T.tmpi[:, 0:128], ["tmp0"], ["hiu"])
-    ts(T.tmpi[:, 128:256], T.posi[:], 511, None, A.bitwise_and, None, ["posi"], ["tmp1"])
-    cuts = [0, 128] + list(range(384, 2048, 256)) + [2048]
+    ts(T.hiu[:], T.posi[:], -255.5, 1.0 / 512, A.add, A.mult, ["posi"], ["hiu"])
+    ts(T.tmpi[:], T.posi[:], 511, None, A.bitwise_and, None, ["posi"], ["tmp1"])
+    cuts = [0] + list(range(160, 2048, 256)) + [2048]
     NC = len(cuts) - 1
     for i in range(NC):
         a, b = cuts[i], cuts[i + 1]
         op("a", lambda: S.activation(T.mk[:, a:b], T.tm[:, 0:16].indirect(T.hiu[:, a // 16:b // 16]), AF.Copy),
            ["tm", "hiu"], ["mk%d" % i])
     act(T.fw[:, 0:2048], T.mk[:], 0.0, 0.0, ["mk%d" % i for i in range(NC)], ["fw"], fn=AF.Silu)
-    ts(T.big[:], T.nid[:, 0:144], -15.0, fG16, A.add, A.is_equal, ["nid", "pf"], ["big"])
-    cp(T.lou[:], T.tmpi[:, 128:256], ["tmp1"], ["lou"])
+    cp(T.lou[:], T.tmpi[:], ["tmp1"], ["lou"])
     done_r = 0
     for i in range(NC):
         a, b = cuts[i], cuts[i + 1]
@@ -195,18 +240,18 @@ def rank_program(g, core, T, topo):
            ["stw", "lou", "mk%d" % i], ["x%d" % i])
         if i == 0:
             cp(T.lef[0:8, 0:1], T.lei[0:8, 0:1], ["lei"], ["lef"])
-            ts(T.pf[:, 9:10], fR, 128.0, -8.0, A.mult, A.add, ["pf"], ["pf9"])
         if i == 1:
             ts(T.jj[:], T.nid[:], T.pf[:, 9:10], None, A.add, None, ["nid", "pf9"], ["jj"])
-        if i == NC - 2:
+        if i == 2:
             mm(T.pb[:, 0:1], T.g8[0:8, :], T.lef[0:8, 0:1], True, True, ["g8", "lef"], ["pb"])
         while done_r < 16 and (i == NC - 1 or 128 * done_r + 144 <= b):
             r = done_r
             mm(T.e0[:, 0:W], T.big[:, 15 - r:143 - r], T.xx[:, 128 * r:128 * r + W], r == 0, r == 15,
                ["big", "xpad0", "xpad1"] + ["x%d" % k for k in range(i + 1)], ["e0"])
             done_r += 1
-    ts(T.inv[:, 0:8], T.jj[:, 0:8], 0.0, 15.0, A.is_lt, A.mult, ["jj"], ["inv0"])
-    ts(T.jt[:], T.jj[:, 0:8], T.pb[:, 0:1], 15.0, A.is_ge, A.mult, ["jj", "pb"], ["jt"])
+        if i == NC - 2:
+            ts(T.inv[:, 0:8], T.jj[:, 0:8], 0.0, 15.0, A.is_lt, A.mult, ["jj"], ["inv0"])
+            ts(T.jt[:], T.jj[:, 0:8], T.pb[:, 0:1], 15.0, A.is_ge, A.mult, ["jj", "pb"], ["jt"])
     ts(T.inv[:, 8:W], T.jj[:, 8:W], T.pb[:, 0:1], 15.0, A.is_ge, A.mult, ["jj", "pb"], ["inv1"])
     tt(T.inv[:, 0:8], T.inv[:, 0:8], T.jt[:], A.max, ["jt", "inv0"], ["inv0"])
     tt(T.fo[:], T.e0[:, 0:W], T.inv[:], A.max, ["e0", "inv0", "inv1"], ["fo"])
@@ -252,84 +297,73 @@ def rank_program(g, core, T, topo):
                    ["idn", "pcr"], [bank])
             for q in range(4):
                 r = 4 * b + q
-                act(T.v0[:, r:2048:16], T[bank][:, 128 * q:128 * q + 128], 116.0, -1.0, [bank], ["v0_%d" % r])
+                act(T.v0[:, r:2048:16], T[bank][:, 128 * q:128 * q + 128], BASE + 16.0, -1.0, [bank], ["v0_%d" % r])
 
     FM, M1 = T.e1[:, 0:W], T.e1[:, 256:256 + W]
-    PCL, PCR = 0, W
-    sA, sB1, sB2, sLow = T.pf[:, 12:13], T.pf[:, 13:14], T.pf[:, 14:15], T.pf[:, 15:16]
+    AL = 128
+    T16, R0 = T.e3, T.e2
+    PCR = W
     off = 0
     for t in range(R):
         NS = S0 + t
         last = t == R - 1
         wd = WID[t]
+        pay = T.pay[:, 16 * t:16 * t + wd]
         if t == 0:
-            n8, nm, nsel, sel, sk = 8 * NS, 8 * NS, 16, T.sel, "sel"
+            nm = 128
             for x in range(NS):
-                ts(T.oh[:, PITCH * x:PITCH * x + 129], T.fo[:, 7:136], float(x), None, A.is_equal, None,
-                   ["fo"], ["oh%d" % x])
-            span = 17 * (n8 - 1) + 1
-            for k in range(17):
-                mm(T.p1[0:n8, 0:n8], T.oh[:, k:k + span:17], T.oh[:, k + 1:k + 1 + span:17], k == 0, k == 16, OH, ["p1"])
+                ts(T.oh[:, PA * x:PA * x + 129], T.fo[:, 7:136], float(x), None, A.is_equal, None, ["fo"], ["oh%d" % x])
+            span = PA * (NS - 1) + 1
+            for j in range(128):
+                q = j - j % 32
+                mm(T.p1[q:q + NS, 0:NS], T.oh[:, j + 1:j + 1 + span:PA], T.oh[:, j:j + span:PA], j == q, j == q + 31,
+                   OH, ["p1"])
+            ts(T16[:, 0:W], T.fo[:], -16.0, float(BASE), A.mult, A.add, ["fo"], ["e3"])
+            ts(T.pb[:, AL:AL + W], T.inv[:], 0.0, None, A.is_equal, None, ["inv0", "inv1"], ["pb"])
             cp(T.pou[:], T.posi[:], ["posi"], ["pou"])
-            ts(T.dm[:], T.n7[:], fP7, None, A.is_equal, None, ["n7", "pf"], ["dm"])
-            ts(T.dm2[:], T.n3[:], fP3, None, A.not_equal, None, ["n3", "pf"], ["dm2"])
-            ts(T.sel[:], T.nid[:, 0:16], fP3, None, A.is_equal, None, ["nid", "pf"], ["sel"])
-            ms(T.p2[:, 0:16], 0.0, ["p2"])
-            tt(T.dm2[:], T.dm[:], T.dm2[:], A.mult, ["dm", "dm2"], ["dm2"])
-            ts(T.pf[:, 7:8], fP3, 156.0, -1.0 / 2048, A.add, A.mult, ["pf"], ["pf7"])
-            ts(T.rep[:], T.n15[:], fP3, 256.0, A.is_equal, A.mult, ["n15", "pf"], ["rep"])
-            ts(T.cst[:], T.nid[:, 0:16], -16.0 / 2048, T.pf[:, 7:8], A.mult, A.add, ["nid", "pf7"], ["cst"])
-            ts(T.t16[:], T.fo[:], -16.0, 100.0, A.mult, A.add, ["fo"], ["t16"])
-            vectors(range(0, 10))
-            mask, mk_ = T.dm2, "dm2"
+            ms(T.pc[:, 0:2 * W:2 * W - 1], 0.0, ["pcl", "pcr"])
+            ms(T.cb[:], 0.0, ["cb0", "cb1", "cb2"])
+            ts(T.pf[:, 10:11], f31, float(AOFF), None, A.add, None, ["pf"], ["pf10"])
+            cp(pay, T.p1[:, 0:wd], ["p1"], ["pay0"])
+            ts(T.rep[:], T.n31[:], T.pf[:, 10:11], 256.0, A.is_equal, A.mult, ["n31", "pf10"], ["rep"])
+            slot_masks(1)
+            vectors(range(0, 11))
         else:
-            nm = 32
-            if t == 1:
-                n8, nsel, sel, sk = 8 * (NS - 1), 16, T.sel, "sel"
-            else:
-                n8, nsel, sel, sk = 8 * NS, NS - 1, T.sel2, "sel2"
+            np_, ns, nc = SLOT[t]
+            n8, nm = np_ * ns, 3 * ns
             u = t - 1
-            K, RK, KR = T.kk[:, u:u + 1], T.rr[:, u:u + 1], ["kk%d" % u, "rr%d" % u]
-            ts(T.eb[:], T.cb[:], RK, K, A.add, A.is_equal, CB + KR, ["eb"])
-            for k in range(17):
-                mm(T.p1[0:n8, 0:32], T.oh[:, k + 1:k + 2 + 17 * (n8 - 1):17], T.eb[:, k + 1:k + 2 + 17 * 31:17],
-                   k == 0, k == 16, OH + ["eb"], ["p1"])
+            K, RK, KR = T.kk[:, 36 * u + 31:36 * u + 32], T.kk[:, 36 * u + 33:36 * u + 34], ["kk%d" % u]
+            cb, oh, pitch, OHK = (T.cc, T.oi, PB, OI) if last else (T.cb, T.oh, PA, OH)
+            ts(T.eb[:, 0:3 * pitch], cb[:, 1:1 + 3 * pitch], RK, K, A.add, A.is_equal, ["cb0", "cb1", "cb2"] + KR, ["eb"])
+            for k in range(nc):
+                mm(T.p1[0:n8, 0:nm], oh[:, k + 1:k + 2 + nc * (n8 - 1):nc], T.eb[:, k:k + 1 + nc * (nm - 1):nc],
+                   k == 0, k == nc - 1, OHK + ["eb"], ["p1"])
             ts(T.ne[:], T.pc[:], RK, K, A.add, A.not_equal, ["pcl", "pcr"] + KR, ["ne"])
             tt(M1, FM, T.ne[:, 0:W], A.mult, ["e1", "ne"], ["e1"])
+            tt(T.pb[:, AL:AL + W], T.pb[:, AL:AL + W], T.ne[:, 0:W], A.mult, ["pb", "ne"], ["pb"])
+            tt(T.mm[0:n8, 0:nm], T.p1[0:n8, 0:nm], T.dm[0:n8, 48 * u:48 * u + nm], A.mult, ["p1", "dm%d" % t], ["mm"])
+            mm(T.p2[0:nm, 0:wd], T.mm[0:n8, 0:nm], T.sel[0:n8, 16 * u:16 * u + wd], True, True, ["mm", "sel%d" % t], ["p2"])
             tt(T.fo[:], M1, T.ne[:, W:2 * W], A.mult, ["e1", "ne"], ["fo"])
-            if t == 1:
-                cp(T.alv[:], T.ne[:, 0:W], ["ne"], ["alv"])
-            else:
-                tt(T.alv[:], T.alv[:], T.ne[:, 0:W], A.mult, ["alv", "ne"], ["alv"])
+            cp(pay, T.p2[:, 0:wd], ["p2"], ["pay%d" % t])
             off = NS - 1
-            act(T.mt4[:, u:u + 1], RK, K, -1.0, KR, ["kr%d" % u])
-            act(T.mt4[:, 6:7], RK, 256.0, 1.0, KR, ["r256"])
-            act(T.mt4[:, 4:5], T.mt4[:, u:u + 1], 92.5 / 16, -1.0 / 16, ["kr%d" % u], ["ma"])
-            act(T.lc[0:32, 0:128], T.ec[0:32, 128 * u:128 * u + 128], 0.0, T.pf[0:32, 12:13], ["ec", "sA"], ["lc0"])
-            act(T.lc[0:32, 128:144], T.ec[0:32, 128 * u:128 * u + 16], 0.0, T.pf[0:32, 13:14], ["ec", "sB1"], ["lc1"])
-            act(T.ded[:], T.alv[:], 1.0, -1.0, ["alv"], ["ded"])
-            ts(T.t16[:], T.fo[:], -16.0, 100.0 - 17 * off, A.mult, A.add, ["fo"], ["t16"])
+            act(T.nk[:, u:u + 1], K, RK, -1.0, KR, ["nk%d" % u])
+            act(T.mt4[:, 0:1], RK, 256.0, 1.0, KR, ["r256"])
+            act(T.wa[:, u:u + 1], T.nk[:, u:u + 1], (BASE - 7.5) / 16 + AOFF, 1.0 / 16, ["nk%d" % u], ["a%d" % u])
+            act(T.wb[:, u:u + 1], T.wa[:, u:u + 1], T.nk[:, u:u + 1], -16.0, ["nk%d" % u, "a%d" % u], ["b%d" % u])
             if last:
-                act(T.pcd[:], T.alv[:, 8:136], 200.0, -200.0, ["alv"], ["pcd"])
+                tt(T.alx[:], T.pb[:, AL:AL + W], T.fst[:], A.add, ["pb", "fst"], ["alx"])
+                act(T16[:, 0:W], T.fo[:], float(BASE - 17 * off), -16.0, ["fo"], ["e3"])
+                act(T.ded[:], T.alx[:], 1.0, -1.0, ["alx"], ["ded"])
             else:
-                act(T.w4[:], T.alv[:], 400.0, -400.0, ["alv"], ["w4"])
+                act(T.ded[:], T.pb[:, AL:AL + W], 1.0, -1.0, ["pb"], ["ded"])
+                act(T16[:, 0:W], T.fo[:], float(BASE - 17 * off), -16.0, ["fo"], ["e3"])
                 act(FM, T.fo[:], float(off - NS), 1.0, ["fo"], ["e1"])
-                for x in range(0 if t == 1 else 1, NS + 1):
-                    act(T.oh[:, PITCH * x:PITCH * x + 129], T.fo[:, 7:136], off - x + 0.5, 1.0, ["fo"], ["oh%d" % x],
+                noh, npitch, nk_ = (T.oi, PB, "oi%d") if t == R - 2 else (T.oh, PA, "oh%d")
+                for x in range(0 if t == 1 else 1, SLOT[t + 1][0]):
+                    act(noh[:, npitch * x + 1:npitch * x + 129], T.fo[:, 8:136], off - x + 0.5, 1.0, ["fo"], [nk_ % x],
                         fn=AF.Sign)
-                vectors(range(7 + 3 * t, 10 + 3 * t))
-            mask, mk_ = T.dm, "dm"
 
-        tt(T.mm[0:n8, 0:nm], T.p1[0:n8, 0:nm], mask[0:n8, 0:nm], A.mult, ["p1", mk_], ["mm"])
-        mm(T.p2[0:nm, 0:nsel], T.mm[0:n8, 0:nm], sel[0:n8, 0:nsel], True, True, ["mm", sk], ["p2"])
-        if t > 0:
-            ts(T.mgs[:, 3 * u:3 * u + 1], T.mt4[:, 4:5], M23, M23, A.add, A.subtract, ["ma"], ["a%d" % u])
-        pay = T.pay[:, 16 * t:16 * t + wd]
-        cp(pay, T.p2[:, 0:wd], ["p2"], ["pay%d" % t])
         slot = T.land[:, 16 * (NR * t + rank):16 * (NR * t + rank) + wd]
-        if t > 0:
-            tt(T.cd[:, 1:W], T.t16[:, 0:W - 1], T.fo[:, 1:W], A.subtract, ["t16", "fo"], ["cd"])
-            tt(T.d1[:, 1:W], T.cd[:, 1:W], T.alv[:, 1:W], A.mult, ["cd", "alv"], ["d1"])
         order("g", ["pay%d" % t], [])
         sem = T.sem["ar%d_%d" % (t, rank)]
         g.remote_dma_fused([
@@ -341,77 +375,76 @@ def rank_program(g, core, T, topo):
         count["sent"] += len(far_eng) + len(near_eng)
 
         if t == 0:
-            for k in range(R - 1):
-                pick(T.ec[0:32, 128 * k:128 * k + 128], T.oneb[0:32, 0:128], [[0, 4], [1, 32]], A.is_equal, -(S0 + k), 0,
-                     ["oneb"], ["ec"])
-            pick(T.idf[:], T.onef[:], [[-1, 128]], A.is_equal, 0, 1, ["onef"], ["idf"])
-            ms(T.p3[:, 16:48], -1.0e9, ["p3"])
-            tt(T.pc[:, 1:W], T.t16[:, 0:W - 1], T.fo[:, 1:W], A.subtract, ["t16", "fo"], ["pcl"])
-            tt(T.pc[:, W:2 * W - 1], T.t16[:, 0:W - 1], T.fo[:, 1:W], A.subtract, ["t16", "fo"], ["pcr"])
+            slot_tables(2)
+            tt(T.pc[:, 1:W], T16[:, 0:W - 1], T.fo[:, 1:W], A.subtract, ["e3", "fo"], ["pcl"])
+            tt(T.pc[:, W:2 * W - 1], T16[:, 0:W - 1], T.fo[:, 1:W], A.subtract, ["e3", "fo"], ["pcr"])
             ts(FM, T.fo[:], float(-NS), None, A.add, None, ["fo"], ["e1"])
-            cp(T.cb[:, PITCH + 1:PITCH + 129], T.pc[:, PCL + 7:PCL + 135], ["pcl"], ["cb1"])
-            cp(T.cb[:, 0:129], T.pc[:, PCR + 8:PCR + 137], ["pcr"], ["cb0"])
+            ms(T.p3[:, 16:48], -1.0e9, ["p3"])
+            ms(T.tr[:, 32:34], -1.0e9, ["trpad"])
+            ms(T.rnd[:, 0:32], 0.0, ["rnd0"])
+            ms(T.rnd[:, 32:33], M31, ["rnd1"])
+            ms(T.rnd[:, 33:34], -M31, ["rnd2"])
         else:
             if t == 1:
+                slot_tables(3)
                 pick(T.idn[:], T.oneb[:], [[-1, 144]], A.is_equal, 0, 1, ["oneb"], ["idn"])
-                pick(T.tri[:], T.onef[:], [[1, 128]], A.is_gt, 0, -1, ["onef"], ["tri"])
             if t == 2:
+                pick(T.tri[:], T.onef[:], [[1, 128]], A.is_gt, 0, -1, ["onef"], ["tri"])
                 io(T.neg[:], [[0, 128]], 0, ["neg"], base=-1)
                 io(T.ee[:, 128:136], [[0, 8]], 0, ["eepad"])
-            if last:
                 pick(T.tri[:], T.tri[:], [[-16, 8], [0, 16]], A.is_ge, 0, 1, ["tri"], ["tri"])
+            if last:
                 pick(T.gsel[:], T.onef[:, 0:8], [[-16, 8]], A.is_ge, 0, 1, ["onef"], ["gsel"])
                 pick(T.gsel[:], T.gsel[:], [[16, 8]], A.is_ge, 15, -1, ["gsel"], ["gsel"])
+            ts(T.ht[0:32, :], T.p3[0:32, 0:16], T.kk[0:32, 36 * u + 31:36 * u + 32], T.mt4[0:32, 0:1], A.is_equal, A.mult,
+               ["p3", "r256"] + KR, ["ht"])
+            tt(T.cd[:, 1:W], T16[:, 0:W - 1], T.fo[:, 1:W], A.subtract, ["e3", "fo"], ["cd"])
+            tt(T.hs[0:32, :], T.p3[0:32, 0:16], T.ht[0:32, :], A.subtract, ["p3", "ht"], ["hs"])
+            if last:
+                tt(T.d1[:, 1:W], T.alx[:, 1:W], T.cd[:, 1:W], A.mult, ["cd", "alx"], ["d1"])
+            else:
+                tt(T.d1[:, 1:W], T.pb[:, AL + 1:AL + W], T.cd[:, 1:W], A.mult, ["cd", "pb"], ["d1"])
+            ts(T.ld[0:nm, 0:128], T.n31[0:nm, :], T.wa[0:nm, u:u + 1], T.slb[0:nm, u:u + 1], A.is_equal, A.mult,
+               ["n31", "sB%d" % t, "a%d" % u], ["ld0"])
             scan(T.pc[:, 2 * W - 2:W - 1:-1], T.ded[:, W - 1:0:-1], T.d1[:, W - 1:0:-1], 0.0, A.mult, A.add,
                  ["ded", "d1"], ["pcr"])
             if last:
                 codes_out([0, 2, 3, 1])
-            if not last:
+            else:
                 scan(T.pc[:, 1:W], T.ded[:, 1:W], T.d1[:, 1:W], 0.0, A.mult, A.add, ["ded", "d1"], ["pcl"])
-            ts(T.mt4[:, 5:6], T.mgs[:, 3 * u:3 * u + 1], -16.0, 100.0, A.mult, A.add, ["a%d" % u], ["mb"])
-            ts(T.ld[0:32, 0:128], T.n31[0:32, :], T.mgs[0:32, 3 * u:3 * u + 1], T.pf[0:32, 12:13], A.is_equal, A.mult,
-               ["n31", "sA", "a%d" % u], ["ld0"])
-            tt(T.mgs[:, 3 * u + 1:3 * u + 2], T.mt4[:, 5:6], T.mt4[:, u:u + 1], A.subtract, ["mb", "kr%d" % u], ["b%d" % u])
-            if t == 1:
-                ts(T.kb[:, 0:16], T.p3[:, 0:16], sLow, None, A.add, None, ["p3", "sLow"], ["kb"])
-            if not last:
-                tt(T.cb[:, 0:129], T.pc[:, PCR + 8:PCR + 137], T.w4[:, 8:137], A.add, ["pcr", "w4"], ["cb0"])
-            ts(T.ld[0:32, 128:144], T.n31[0:32, 0:16], T.mgs[0:32, 3 * u + 1:3 * u + 2], T.pf[0:32, 14:15], A.is_equal, A.mult,
-               ["n31", "sB2", "b%d" % u], ["ld1"])
-            keys, kn = (T.kb[:, 0:16], "kb") if t == 1 else (T.p3[:, 0:16], "p3")
-            ts(T.ht[:], keys, K, T.mt4[:, 6:7], A.is_equal, A.mult, [kn, "r256"] + KR, ["ht"])
-            tt(T.lab[0:32, 0:144], T.lc[0:32, 0:144], T.ld[0:32, 0:144], A.subtract, ["lc0", "ld0", "lc1", "ld1"], ["lab"])
-            tt(T.hs[:], keys, T.ht[:], A.subtract, [kn, "ht"], ["hs"])
-            if not last:
-                tt(T.cb[:, PITCH + 1:PITCH + 129], T.pc[:, PCL + 7:PCL + 135], T.w4[:, 8:136], A.add, ["pcl", "w4"], ["cb1"])
+            ts(T.ld[0:nm, 128:144], T.n16[0:nm, :], T.wb[0:nm, u:u + 1], T.rows[0:nm, 4 * u + 2:4 * u + 3], A.is_equal, A.mult,
+               ["n16", "sR%d" % t, "b%d" % u], ["ld1"])
+        if t == R - 2:
+            ms(T.cc[:], 0.0, ["cb0", "cb1", "cb2"])
         if not last:
-            tt(T.nq[:, 7:136], T.pc[:, PCL + 7:PCL + 136], T.cb[:, 0:129], A.not_equal, ["pcl", "cb0"], ["nq"])
-            ts(T.nq[:, 7:136], T.nq[:, 7:136], 400.0, None, A.mult, None, ["nq"], ["nq"])
-            tt(T.cb[:, 2 * PITCH + 1:2 * PITCH + 129], T.nq[:, 8:136], T.pc[:, PCL + 8:PCL + 136], A.add, ["nq", "pcl"], ["cb2"])
-            tt(T.cb[:, 3 * PITCH + 1:3 * PITCH + 129], T.nq[:, 7:135], T.pc[:, PCL + 7:PCL + 135], A.add, ["nq", "pcl"], ["cb3"])
+            cb, pitch = (T.cc, PB) if t == R - 2 else (T.cb, PA)
+            tt(cb[:, 0:129], T.pb[:, AL + 8:AL + 137], T.pc[:, PCR + 8:PCR + 137], A.mult, ["pb", "pcr"], ["cb0"])
+            tt(R0[:, 0:129], T.pb[:, AL + 8:AL + 137], T.pc[:, 7:136], A.mult, ["pb", "pcl"], ["e2"])
+        if t > 0:
+            tt(T.lab[0:nm, :], T.lc[0:nm, 144 * u:144 * u + 144], T.ld[0:nm, :], A.subtract,
+               ["lc%d" % t, "lr%d" % t, "ld0", "ld1"], ["lab"])
+        if not last:
+            tt(T.nq[:, 0:129], R0[:, 0:129], cb[:, 0:129], A.not_equal, ["e2", "cb0"], ["nq"])
+            tt(cb[:, pitch + 1:pitch + 130], R0[:, 0:129], T.nq[:, 0:129], A.mult, ["e2", "nq"], ["cb1"])
+            tt(cb[:, 2 * pitch + 1:2 * pitch + 129], R0[:, 1:129], cb[:, pitch + 2:pitch + 130], A.subtract, ["e2", "cb1"], ["cb2"])
         if t == 0:
-            ts(T.pf[:, 10:11], fP3, 0.0, 256.0, A.is_equal, A.mult, ["pf"], ["s0"])
-            ts(T.pf[:, 11:12], fP3, 2.0, 256.0, A.is_equal, A.mult, ["pf"], ["s2"])
-            ts(sB2, fP3, 1.0, 256.0, A.is_equal, A.mult, ["pf"], ["sB2"])
-            ts(T.pf[:, 16:17], fP3, 3.0, 256.0, A.is_equal, A.mult, ["pf"], ["s3"])
-            ts(sLow, fH, -1.0e8, None, A.mult, None, ["pf"], ["sLow"])
-            tt(sA, T.pf[:, 10:11], T.pf[:, 11:12], A.subtract, ["s0", "s2"], ["sA"])
-            tt(sB1, sB2, T.pf[:, 16:17], A.subtract, ["sB2", "s3"], ["sB1"])
-            ts(T.sa[:, 0:16], T.nid[:, 0:16], fP3, 0.5, A.is_equal, A.mult, ["nid", "pf"], ["sa0"])
-            ts(T.sa[:, 16:32], T.nid[:, 1:17], fP3, 0.5, A.is_equal, A.mult, ["nid", "pf"], ["sa1"])
-            ts(T.val[:], T.jj[:, 8:136], T.pb[:, 0:1], None, A.is_lt, None, ["jj", "pb"], ["val"])
-            tt(T.sel2[:], T.sa[:, 0:16], T.sa[:, 16:32], A.subtract, ["sa0", "sa1"], ["sel2"])
+            ts(T.fst[:], T.jj[:], T.pb[:, 0:1], None, A.is_equal, None, ["jj", "pb"], ["fst"])
+            ms(T.oi[:], 0.0, OI)
+            io(T.oi[:, 1:129], [[0, 128]], 0, ["oi0"], base=1)
         if t == 1:
             io(T.yw[:, 0:1024], [[0, 1024]], 0, ["yw"])
+            slot_masks(2)
+            vectors(range(11, 13))
             act(T.tt[:], T.jj[:, 8:136], 4096.0, -1.0, ["jj"], ["tt"])
             act(T.pf[:, 8:9], T.jj[:, 135:136], 4095.0, -1.0, ["jj"], ["pf8"])
         if t == 2:
+            slot_masks(3)
+            vectors(range(13, 16))
             io(T.yw[:, 1024:2048], [[0, 1024]], 0, ["yw2"])
         if last:
-            tt(T.av[:], T.alv[:, 8:136], T.val[:], A.mult, ["alv", "val"], ["av"])
-            tt(T.pcd[:], T.pcd[:], T.d1[:, 8:136], A.add, ["pcd", "d1"], ["pcd"])
-            scan(T.ss[:, 0:128], T.av[:], T.neg[:], T.tt[:, 0:1], A.add, A.add, ["av", "neg", "tt"], ["ss"])
-            tt(T.p2[:, 128:256], T.av[:], T.tt[:], A.mult, ["av", "tt"], ["p2"])
+            av = T.pb[:, AL + 8:AL + 136]
+            scan(T.ss[:, 0:128], av, T.neg[:], T.tt[:, 0:1], A.add, A.add, ["pb", "neg", "tt"], ["ss"])
+            tt(T.p2[:, 128:256], av, T.tt[:], A.mult, ["pb", "tt"], ["p2"])
             tt(T.zz[:], T.ss[:, 0:128], T.p2[:, 128:256], A.subtract, ["ss", "p2"], ["zz"])
             ts(T.nd[:, 128:129], T.p2[:, 255:256], -1.0, T.pf[:, 8:9], A.mult, A.add, ["p2", "pf8"], ["nd2"])
             tt(T.nd[:, 1:128], T.zz[:, 0:127], T.zz[:, 1:128], A.subtract, ["zz"], ["nd1"])
@@ -421,28 +454,25 @@ def rank_program(g, core, T, topo):
         for c, n in senders:
             s = T.rank_of(c)
             srcs.append((T.land[0:nm, 16 * (NR * t + s):16 * (NR * t + s) + wd], ("ar%d_%d" % (t, s), n)))
-        if t == 0:
-            mm(T.p3[:, 0:16], T.rep[:], T.cst[:], True, False, ["rep", "cst"], ["p3"])
-        else:
-            mm(T.p3[:, 0:16], T.idf[:], T.hs[:], True, False, ["idf", "hs"], ["p3"])
+        mm(T.p3[:, 0:16], T.repf[0:32, :], T.hs[0:32, :], True, False, ["repf", "hs"], ["p3"])
         for i, (src, tok) in enumerate(srcs):
             end = i == len(srcs) - 1
             if tok:
                 need("p", [tok])
             if t == 0:
-                mm(T.p3[:, 0:wd], T.rep[0:nm, :], src, False, end, ["pay0"], ["p3"])
+                mm(T.p3[:, 0:wd], T.rep[:], src, False, end, ["pay0", "rep"], ["p3"])
             else:
                 for q in range(0, 128, 32):
-                    mm(T.p3[q:q + wd, 0:16], src, T.lab[0:32, 128:144], False, False, ["lab", "pay%d" % t], ["p3"])
-                mm(T.p3[:, 0:wd], T.lab[0:32, 0:128], src, False, end, ["lab"], ["p3"])
-        K, RK = T.kk[:, t:t + 1], T.rr[:, t:t + 1]
+                    mm(T.p3[q:q + wd, 0:16], src, T.lab[0:nm, 128:144], False, False, ["lab", "pay%d" % t], ["p3"])
+                mm(T.p3[:, 0:wd], T.lab[0:nm, 0:128], src, False, end, ["lab"], ["p3"])
         scan(T.sc[:], T.p3[:, 0:48], T.low[:], -1.0e9, A.max, A.max, ["p3", "low"], ["sc"])
-        op("v", lambda: V.transpose(T.tr[:], T.sc[:, 16:48]), ["sc"], ["tr"])
-        op("v", lambda: V.tensor_reduce(K, T.tr[:], AX.X, A.max), ["tr"], ["kk%d" % t])
-        ts(RK, K, M31, M31, A.add, A.subtract, ["kk%d" % t], ["rr%d" % t])
+        op("v", lambda: V.transpose(T.tr[:, 0:32], T.sc[:, 16:48]), ["sc"], ["tr"])
+        scan(T.kk[:, 36 * t:36 * t + 34], T.tr[:, 0:34], T.rnd[:, 0:34], -1.0e9, A.max, A.add,
+             ["tr", "trpad", "rnd0", "rnd1", "rnd2"], ["kk%d" % t])
 
-    K, RK = T.kk[:, 3:4], T.rr[:, 3:4]
-    ts(T.ee[:, 0:128], T.pcd[:], RK, K, A.add, A.is_equal, ["pcd", "kk3", "rr3"], ["ee"])
+    u = R - 1
+    K, RK = T.kk[:, 36 * u + 31:36 * u + 32], T.kk[:, 36 * u + 33:36 * u + 34]
+    ts(T.ee[:, 0:128], T.d1[:, 8:136], RK, K, A.add, A.is_equal, ["d1", "kk3"], ["ee"])
     scan(T.ss[:, 0:129], T.ee[:, 0:129], T.nd[:, 0:129], 0.0, A.add, A.add, ["ee", "eepad", "nd0", "nd1", "nd2"], ["ss"])
     mm(T.pb[:, 1:2], T.tri[:], T.ss[:, 128:129], True, True, ["tri", "ss"], ["pb"])
     ts(T.p2[:, 128:256], T.ee[:, 0:128], 4096.0, None, A.mult, None, ["ee"], ["p2"])
@@ -454,23 +484,23 @@ def rank_program(g, core, T, topo):
     dma("s", "dft", T.ft[:], T.fw[0:128:16, 0:2048], ["fw"], ["ft"])
     dma("a", "dout2", T.y[:], T.yw[:, 0:2048], ["yw", "fw"], [])
 
-    KR = ["kk%d" % t for t in range(R)] + ["rr%d" % t for t in range(R)]
+    KR = ["kk%d" % t for t in range(R)]
     mm(T.pb[0:8, 2:3], T.gsel[:], T.ss[:, 128:129], True, True, ["gsel", "ss"], ["pb"])
-    tt(T.mt4[:, 3:4], K, RK, A.subtract, KR, ["kr3"])
-    ts(T.mgs[0:1, 2:12:3], T.rr[0:1, :], 1.0 / 256, 1.0, A.mult, A.add, KR, ["mg2"])
-    ts(T.mt4[:, 4:5], T.mt4[:, 3:4], -1.0 / 16, 92.5 / 16, A.mult, A.add, ["kr3"], ["ma"])
-    ts(T.mt4[:, 12:13], T.mt4[:, 3:4], -1.0, 116.0, A.mult, A.add, ["kr3"], ["c3"])
-    ts(T.mgs[:, 9:10], T.mt4[:, 4:5], M23, M23, A.add, A.subtract, ["ma"], ["a3"])
+    tt(T.nk[:, u:u + 1], RK, K, A.subtract, KR, ["nk3"])
+    ts(T.mgs[0:1, 2:12:3], T.kk[0:1, 33:36 * R:36], 1.0 / 256, 1.0, A.mult, A.add, KR, ["mg2"])
+    ts(T.wa[:, u:u + 1], T.nk[:, u:u + 1], 1.0 / 16, (BASE - 7.5) / 16 + AOFF, A.mult, A.add, ["nk3"], ["a3"])
+    ts(T.mt4[:, 2:3], T.nk[:, u:u + 1], BASE + 16.0, None, A.add, None, ["nk3"], ["c3"])
     ts(T.fls[0:8, 0:1], T.pb[0:8, 2:3], -1.0, None, A.mult, None, ["pb"], ["fls"])
-    ts(T.mt4[:, 5:6], T.mgs[:, 9:10], -16.0, 100.0, A.mult, A.add, ["a3"], ["mb"])
-    ts(T.mt4[:, 13:14], T.mgs[:, 9:10], -1.0, float(S0 + R - 1), A.mult, A.add, ["a3"], ["c4"])
-    tt(T.mgs[:, 10:11], T.mt4[:, 5:6], T.mt4[:, 3:4], A.subtract, ["mb", "kr3"], ["b3"])
+    ts(T.wb[:, u:u + 1], T.wa[:, u:u + 1], -16.0, T.nk[:, u:u + 1], A.mult, A.add, ["a3", "nk3"], ["b3"])
+    ts(T.mt4[:, 3:4], T.wa[:, u:u + 1], -1.0, float(AOFF + S0 + R - 1), A.mult, A.add, ["a3"], ["c4"])
+    ts(T.mgs[0:1, 0:12:3], T.wa[0:1, 0:4], float(-AOFF), None, A.add, None, ["a%d" % t for t in range(R)], ["mg0"])
+    ts(T.mgs[0:1, 1:12:3], T.wb[0:1, 0:4], float(BOFF), None, A.add, None, ["b%d" % t for t in range(R)], ["mg1"])
 
     act(T.fa[:], T.ft[:], -23.5 / 16, 1.0 / 16, ["ft"], ["fa"])
     dma("a", "dout2", T.fl[:], T.fls[0:8, 0:1], ["fls"], [])
-    dma("a", "dout2", T.mg[:], T.mgs[0:1, 0:12], ["mg2"] + ["a%d" % t for t in range(R)] + ["b%d" % t for t in range(R)], [])
+    dma("a", "dout2", T.mg[:], T.mgs[0:1, 0:12], ["mg0", "mg1", "mg2"], [])
     ts(T.fb[:], T.ft[:], M23, M23, A.add, A.subtract, ["ft"], ["fb"])
-    ts(T.p2[:, 256:384], T.fb[:], T.mt4[:, 12:13], T.mt4[:, 13:14], A.is_equal, A.mult, ["fb", "c3", "c4"], ["p2"])
+    ts(T.p2[:, 256:384], T.fb[:], T.mt4[:, 2:3], T.mt4[:, 3:4], A.is_equal, A.mult, ["fb", "c3", "c4"], ["p2"])
     ts(T.fa[:], T.fa[:], M23, M23, A.add, A.subtract, ["fa"], ["fa"])
     tt(T.fc[:], T.p2[:, 256:384], T.fa[:], A.add, ["fa", "p2"], ["fc"])
     dma("s", "dout", T.fs[:], T.fc[:], ["fc"], [])

@@ -1,16 +1,18 @@
 from concourse.bass import DstId, RemoteDMATransfer
 from concourse.mybir import AluOpType as A, ActivationFunctionType as AF
 
-W = 152
+W = 144
 R = 4
 S0 = 10
 NR = 8
 WIN = 6144
 LOW = -16000000
 BASE = 102
-WID = (10, 10, 12, 12)
-SLOT = {1: (10, 12, 11), 2: (11, 11, 12), 3: (12, 10, 13)}
-PA, PB = 132, 130
+C0 = 2
+WID = (10 * C0, 10, 11, 12)
+P1 = 130
+SLOT = {1: (9, 13, 10), 2: (10, 12, 11), 3: (11, 11, 12)}
+PITCH = 136
 M31 = 1.5 * 2.0 ** 31
 M23 = 1.5 * 2.0 ** 23
 AOFF = 192
@@ -22,24 +24,24 @@ SCRATCH = {
     "vew": ("sbuf", [128, 8192], bf), "tmpi": ("sbuf", [128, 128], i32),
     "hiu": ("sbuf", [128, 128], u16), "lou": ("sbuf", [128, 128], u16), "pou": ("sbuf", [128, 128], u16),
     "offu": ("sbuf", [128, 128], u16),
-    "pin": ("sbuf", [128, 8], i32), "pf": ("sbuf", [128, 24], f32), "lef": ("sbuf", [128, 4], f32),
-    "nid": ("sbuf", [128, W], f32), "n31": ("sbuf", [128, 128], bf), "n16": ("sbuf", [128, 16], f32),
+    "pin": ("sbuf", [128, 16], i32), "pf": ("sbuf", [128, 24], f32), "lef": ("sbuf", [128, 4], f32),
+    "nid": ("sbuf", [128, W], f32), "n31": ("sbuf", [128, 128], bf), "n16": ("sbuf", [128, 32], f32),
     "tm": ("sbuf", [128, 16], bf), "big": ("sbuf", [128, 144], bf), "idn": ("sbuf", [128, 144], bf),
     "sel": ("sbuf", [128, 48], bf), "rows": ("sbuf", [128, 12], f32), "slb": ("sbuf", [128, 4], bf), "aa": ("sbuf", [128, 384], bf),
-    "rep": ("sbuf", [128, 128], f16), "repf": ("sbuf", [128, 128], f32),
+    "rep": ("sbuf", [128, 384], bf), "tri3": ("sbuf", [128, 384], bf), "repb": ("sbuf", [128, 128], bf), "repf": ("sbuf", [128, 128], f32),
     "dm": ("sbuf", [128, 144], bf), "g8": ("sbuf", [128, 128], f32),
     "onef": ("sbuf", [128, 128], f32), "oneb": ("sbuf", [128, 144], bf), "ec": ("sbuf", [128, 384], bf),
     "tri": ("sbuf", [128, 128], f32), "gsel": ("sbuf", [128, 8], f32),
     "hs": ("sbuf", [128, 16], f32), "ht": ("sbuf", [128, 16], f32),
-    "lab": ("sbuf", [128, 144], f16), "lc": ("sbuf", [128, 432], bf), "ld": ("sbuf", [128, 144], bf),
-    "cb": ("sbuf", [128, 3 * PA + 8], bf), "cc": ("sbuf", [128, 3 * PB + 8], bf), "eb": ("sbuf", [128, 3 * PA], bf),
-    "nq": ("sbuf", [128, 136], bf), "fst": ("sbuf", [128, W], bf), "alx": ("sbuf", [128, W], bf),
+    "lab": ("sbuf", [128, 32], bf), "lc": ("sbuf", [128, 96], bf), "ld": ("sbuf", [128, 32], bf),
+    "cb": ("sbuf", [128, 3, PITCH], bf), "eb": ("sbuf", [128, 3, PITCH], bf),
+    "nq": ("sbuf", [128, 136], bf), "nn": ("sbuf", [128, 128], bf),
     "jj": ("sbuf", [128, W], f32), "jt": ("sbuf", [128, 8], f32), "inv": ("sbuf", [128, W], bf),
     "tt": ("sbuf", [128, 128], f32),
     "mk": ("sbuf", [128, 2048], bf), "xx": ("sbuf", [128, 2072], bf),
-    "oh": ("sbuf", [128, 11 * PA + 8], bf), "oi": ("sbuf", [128, 12 * PB + 8], bf),
-    "mm": ("sbuf", [128, 48], f16), "pay": ("sbuf", [128, 16 * R], f16), "land": ("sbuf", [128, 16 * NR * R], f16),
-    "neg": ("sbuf", [128, 128], bf), "low": ("sbuf", [128, 48], f32),
+    "o0": ("sbuf", [128, 10 * P1 + 8], bf), "o1": ("sbuf", [128, 10, 122], bf), "o2": ("sbuf", [128, 11, 122], bf), "o3": ("sbuf", [128, 12, 122], bf),
+    "mm": ("sbuf", [128, 48], f16), "pay": ("sbuf", [128, 32 * R], f16), "land": ("sbuf", [128, 32 * NR * R], f16),
+    "neg": ("sbuf", [128, 128], bf), "far": ("sbuf", [128, 128], bf), "low": ("sbuf", [128, 48], f32),
     "sc": ("sbuf", [128, 48], f32), "tr": ("sbuf", [128, 36], f32), "rnd": ("sbuf", [128, 36], f32),
     "kk": ("sbuf", [128, 36 * R], f32),
     "fo": ("sbuf", [128, W], bf), "ded": ("sbuf", [128, W], bf),
@@ -50,7 +52,7 @@ SCRATCH = {
     "zz": ("sbuf", [128, 128], f32),
     "y0": ("sbuf", [128, 2048], bf), "yw": ("sbuf", [128, WIN], bf),
     "v0": ("sbuf", [128, 2048], f32), "fw": ("sbuf", [128, WIN], f32),
-    "ft": ("sbuf", [128, 128], f32), "fa": ("sbuf", [128, 128], f32), "fb": ("sbuf", [128, 128], f32),
+    "ft": ("sbuf", [128, 128], f32), "fa": ("sbuf", [128, 128], f32), "fu": ("sbuf", [128, 128], f32),
     "fc": ("sbuf", [128, 128], f32),
     "mgs": ("sbuf", [128, 12], f32), "nk": ("sbuf", [128, 4], f32), "wa": ("sbuf", [128, 4], bf),
     "wb": ("sbuf", [128, 4], f32), "mt4": ("sbuf", [128, 8], f32), "fls": ("sbuf", [128, 4], f32),
@@ -59,7 +61,7 @@ SCRATCH = {
     "e2": ("psum", [128, 512], f32), "e3": ("psum", [128, 512], f32),
 }
 PSUM = ("p1", "p2", "p3", "pb", "e0", "e1", "e2", "e3")
-SEMAPHORES = (["cv", "ca", "cp", "cg", "dpos", "dst", "dle", "dve", "dft", "dout", "dout2", "sent"]
+SEMAPHORES = (["cv", "ca", "cp", "cg", "dpos", "dst", "dle", "dve", "dft", "dfu", "dy", "dz", "dout", "dout2", "sent"]
               + ["ar%d_%d" % (t, s) for t in range(R) for s in range(NR)])
 
 
@@ -156,105 +158,100 @@ def rank_program(g, core, T, topo):
         u, k = t - 1, "%d" % t
         sel, sk = T.sel[:, 16 * u:16 * u + WID[t]], ["sel" + k]
         pat, neg, one = [[-ns, WID[t]]], [[ns, WID[t]]], [[0, 1]]
-        scale = 256 if t == 1 else 128
-        sL, sA, sR = [T.rows[:, 4 * u + i:4 * u + i + 1] for i in range(3)]
-        if t == 1:
-            sels = [lambda: pick(sel, T.oneb[:, 0:WID[t]], pat, A.is_ge, 0, 1, ["oneb"], sk),
-                    lambda: pick(sel, sel, neg, A.is_ge, ns - 1, -1, sk, sk)]
-        else:
-            top = T.sel[:, 16 * u + np_ - 1:16 * u + np_]
-            sels = [lambda: io(sel, [[0, WID[t]]], 0, sk, base=-1),
-                    lambda: pick(sel, sel, pat, A.is_ge, -ns, 1, sk, sk, fill=1.0),
-                    lambda: pick(sel, sel, pat, A.is_ge, 0, 1, sk, sk),
-                    lambda: pick(sel, sel, neg, A.is_ge, 2 * ns - 1, -1, sk, sk),
-                    lambda: pick(top, top, one, A.is_ge, -ns, 1, sk, sk, fill=1.0)]
-        rest = [lambda: io(T.rows[:, 4 * u:4 * u + 3], [[0, 3]], 0, ["sL" + k, "sA" + k, "sR" + k], base=scale),
-                lambda: pick(T.aa[0:ns, 128 * u:128 * u + np_ * ns], T.oneb[0:ns, 0:np_ * ns], [[0, np_], [-1, ns]],
+        scale = 128
+        lc, old = T.lc[0:64, 32 * u:32 * u + 32], T.rows[0:64, u:u + 1]
+        left, right = T.lc[0:64, 32 * u:32 * u + 16], T.lc[0:64, 32 * u + 16:32 * u + 32]
+        ends = T.sel[:, 16 * u:16 * u + np_ + 1:np_]
+        sels = [lambda: io(sel, [[0, WID[t]]], 0, sk, base=-1),
+                lambda: pick(sel, sel, pat, A.is_ge, 0, 1, sk, sk, fill=1.0),
+                lambda: pick(sel, sel, pat, A.is_ge, ns, 1, sk, sk),
+                lambda: pick(sel, sel, neg, A.is_ge, ns - 1, -1, sk, sk),
+                lambda: pick(ends, ends, [[0, 2]], A.is_ge, np_ * ns - 1, -1, sk, sk, fill=1.0)]
+        io(T.aa[0:ns, 128 * u + np_ * ns:128 * u + np_ * ns + 1], one, 0, ["a1" + k], base=1)
+        rest = [lambda: pick(T.aa[0:ns, 128 * u:128 * u + np_ * ns], T.oneb[0:ns, 0:np_ * ns], [[0, np_], [-1, ns]],
                              A.is_equal, 0, 1, ["oneb"], ["aa" + k]),
-                lambda: pick(sL, sL, one, A.is_ge, ns - 1, -1, ["sL" + k], ["sL" + k]),
-                lambda: pick(sR, sR, one, A.is_ge, -ns, 1, ["sR" + k], ["sR" + k]),
-                lambda: pick(T.ec[0:64, 128 * u:128 * u + 128], T.oneb[0:64, 0:128], [[0, 4], [1, 32]], A.is_equal,
-                             -(S0 + u), 0, ["oneb"], ["ec" + k]),
-                lambda: pick(sA, sL, one, A.is_ge, 2 * ns - 1, -1, ["sL" + k], ["sA" + k], fill=float(-scale)),
-                lambda: pick(sR, sR, one, A.is_ge, 2 * ns - 1, -1, ["sR" + k], ["sR" + k]),
-                lambda: pick(T.slb[:, u:u + 1], sL, one, A.is_ge, 0, 0, ["sL" + k], ["sB" + k])]
+                lambda: io(lc, [[0, 32]], 0, ["lc" + k, "lr" + k], base=scale),
+                lambda: io(old, one, 0, ["old" + k], base=scale),
+                lambda: pick(left, left, [[0, 16]], A.is_ge, ns - 1, -1, ["lc" + k], ["lc" + k], fill=float(-scale)),
+                lambda: pick(right, right, [[0, 16]], A.is_ge, -32, 1, ["lr" + k], ["lr" + k]),
+                lambda: pick(left, left, [[0, 16]], A.is_ge, 2 * ns - 1, -1, ["lc" + k], ["lc" + k]),
+                lambda: pick(T.rows[0:32, u:u + 1], T.rows[0:32, u:u + 1], one, A.is_ge, ns - 1, -1, ["old" + k], ["old" + k]),
+                lambda: pick(lc, lc, [[0, 2], [1, 16]], A.is_equal, -(S0 + u), 0, ["lc" + k, "lr" + k], ["lc" + k])]
         for i, call in enumerate(rest):
+            call()
             if i < len(sels):
                 sels[i]()
-            call()
 
     def slot_masks(t):
         np_, ns, _ = SLOT[t]
         u, k = t - 1, "%d" % t
-        mm(T.e0[0:np_ * ns, 0:3 * ns], T.aa[0:ns, 128 * u:128 * u + np_ * ns], T.aa[0:ns, 128 * u:128 * u + 3 * ns],
-           True, True, ["aa" + k], ["e0"])
-        act(T.dm[0:np_ * ns, 48 * u:48 * u + 3 * ns], T.e0[0:np_ * ns, 0:3 * ns], 0.0, 1.0, ["e0"], ["dm" + k])
-        act(T.lc[0:64, 144 * u:144 * u + 128], T.ec[0:64, 128 * u:128 * u + 128], 0.0, T.rows[0:64, 4 * u + 1:4 * u + 2],
-            ["ec" + k, "sA" + k], ["lc" + k])
-        act(T.lc[0:64, 144 * u + 128:144 * u + 144], T.ec[0:64, 128 * u:128 * u + 16], 0.0, T.rows[0:64, 4 * u + 2:4 * u + 3],
-            ["ec" + k, "sR" + k], ["lr" + k])
+        n8 = np_ * ns + 1
+        mm(T.e0[0:n8, 0:3 * ns], T.aa[0:ns, 128 * u:128 * u + n8], T.aa[0:ns, 128 * u:128 * u + 3 * ns],
+           True, True, ["aa" + k, "a1" + k], ["e0"])
+        act(T.dm[0:n8, 48 * u:48 * u + 3 * ns], T.e0[0:n8, 0:3 * ns], 0.0, 1.0, ["e0"], ["dm" + k])
 
-    op("g", lambda: g.iota(T.pin[:, 0:1], [[0, 1]], 0, 1), [], ["pin0"])
-    io(T.nid[:], [[1, W]], 0, ["nid"])
+    op("g", lambda: g.iota(T.pin[:], [[-1, 16]], 128, 1), [], ["pin0"])
+    io(T.oneb[:], [[0, 144]], 0, ["oneb"], base=1)
+    io(T.pf[0:8, 0:1], [[0, 1]], 2048, ["goff"])
+    pick(T.big[:], T.oneb[:], [[-16, 9], [1000, 16]], A.is_ge, -15000, 1, ["oneb"], ["big"])
+    pick(T.big[:], T.big[:], [[16, 9], [0, 16]], A.is_ge, 15, -1, ["big"], ["big"])
     io(T.onef[:], [[0, 128]], 0, ["onef"], base=1)
     pick(T.g8[0:8, :], T.onef[0:8, :], [[-1, 8], [0, 16]], A.is_equal, 0, 1, ["onef"], ["g8"])
-    io(T.n31[:], [[0, 4], [1, 32]], 0, ["n31"], base=AOFF)
-    io(T.oneb[:], [[0, 144]], 0, ["oneb"], base=1)
-    io(T.hs[0:32, :], [[-16, 16]], -1, ["hs"], base=BASE - 256)
+    io(T.jj[:], [[1, W]], 128, ["jj"], base=-8)
     pick(T.repf[0:32, :], T.onef[0:32, :], [[0, 4], [-1, 32]], A.is_equal, 0, 1, ["onef"], ["repf"])
-    pick(T.hs[0:32, :], T.hs[0:32, :], [[-1, 16]], A.not_equal, 0, 1, ["hs"], ["hs"], fill=-1.0e9)
+    OH = {t: ["o%d_%d" % (t, x) for x in range(SLOT[t][0] + 1 if t else S0)] for t in range(R)}
+    io(T.hs[0:32, :], [[-16, 16]], -1, ["hs"], base=BASE - 256)
     io(T.low[:], [[0, 48]], 0, ["low"], base=LOW)
-    io(T.n16[0:64, :], [[1, 16]], 0, ["n16"], base=-BOFF)
-    slot_tables(1)
-    OH = ["oh%d" % x for x in range(12)]
-    OI = ["oi%d" % x for x in range(12)]
-    ms(T.oh[:], 0.0, OH)
-    ms(T.xx[:, 0:8], 0.0, ["xpad0"])
+    pick(T.hs[0:32, :], T.hs[0:32, :], [[-1, 16]], A.not_equal, 0, 1, ["hs"], ["hs"], fill=-1.0e9)
+    pick(T.repb[0:32, :], T.oneb[0:32, 0:128], [[0, 4], [-1, 32]], A.is_equal, 0, 1, ["oneb"], ["repb"])
+    for c in range(129, P1):
+        io(T.o0[:, c:10 * P1:P1], [[0, 10]], 0, ["o0gap%d" % c])
+    io(T.o0[:, 10 * P1:10 * P1 + 1], [[0, 1]], 0, ["o0pad"])
+    for i in range(C0):
+        pick(T.tri3[0:32, 128 * i:128 * i + 128], T.oneb[0:32, 0:128], [[0, 4], [1, 32]], A.is_equal, -i, -C0,
+             ["oneb"], ["tri3_%d" % i])
+    io(T.rows[0:64, 4:5], [[0, 1]], 0, ["ab4"], base=1)
+    io(T.rows[0:64, 5:7], [[0, 2]], 0, ["ab5", "ab6"])
+    io(T.n16[0:64, :], [[0, 2], [1, 16]], 0, ["n16", "n16r"], base=AOFF)
+    for c, fill in ((4, -16), (5, 1), (6, AOFF + BOFF)):
+        pick(T.rows[0:64, c:c + 1], T.rows[0:64, c:c + 1], [[0, 1]], A.is_ge, 31, -1, ["ab%d" % c], ["ab%d" % c],
+             fill=float(fill))
+    ts(T.pin[:], T.pin[:], 15, None, A.bitwise_and, None, ["pin0"], ["pin0"])
     ms(T.xx[:, 2056:2072], 0.0, ["xpad1"])
-    p0 = T.pin[:, 0:1]
-    ts(T.pin[:, 1:2], p0, 15, None, A.bitwise_and, None, ["pin0"], ["pin1"])
-    ts(T.pin[:, 2:3], p0, 31, None, A.bitwise_and, None, ["pin0"], ["pin2"])
-    ts(T.pin[:, 3:4], p0, 112, None, A.bitwise_and, None, ["pin0"], ["pin3"])
-    ms(T.p1[:, 0:16], 0.0, ["p1"])
-    cp(T.pf[:, 0:4], T.pin[:, 0:4], ["pin%d" % i for i in range(4)], ["pf"])
-    fR, f31, fG16 = [T.pf[:, i:i + 1] for i in range(1, 4)]
-    ms(T.p2[:, 0:16], 0.0, ["p2"])
-    ts(T.tm[:], T.nid[:, 0:16], fR, None, A.is_equal, None, ["nid", "pf"], ["tm"])
-    ts(T.big[:], T.nid[:, 0:144], -15.0, fG16, A.add, A.is_equal, ["nid", "pf"], ["big"])
-    ts(T.pf[:, 9:10], fR, 128.0, -8.0, A.mult, A.add, ["pf"], ["pf9"])
+    ms(T.xx[:, 0:8], 15.0 / 16, ["xpad0"])
+    ts(T.tm[:], T.pin[:], 0.0, None, A.is_equal, None, ["pin0"], ["tm"])
+    ms(T.p1[:, 0:32], 0.0, ["p1"])
 
     ts(T.hiu[:], T.posi[:], -255.5, 1.0 / 512, A.add, A.mult, ["posi"], ["hiu"])
     ts(T.tmpi[:], T.posi[:], 511, None, A.bitwise_and, None, ["posi"], ["tmp1"])
-    cuts = [0] + list(range(160, 2048, 256)) + [2048]
+    cuts = [0, 128, 448, 768, 1120, 1440, 1696, 1824, 1952, 2048]
     NC = len(cuts) - 1
-    for i in range(NC):
+    cp(T.mk[:, 0:cuts[1]], T.tm[:, 0:16].indirect(T.hiu[:, 0:cuts[1] // 16]), ["tm", "hiu"], ["mk0"])
+    for i in range(1, NC):
         a, b = cuts[i], cuts[i + 1]
         op("a", lambda: S.activation(T.mk[:, a:b], T.tm[:, 0:16].indirect(T.hiu[:, a // 16:b // 16]), AF.Copy),
            ["tm", "hiu"], ["mk%d" % i])
-    act(T.fw[:, 0:2048], T.mk[:], 0.0, 0.0, ["mk%d" % i for i in range(NC)], ["fw"], fn=AF.Silu)
+    act(T.fc[:], T.mk[:, 0:128], 0.0, 0.0, ["mk0"], ["fc"], fn=AF.Silu)
     cp(T.lou[:], T.tmpi[:], ["tmp1"], ["lou"])
+    ts(T.lef[0:8, 0:1], T.lei[0:8, 0:1], T.pf[0:8, 0:1], None, A.add, None, ["lei", "goff"], ["lef"])
     done_r = 0
     for i in range(NC):
         a, b = cuts[i], cuts[i + 1]
         tt(T.xx[:, 8 + a:8 + b], T.stw[:, 0:512].indirect(T.lou[:, a // 16:b // 16]), T.mk[:, a:b], A.mult,
            ["stw", "lou", "mk%d" % i], ["x%d" % i])
-        if i == 0:
-            cp(T.lef[0:8, 0:1], T.lei[0:8, 0:1], ["lei"], ["lef"])
-        if i == 1:
-            ts(T.jj[:], T.nid[:], T.pf[:, 9:10], None, A.add, None, ["nid", "pf9"], ["jj"])
-        if i == 2:
+        if i == 3:
             mm(T.pb[:, 0:1], T.g8[0:8, :], T.lef[0:8, 0:1], True, True, ["g8", "lef"], ["pb"])
-        while done_r < 16 and (i == NC - 1 or 128 * done_r + 144 <= b):
+        while done_r < 16 and (i == NC - 1 or 128 * done_r + W - 8 <= b):
             r = done_r
-            mm(T.e0[:, 0:W], T.big[:, 15 - r:143 - r], T.xx[:, 128 * r:128 * r + W], r == 0, r == 15,
+            c = cuts[-2] + 8 - 128 * r if r == 15 else 0
+            mm(T.e0[:, c:W], T.big[:, 15 - r:143 - r], T.xx[:, 128 * r + c:128 * r + W], r == 0, r == 15,
                ["big", "xpad0", "xpad1"] + ["x%d" % k for k in range(i + 1)], ["e0"])
             done_r += 1
         if i == NC - 2:
-            ts(T.inv[:, 0:8], T.jj[:, 0:8], 0.0, 15.0, A.is_lt, A.mult, ["jj"], ["inv0"])
-            ts(T.jt[:], T.jj[:, 0:8], T.pb[:, 0:1], 15.0, A.is_ge, A.mult, ["jj", "pb"], ["jt"])
-    ts(T.inv[:, 8:W], T.jj[:, 8:W], T.pb[:, 0:1], 15.0, A.is_ge, A.mult, ["jj", "pb"], ["inv1"])
-    tt(T.inv[:, 0:8], T.inv[:, 0:8], T.jt[:], A.max, ["jt", "inv0"], ["inv0"])
-    tt(T.fo[:], T.e0[:, 0:W], T.inv[:], A.max, ["e0", "inv0", "inv1"], ["fo"])
+            mm(T.e0[:, 0:b + 8 - 128 * 15], T.big[:, 0:128], T.xx[:, 128 * 15:b + 8], False, False,
+               ["big"] + ["x%d" % k for k in range(i + 1)], ["e0"])
+    ts(T.inv[:], T.jj[:], T.pb[:, 0:1], 15.0, A.is_ge, A.mult, ["jj", "pb"], ["inv"])
+    tt(T.fo[:], T.e0[:, 0:W], T.inv[:], A.max, ["e0", "inv"], ["fo"])
 
     cores = list(T.cores)
     chips = []
@@ -263,6 +260,9 @@ def rank_program(g, core, T, topo):
             chips.append(topo.chip(c))
     on = {ch: [c for c in cores if topo.chip(c) == ch] for ch in chips}
 
+    def one_link(c, x):
+        return topo.same_plane(topo.chip(c), topo.chip(x)) or topo.mates(topo.chip(c), topo.chip(x))
+
     def far_of(c):
         i = chips.index(topo.chip(c))
         m = on[topo.chip(c)].index(c)
@@ -270,14 +270,14 @@ def rank_program(g, core, T, topo):
         for d in range(1, len(chips)):
             row = on[chips[(i + d) % len(chips)]]
             out += [row[(m + k) % len(row)] for k in range(len(row))]
-        return sorted(out, key=lambda x: topo.same_plane(topo.chip(c), topo.chip(x)) or topo.mates(topo.chip(c), topo.chip(x)))
+        return sorted(out, key=lambda x: one_link(c, x))
 
     far = far_of(core)
     near = [c for c in on[topo.chip(core)] if c != core]
     far_eng = [e for e in topo.engines(core, far[0]) if all(e in topo.engines(core, c) for c in far)]
     near_eng = [e for e in topo.engines(core, near[0]) if e not in far_eng][0:4:2]
     senders = [(c, len(near_eng)) for c in near]
-    senders += [(c, len(far_eng)) for c in sorted(far, key=lambda c: far_of(c).index(core))]
+    senders += [(c, len(far_eng)) for c in sorted(far, key=lambda c: far_of(c).index(core) + 1.5 * (not one_link(c, core)))]
 
     def did(c):
         a = topo.addr(c)
@@ -288,82 +288,104 @@ def rank_program(g, core, T, topo):
             op("a", lambda: S.activation(T.y0[:, r:2048:16], T.vew[:, 0:8192].indirect(T.pou[:, 8 * r:8 * r + 8]),
                                          AF.Copy), ["vew", "pou"], ["y0_%d" % r])
 
+    def sign_planes(t, off):
+        planes, slots, steps = SLOT[t]
+        for x in range(planes):
+            act(T["o%d" % t][:, :, slots * x:slots * (x + 1)], T.fo[:, 8:8 + slots * steps], off - x - 0.5, 1.0,
+                ["fo"], [OH[t][x]], fn=AF.Sign)
+
     def codes_out(banks):
         for b in banks:
             bank = "e%d" % b
             for q in range(4):
                 r = 4 * b + q
-                mm(T[bank][:, 128 * q:128 * q + 128], T.idn[:, r:r + 128], T.pc[:, W + 8:W + 136], True, True,
-                   ["idn", "pcr"], [bank])
-            for q in range(4):
-                r = 4 * b + q
-                act(T.v0[:, r:2048:16], T[bank][:, 128 * q:128 * q + 128], BASE + 16.0, -1.0, [bank], ["v0_%d" % r])
+                mm(T[bank][:, 128 * q:128 * q + 128], T.idn[:, r:r + 128], T.fo[:, 8:136], True, True,
+                   ["idn", "fo"], [bank])
+            if b < 3:
+                for q in range(4):
+                    r = 4 * b + q
+                    act(T.v0[:, r:2048:16], T[bank][:, 128 * q:128 * q + 128], 32.0 + S0 + R - 2, 1.0, [bank], ["v0_%d" % r])
 
     FM, M1 = T.e1[:, 0:W], T.e1[:, 256:256 + W]
     AL = 128
     T16, R0 = T.e3, T.e2
     PCR = W
+    fR = T.pf[:, 1:2]
     off = 0
     for t in range(R):
         NS = S0 + t
         last = t == R - 1
         wd = WID[t]
-        pay = T.pay[:, 16 * t:16 * t + wd]
+        pay = T.pay[:, 32 * t:32 * t + wd]
         if t == 0:
-            nm = 128
-            for x in range(NS):
-                ts(T.oh[:, PA * x:PA * x + 129], T.fo[:, 7:136], float(x), None, A.is_equal, None, ["fo"], ["oh%d" % x])
-            span = PA * (NS - 1) + 1
-            for j in range(128):
-                q = j - j % 32
-                mm(T.p1[q:q + NS, 0:NS], T.oh[:, j + 1:j + 1 + span:PA], T.oh[:, j:j + span:PA], j == q, j == q + 31,
-                   OH, ["p1"])
+            act(T.nq[:, 0:129], T.fo[:, 7:136], 1.0 - NS, 1.0, ["fo"], ["nq"], fn=AF.Abs)
+            act(T.o0[:, 0:129], T.fo[:, 7:136], 1.0, -1.0, ["fo"], [OH[0][0]], fn=AF.Relu)
+            act(T.o0[:, P1 * (NS - 1):P1 * (NS - 1) + 129], T.nq[:, 0:129], 1.0, -1.0, ["nq"], [OH[0][NS - 1]], fn=AF.Relu)
+            sign_planes(1, 0)
+            for x in range(1, NS - 1):
+                ts(T.o0[:, P1 * x:P1 * x + 129], T.fo[:, 7:136], float(x), None, A.is_equal, None, ["fo"], [OH[0][x]])
+            step = P1 // C0
+            per = -(-step // 4)
+            for j in range(step):
+                q = 32 * (j // per)
+                mm(T.p1[q:q + wd, 0:wd], T.o0[:, j + 1:j + 2 + step * (wd - 1):step], T.o0[:, j:j + 1 + step * (wd - 1):step],
+                   j % per == 0, j % per == per - 1 or j == step - 1, OH[0] + ["o0pad"], ["p1"])
+            for i in range(C0):
+                mm(T.e0[:, 128 * i:128 * i + 128], T.tri3[0:32, 128 * i:128 * i + 128], T.repb[0:32, :], True, True,
+                   ["tri3_%d" % i, "repb"], ["e0"])
+            act(T.rep[:, 0:128 * C0], T.e0[:, 0:128 * C0], 0.0, 256.0, ["e0"], ["rep"])
             ts(T16[:, 0:W], T.fo[:], -16.0, float(BASE), A.mult, A.add, ["fo"], ["e3"])
-            ts(T.pb[:, AL:AL + W], T.inv[:], 0.0, None, A.is_equal, None, ["inv0", "inv1"], ["pb"])
+            ts(T.pb[:, AL:AL + W], T.inv[:], 0.0, None, A.is_equal, None, ["inv"], ["pb"])
             cp(T.pou[:], T.posi[:], ["posi"], ["pou"])
             ms(T.pc[:, 0:2 * W:2 * W - 1], 0.0, ["pcl", "pcr"])
-            ms(T.cb[:], 0.0, ["cb0", "cb1", "cb2"])
-            ts(T.pf[:, 10:11], f31, float(AOFF), None, A.add, None, ["pf"], ["pf10"])
             cp(pay, T.p1[:, 0:wd], ["p1"], ["pay0"])
-            ts(T.rep[:], T.n31[:], T.pf[:, 10:11], 256.0, A.is_equal, A.mult, ["n31", "pf10"], ["rep"])
-            slot_masks(1)
-            vectors(range(0, 11))
+            ms(T.cb[:], 0.0, ["cb0", "cb1", "cb2"])
+            cp(fR, T.pin[:, 0:1], ["pin0"], ["pf"])
+            ms(T.p2[:, 0:16], 0.0, ["p2"])
+            vectors(range(0, 9))
         else:
             np_, ns, nc = SLOT[t]
-            n8, nm = np_ * ns, 3 * ns
+            n8, nm = np_ * ns + 1, 3 * ns
             u = t - 1
             K, RK, KR = T.kk[:, 36 * u + 31:36 * u + 32], T.kk[:, 36 * u + 33:36 * u + 34], ["kk%d" % u]
-            cb, oh, pitch, OHK = (T.cc, T.oi, PB, OI) if last else (T.cb, T.oh, PA, OH)
-            ts(T.eb[:, 0:3 * pitch], cb[:, 1:1 + 3 * pitch], RK, K, A.add, A.is_equal, ["cb0", "cb1", "cb2"] + KR, ["eb"])
-            for k in range(nc):
-                mm(T.p1[0:n8, 0:nm], oh[:, k + 1:k + 2 + nc * (n8 - 1):nc], T.eb[:, k:k + 1 + nc * (nm - 1):nc],
-                   k == 0, k == nc - 1, OHK + ["eb"], ["p1"])
+            if t == 1:
+                dma("s", "dy", T.fw[0:128:16, 0:2048], T.fc[:], ["fc"] + KR, ["fw"])
+                dma("s", "dz", T.fw[0:128:16, 4096:WIN], T.fc[:], ["fc"], ["fwz"])
+            for i, (a, b) in enumerate([(0, 4), (4, nc)]):
+                ts(T.eb[:, :, 1 + a * ns:1 + b * ns], T.cb[:, :, 1 + a * ns:1 + b * ns], RK, K, A.add, A.is_equal,
+                   ["cb0", "cb1", "cb2"] + KR, ["eb%d" % i])
+                for k in range(a, b):
+                    mm(T.p1[0:n8, 0:nm], T["o%d" % t][:, k, 0:n8], T.eb[:, :, 1 + k * ns:1 + (k + 1) * ns], k == 0, k == nc - 1,
+                       OH[t] + ["eb%d" % i], ["p1"])
             ts(T.ne[:], T.pc[:], RK, K, A.add, A.not_equal, ["pcl", "pcr"] + KR, ["ne"])
             tt(M1, FM, T.ne[:, 0:W], A.mult, ["e1", "ne"], ["e1"])
-            tt(T.pb[:, AL:AL + W], T.pb[:, AL:AL + W], T.ne[:, 0:W], A.mult, ["pb", "ne"], ["pb"])
             tt(T.mm[0:n8, 0:nm], T.p1[0:n8, 0:nm], T.dm[0:n8, 48 * u:48 * u + nm], A.mult, ["p1", "dm%d" % t], ["mm"])
-            mm(T.p2[0:nm, 0:wd], T.mm[0:n8, 0:nm], T.sel[0:n8, 16 * u:16 * u + wd], True, True, ["mm", "sel%d" % t], ["p2"])
+            for lo, a, b in ((0, 0, 2 * ns), (32, 2 * ns, nm)):
+                mm(T.p2[lo:lo + b - a, 0:wd], T.mm[0:n8, a:b], T.sel[0:n8, 16 * u:16 * u + wd], True, True,
+                   ["mm", "sel%d" % t], ["p2"])
             tt(T.fo[:], M1, T.ne[:, W:2 * W], A.mult, ["e1", "ne"], ["fo"])
-            cp(pay, T.p2[:, 0:wd], ["p2"], ["pay%d" % t])
             off = NS - 1
             act(T.nk[:, u:u + 1], K, RK, -1.0, KR, ["nk%d" % u])
             act(T.mt4[:, 0:1], RK, 256.0, 1.0, KR, ["r256"])
             act(T.wa[:, u:u + 1], T.nk[:, u:u + 1], (BASE - 7.5) / 16 + AOFF, 1.0 / 16, ["nk%d" % u], ["a%d" % u])
-            act(T.wb[:, u:u + 1], T.wa[:, u:u + 1], T.nk[:, u:u + 1], -16.0, ["nk%d" % u, "a%d" % u], ["b%d" % u])
+            act(T.mt4[0:64, 1:2], T.nk[0:64, u:u + 1], T.rows[0:64, 6:7], T.rows[0:64, 5:6], ["nk%d" % u, "ab5", "ab6"], ["nkb"])
+            act(T.mt4[0:64, 2:3], T.wa[0:64, u:u + 1], T.mt4[0:64, 1:2], T.rows[0:64, 4:5], ["nkb", "ab4", "a%d" % u], ["ab"])
+            cp(pay, T.p2[:, 0:wd], ["p2"], ["pay%d" % t])
+            tt(T.pb[:, AL:AL + W], T.pb[:, AL:AL + W], T.ne[:, 0:W], A.mult, ["pb", "ne"], ["pb"])
+            ts(T.ht[0:32, :], T.p3[0:32, 0:16], T.kk[0:32, 36 * u + 31:36 * u + 32], T.mt4[0:32, 0:1], A.is_equal, A.mult,
+               ["p3", "r256"] + KR, ["ht"])
+            ts(T.ld[0:64, :], T.n16[0:64, :], T.mt4[0:64, 2:3], T.rows[0:64, u:u + 1], A.is_equal, A.mult,
+               ["n16", "n16r", "old%d" % t, "ab"], ["ld"])
+            act(T16[:, 0:W], T.fo[:], float(BASE - 17 * off), -16.0, ["fo"], ["e3"])
+            act(T.wb[0:1, u:u + 1], T.wa[0:1, u:u + 1], T.nk[0:1, u:u + 1], -16.0, ["a%d" % u, "nk%d" % u], ["b%d" % u])
             if last:
-                tt(T.alx[:], T.pb[:, AL:AL + W], T.fst[:], A.add, ["pb", "fst"], ["alx"])
-                act(T16[:, 0:W], T.fo[:], float(BASE - 17 * off), -16.0, ["fo"], ["e3"])
-                act(T.ded[:], T.alx[:], 1.0, -1.0, ["alx"], ["ded"])
+                codes_out([0, 2, 1])
             else:
                 act(T.ded[:], T.pb[:, AL:AL + W], 1.0, -1.0, ["pb"], ["ded"])
-                act(T16[:, 0:W], T.fo[:], float(BASE - 17 * off), -16.0, ["fo"], ["e3"])
                 act(FM, T.fo[:], float(off - NS), 1.0, ["fo"], ["e1"])
-                noh, npitch, nk_ = (T.oi, PB, "oi%d") if t == R - 2 else (T.oh, PA, "oh%d")
-                for x in range(0 if t == 1 else 1, SLOT[t + 1][0]):
-                    act(noh[:, npitch * x + 1:npitch * x + 129], T.fo[:, 8:136], off - x + 0.5, 1.0, ["fo"], [nk_ % x],
-                        fn=AF.Sign)
+                sign_planes(t + 1, off)
 
-        slot = T.land[:, 16 * (NR * t + rank):16 * (NR * t + rank) + wd]
+        slot = T.land[:, 32 * (NR * t + rank):32 * (NR * t + rank) + wd]
         order("g", ["pay%d" % t], [])
         sem = T.sem["ar%d_%d" % (t, rank)]
         g.remote_dma_fused([
@@ -374,8 +396,13 @@ def rank_program(g, core, T, topo):
         ], local_sem=T.sem.sent)
         count["sent"] += len(far_eng) + len(near_eng)
 
+        if not last:
+            planes, slots, steps = SLOT[t + 1]
+            io(T["o%d" % (t + 1)][:, :, planes * slots], [[0, steps]], 0, [OH[t + 1][planes]], base=1)
+            slot_tables(t + 1)
         if t == 0:
-            slot_tables(2)
+            pick(T.n16[0:64, 0:16], T.n16[0:64, 0:16], [[0, 16]], A.is_ge, 31, -1, ["n16"], ["n16"])
+            pick(T.n16[0:64, 16:32], T.n16[0:64, 16:32], [[0, 16]], A.is_ge, -32, 1, ["n16r"], ["n16r"])
             tt(T.pc[:, 1:W], T16[:, 0:W - 1], T.fo[:, 1:W], A.subtract, ["e3", "fo"], ["pcl"])
             tt(T.pc[:, W:2 * W - 1], T16[:, 0:W - 1], T.fo[:, 1:W], A.subtract, ["e3", "fo"], ["pcr"])
             ts(FM, T.fo[:], float(-NS), None, A.add, None, ["fo"], ["e1"])
@@ -386,61 +413,48 @@ def rank_program(g, core, T, topo):
             ms(T.rnd[:, 33:34], -M31, ["rnd2"])
         else:
             if t == 1:
-                slot_tables(3)
                 pick(T.idn[:], T.oneb[:], [[-1, 144]], A.is_equal, 0, 1, ["oneb"], ["idn"])
             if t == 2:
-                pick(T.tri[:], T.onef[:], [[1, 128]], A.is_gt, 0, -1, ["onef"], ["tri"])
                 io(T.neg[:], [[0, 128]], 0, ["neg"], base=-1)
                 io(T.ee[:, 128:136], [[0, 8]], 0, ["eepad"])
-                pick(T.tri[:], T.tri[:], [[-16, 8], [0, 16]], A.is_ge, 0, 1, ["tri"], ["tri"])
             if last:
+                io(T.far[:], [[0, 128]], 0, ["far"], base=4096)
+                pick(T.tri[:], T.onef[:], [[1, 128]], A.is_gt, 0, -1, ["onef"], ["tri"])
+                pick(T.far[:], T.far[:], [[-1, 128]], A.is_equal, 0, 1, ["far"], ["far"])
                 pick(T.gsel[:], T.onef[:, 0:8], [[-16, 8]], A.is_ge, 0, 1, ["onef"], ["gsel"])
+                pick(T.tri[:], T.tri[:], [[-16, 8], [0, 16]], A.is_ge, 0, 1, ["tri"], ["tri"])
                 pick(T.gsel[:], T.gsel[:], [[16, 8]], A.is_ge, 15, -1, ["gsel"], ["gsel"])
-            ts(T.ht[0:32, :], T.p3[0:32, 0:16], T.kk[0:32, 36 * u + 31:36 * u + 32], T.mt4[0:32, 0:1], A.is_equal, A.mult,
-               ["p3", "r256"] + KR, ["ht"])
             tt(T.cd[:, 1:W], T16[:, 0:W - 1], T.fo[:, 1:W], A.subtract, ["e3", "fo"], ["cd"])
             tt(T.hs[0:32, :], T.p3[0:32, 0:16], T.ht[0:32, :], A.subtract, ["p3", "ht"], ["hs"])
             if last:
-                tt(T.d1[:, 1:W], T.alx[:, 1:W], T.cd[:, 1:W], A.mult, ["cd", "alx"], ["d1"])
-            else:
-                tt(T.d1[:, 1:W], T.pb[:, AL + 1:AL + W], T.cd[:, 1:W], A.mult, ["cd", "pb"], ["d1"])
-            ts(T.ld[0:nm, 0:128], T.n31[0:nm, :], T.wa[0:nm, u:u + 1], T.slb[0:nm, u:u + 1], A.is_equal, A.mult,
-               ["n31", "sB%d" % t, "a%d" % u], ["ld0"])
-            scan(T.pc[:, 2 * W - 2:W - 1:-1], T.ded[:, W - 1:0:-1], T.d1[:, W - 1:0:-1], 0.0, A.mult, A.add,
-                 ["ded", "d1"], ["pcr"])
-            if last:
-                codes_out([0, 2, 3, 1])
-            else:
+                codes_out([3])
+            tt(T.d1[:, 1:W], T.pb[:, AL + 1:AL + W], T.cd[:, 1:W], A.mult, ["cd", "pb"], ["d1"])
+            tt(T.lab[0:64, :], T.lc[0:64, 32 * u:32 * u + 32], T.ld[0:64, :], A.subtract, ["lc%d" % t, "ld"], ["lab"])
+            if not last:
+                scan(T.pc[:, 2 * W - 2:W - 1:-1], T.ded[:, W - 1:0:-1], T.d1[:, W - 1:0:-1], 0.0, A.mult, A.add,
+                     ["ded", "d1"], ["pcr"])
                 scan(T.pc[:, 1:W], T.ded[:, 1:W], T.d1[:, 1:W], 0.0, A.mult, A.add, ["ded", "d1"], ["pcl"])
-            ts(T.ld[0:nm, 128:144], T.n16[0:nm, :], T.wb[0:nm, u:u + 1], T.rows[0:nm, 4 * u + 2:4 * u + 3], A.is_equal, A.mult,
-               ["n16", "sR%d" % t, "b%d" % u], ["ld1"])
-        if t == R - 2:
-            ms(T.cc[:], 0.0, ["cb0", "cb1", "cb2"])
         if not last:
-            cb, pitch = (T.cc, PB) if t == R - 2 else (T.cb, PA)
-            tt(cb[:, 0:129], T.pb[:, AL + 8:AL + 137], T.pc[:, PCR + 8:PCR + 137], A.mult, ["pb", "pcr"], ["cb0"])
+            tt(T.cb[:, 0, 0:129], T.pb[:, AL + 8:AL + 137], T.pc[:, PCR + 8:PCR + 137], A.mult, ["pb", "pcr"], ["cb0"])
             tt(R0[:, 0:129], T.pb[:, AL + 8:AL + 137], T.pc[:, 7:136], A.mult, ["pb", "pcl"], ["e2"])
-        if t > 0:
-            tt(T.lab[0:nm, :], T.lc[0:nm, 144 * u:144 * u + 144], T.ld[0:nm, :], A.subtract,
-               ["lc%d" % t, "lr%d" % t, "ld0", "ld1"], ["lab"])
-        if not last:
-            tt(T.nq[:, 0:129], R0[:, 0:129], cb[:, 0:129], A.not_equal, ["e2", "cb0"], ["nq"])
-            tt(cb[:, pitch + 1:pitch + 130], R0[:, 0:129], T.nq[:, 0:129], A.mult, ["e2", "nq"], ["cb1"])
-            tt(cb[:, 2 * pitch + 1:2 * pitch + 129], R0[:, 1:129], cb[:, pitch + 2:pitch + 130], A.subtract, ["e2", "cb1"], ["cb2"])
+            tt(T.nq[:, 0:129], R0[:, 0:129], T.cb[:, 0, 0:129], A.is_equal, ["e2", "cb0"], ["nq"])
+            tt(T.nn[:], R0[:, 0:128], T.cb[:, 0, 0:128], A.not_equal, ["e2", "cb0"], ["nn"])
+            tt(T.cb[:, 1, 1:129], R0[:, 1:129], T.nq[:, 1:129], A.mult, ["e2", "nq"], ["cb1"])
+            tt(T.cb[:, 2, 1:129], R0[:, 0:128], T.nn[:], A.mult, ["e2", "nn"], ["cb2"])
         if t == 0:
-            ts(T.fst[:], T.jj[:], T.pb[:, 0:1], None, A.is_equal, None, ["jj", "pb"], ["fst"])
-            ms(T.oi[:], 0.0, OI)
-            io(T.oi[:, 1:129], [[0, 128]], 0, ["oi0"], base=1)
+            io(T.nid[:, 0:128], [[1, 128]], 0, ["nid"])
+            slot_masks(1)
+            vectors(range(9, 13))
+            ms(T.yw[:, 0:2048], 0.0, ["yw"])
         if t == 1:
-            io(T.yw[:, 0:1024], [[0, 1024]], 0, ["yw"])
             slot_masks(2)
-            vectors(range(11, 13))
-            act(T.tt[:], T.jj[:, 8:136], 4096.0, -1.0, ["jj"], ["tt"])
-            act(T.pf[:, 8:9], T.jj[:, 135:136], 4095.0, -1.0, ["jj"], ["pf8"])
+            act(T.pf[:, 7:8], fR, 4096.0, -128.0, ["pf"], ["pf7"])
+            act(T.pf[:, 8:9], fR, 4095.0 - 127, -128.0, ["pf"], ["pf8"])
+            vectors(range(13, 14))
+            act(T.tt[:], T.nid[:, 0:128], T.pf[:, 7:8], -1.0, ["nid", "pf7"], ["tt"])
         if t == 2:
             slot_masks(3)
-            vectors(range(13, 16))
-            io(T.yw[:, 1024:2048], [[0, 1024]], 0, ["yw2"])
+            vectors(range(14, 16))
         if last:
             av = T.pb[:, AL + 8:AL + 136]
             scan(T.ss[:, 0:128], av, T.neg[:], T.tt[:, 0:1], A.add, A.add, ["pb", "neg", "tt"], ["ss"])
@@ -449,22 +463,28 @@ def rank_program(g, core, T, topo):
             ts(T.nd[:, 128:129], T.p2[:, 255:256], -1.0, T.pf[:, 8:9], A.mult, A.add, ["p2", "pf8"], ["nd2"])
             tt(T.nd[:, 1:128], T.zz[:, 0:127], T.zz[:, 1:128], A.subtract, ["zz"], ["nd1"])
             ts(T.nd[:, 0:1], T.zz[:, 0:1], -1.0, None, A.mult, None, ["zz"], ["nd0"])
+            for q in range(4):
+                ts(T.v0[:, 12 + q:2048:16], T.e3[:, 128 * q:128 * q + 128], 32.0 + S0 + R - 2, None, A.add, None,
+                   ["e3"], ["v0_%d" % (12 + q)])
 
-        srcs = [(T.pay[0:nm, 16 * t:16 * t + wd], None)]
+        srcs = [(T.pay, 32 * t, None)]
         for c, n in senders:
             s = T.rank_of(c)
-            srcs.append((T.land[0:nm, 16 * (NR * t + s):16 * (NR * t + s) + wd], ("ar%d_%d" % (t, s), n)))
+            srcs.append((T.land, 32 * (NR * t + s), ("ar%d_%d" % (t, s), n)))
         mm(T.p3[:, 0:16], T.repf[0:32, :], T.hs[0:32, :], True, False, ["repf", "hs"], ["p3"])
-        for i, (src, tok) in enumerate(srcs):
+        for i, (src, c0, tok) in enumerate(srcs):
             end = i == len(srcs) - 1
             if tok:
                 need("p", [tok])
             if t == 0:
-                mm(T.p3[:, 0:wd], T.rep[:], src, False, end, ["pay0", "rep"], ["p3"])
-            else:
-                for q in range(0, 128, 32):
-                    mm(T.p3[q:q + wd, 0:16], src, T.lab[0:nm, 128:144], False, False, ["lab", "pay%d" % t], ["p3"])
-                mm(T.p3[:, 0:wd], T.lab[0:nm, 0:128], src, False, end, ["lab"], ["p3"])
+                for k in range(C0):
+                    mm(T.p3[:, 0:NS], T.rep[:, 128 * k:128 * k + 128], src[:, c0 + k:c0 + wd:C0], False, end and k == C0 - 1,
+                       ["pay0", "rep"], ["p3"])
+                continue
+            for q in range(0, 128, 32):
+                mm(T.p3[q:q + wd, 0:NS], src[0:32 + ns, c0:c0 + wd], T.lab[0:32 + ns, 16:16 + NS], False, False,
+                   ["lab", "pay%d" % t], ["p3"])
+                mm(T.p3[q:q + NS, 0:wd], T.lab[0:32 + ns, 0:NS], src[0:32 + ns, c0:c0 + wd], False, end, ["lab"], ["p3"])
         scan(T.sc[:], T.p3[:, 0:48], T.low[:], -1.0e9, A.max, A.max, ["p3", "low"], ["sc"])
         op("v", lambda: V.transpose(T.tr[:, 0:32], T.sc[:, 16:48]), ["sc"], ["tr"])
         scan(T.kk[:, 36 * t:36 * t + 34], T.tr[:, 0:34], T.rnd[:, 0:34], -1.0e9, A.max, A.add,
@@ -474,35 +494,32 @@ def rank_program(g, core, T, topo):
     K, RK = T.kk[:, 36 * u + 31:36 * u + 32], T.kk[:, 36 * u + 33:36 * u + 34]
     ts(T.ee[:, 0:128], T.d1[:, 8:136], RK, K, A.add, A.is_equal, ["d1", "kk3"], ["ee"])
     scan(T.ss[:, 0:129], T.ee[:, 0:129], T.nd[:, 0:129], 0.0, A.add, A.add, ["ee", "eepad", "nd0", "nd1", "nd2"], ["ss"])
+    mm(T.p2[:, 128:256], T.far[:], T.ee[:, 0:128], True, True, ["far", "ee"], ["p2"])
     mm(T.pb[:, 1:2], T.tri[:], T.ss[:, 128:129], True, True, ["tri", "ss"], ["pb"])
-    ts(T.p2[:, 128:256], T.ee[:, 0:128], 4096.0, None, A.mult, None, ["ee"], ["p2"])
     tt(T.zz[:], T.p2[:, 128:256], T.ss[:, 0:128], A.subtract, ["p2", "ss"], ["zz"])
     ts(T.offu[:], T.zz[:], T.pb[:, 1:2], None, A.subtract, None, ["zz", "pb"], ["offu"])
     op("a", lambda: S.activation(T.fw[:, 0:WIN].indirect(T.offu[:, 0:128]), T.v0[:], AF.Silu),
-       ["offu"] + ["v0_%d" % r for r in range(16)], ["fw"])
-    cp(T.yw[:, 0:WIN].indirect(T.offu[:, 0:128]), T.y0[:], ["offu"] + ["y0_%d" % r for r in range(16)], ["yw", "yw2"])
+       ["offu"] + ["v0_%d" % r for r in range(16)], ["fw", "fwz"])
+    cp(T.yw[:, 0:WIN].indirect(T.offu[:, 0:128]), T.y0[:], ["offu"] + ["y0_%d" % r for r in range(16)], ["yw"])
     dma("s", "dft", T.ft[:], T.fw[0:128:16, 0:2048], ["fw"], ["ft"])
-    dma("a", "dout2", T.y[:], T.yw[:, 0:2048], ["yw", "fw"], [])
+    dma("a", "dfu", T.fu[:], T.fw[0:128:16, 4096:WIN], ["fw"], ["fu"])
+    dma("s", "dout", T.y[:], T.yw[:, 0:2048], ["yw"], [])
 
     KR = ["kk%d" % t for t in range(R)]
     mm(T.pb[0:8, 2:3], T.gsel[:], T.ss[:, 128:129], True, True, ["gsel", "ss"], ["pb"])
-    tt(T.nk[:, u:u + 1], RK, K, A.subtract, KR, ["nk3"])
-    ts(T.mgs[0:1, 2:12:3], T.kk[0:1, 33:36 * R:36], 1.0 / 256, 1.0, A.mult, A.add, KR, ["mg2"])
-    ts(T.wa[:, u:u + 1], T.nk[:, u:u + 1], 1.0 / 16, (BASE - 7.5) / 16 + AOFF, A.mult, A.add, ["nk3"], ["a3"])
-    ts(T.mt4[:, 2:3], T.nk[:, u:u + 1], BASE + 16.0, None, A.add, None, ["nk3"], ["c3"])
-    ts(T.fls[0:8, 0:1], T.pb[0:8, 2:3], -1.0, None, A.mult, None, ["pb"], ["fls"])
-    ts(T.wb[:, u:u + 1], T.wa[:, u:u + 1], -16.0, T.nk[:, u:u + 1], A.mult, A.add, ["a3", "nk3"], ["b3"])
-    ts(T.mt4[:, 3:4], T.wa[:, u:u + 1], -1.0, float(AOFF + S0 + R - 1), A.mult, A.add, ["a3"], ["c4"])
-    ts(T.mgs[0:1, 0:12:3], T.wa[0:1, 0:4], float(-AOFF), None, A.add, None, ["a%d" % t for t in range(R)], ["mg0"])
-    ts(T.mgs[0:1, 1:12:3], T.wb[0:1, 0:4], float(BOFF), None, A.add, None, ["b%d" % t for t in range(R)], ["mg1"])
-
-    act(T.fa[:], T.ft[:], -23.5 / 16, 1.0 / 16, ["ft"], ["fa"])
+    act(T.nk[:, u:u + 1], K, RK, -1.0, KR, ["nk3"])
+    act(T.fls[0:8, 0:1], T.pb[0:8, 2:3], 0.0, -1.0, ["pb"], ["fls"])
+    act(T.wa[:, u:u + 1], T.nk[:, u:u + 1], (BASE - 7.5) / 16 + AOFF, 1.0 / 16, ["nk3"], ["a3"])
+    act(T.mgs[0:1, 2:12:3], T.kk[0:1, 33:36 * R:36], 1.0, 1.0 / 256, KR, ["mg2"])
     dma("a", "dout2", T.fl[:], T.fls[0:8, 0:1], ["fls"], [])
+    act(T.wb[0:1, u:u + 1], T.wa[0:1, u:u + 1], T.nk[0:1, u:u + 1], -16.0, ["a3", "nk3"], ["b3"])
+    act(T.mgs[0:1, 0:12:3], T.wa[0:1, :], float(-AOFF), 1.0, ["a%d" % t for t in range(R)], ["mg0"])
+    act(T.mgs[0:1, 1:12:3], T.wb[0:1, :], float(BOFF), 1.0, ["b%d" % t for t in range(R)], ["mg1"])
     dma("a", "dout2", T.mg[:], T.mgs[0:1, 0:12], ["mg0", "mg1", "mg2"], [])
-    ts(T.fb[:], T.ft[:], M23, M23, A.add, A.subtract, ["ft"], ["fb"])
-    ts(T.p2[:, 256:384], T.fb[:], T.mt4[:, 2:3], T.mt4[:, 3:4], A.is_equal, A.mult, ["fb", "c3", "c4"], ["p2"])
-    ts(T.fa[:], T.fa[:], M23, M23, A.add, A.subtract, ["fa"], ["fa"])
-    tt(T.fc[:], T.p2[:, 256:384], T.fa[:], A.add, ["fa", "p2"], ["fc"])
+
+    ts(T.fa[:], T.ft[:], M23, M23 + 32, A.add, A.subtract, ["ft"], ["fa"])
+    ts(T.p2[:, 256:384], T.fu[:], -1.0, float(S0 + R - 1), A.add, A.min, ["fu"], ["p2"])
+    tt(T.fc[:], T.p2[:, 256:384], T.fa[:], A.max, ["fa", "p2"], ["fc"])
     dma("s", "dout", T.fs[:], T.fc[:], ["fc"], [])
 
     need("s", [("dout", count["dout"])])

from concourse.bass import DstId, RemoteDMATransfer
from concourse.mybir import AluOpType as A, ActivationFunctionType as AF

W = 144
R = 4
S0 = 10
NR = 8
WIN = 6144
LOW = -16000000
BASE = 102
C0 = 2
WID = (10 * C0, 10, 11, 12)
P1 = 130
SLOT = {1: (9, 13, 10), 2: (10, 12, 11), 3: (11, 11, 12)}
PITCH = 136
M31 = 1.5 * 2.0 ** 31
M23 = 1.5 * 2.0 ** 23
AOFF = 192
BOFF = BASE + 16 * AOFF

f32, bf, f16, i32, u16 = "float32", "bfloat16", "float16", "int32", "uint16"
SCRATCH = {
    "posi": ("sbuf", [128, 128], i32), "stw": ("sbuf", [128, 512], i32), "lei": ("sbuf", [128, 4], i32),
    "vew": ("sbuf", [128, 8192], bf), "tmpi": ("sbuf", [128, 128], i32),
    "hiu": ("sbuf", [128, 128], u16), "lou": ("sbuf", [128, 128], u16), "pou": ("sbuf", [128, 128], u16),
    "offu": ("sbuf", [128, 128], u16),
    "pin": ("sbuf", [128, 16], i32), "pf": ("sbuf", [128, 24], f32), "lef": ("sbuf", [128, 4], f32),
    "nid": ("sbuf", [128, W], f32), "n31": ("sbuf", [128, 128], bf), "n16": ("sbuf", [128, 32], f32),
    "tm": ("sbuf", [128, 16], bf), "big": ("sbuf", [128, 144], bf), "idn": ("sbuf", [128, 144], bf),
    "sel": ("sbuf", [128, 48], bf), "rows": ("sbuf", [128, 12], f32), "slb": ("sbuf", [128, 4], bf), "aa": ("sbuf", [128, 384], bf),
    "rep": ("sbuf", [128, 384], bf), "tri3": ("sbuf", [128, 384], bf), "repb": ("sbuf", [128, 128], bf), "repf": ("sbuf", [128, 128], f32),
    "dm": ("sbuf", [128, 144], bf), "g8": ("sbuf", [128, 128], f32),
    "onef": ("sbuf", [128, 128], f32), "oneb": ("sbuf", [128, 144], bf), "ec": ("sbuf", [128, 384], bf),
    "tri": ("sbuf", [128, 128], f32), "gsel": ("sbuf", [128, 8], f32),
    "hs": ("sbuf", [128, 16], f32), "ht": ("sbuf", [128, 16], f32),
    "lab": ("sbuf", [128, 32], bf), "lc": ("sbuf", [128, 96], bf), "ld": ("sbuf", [128, 32], bf),
    "cb": ("sbuf", [128, 3, PITCH], bf), "eb": ("sbuf", [128, 3, PITCH], bf),
    "nq": ("sbuf", [128, 136], bf), "nn": ("sbuf", [128, 128], bf),
    "jj": ("sbuf", [128, W], f32), "jt": ("sbuf", [128, 8], f32), "inv": ("sbuf", [128, W], bf),
    "tt": ("sbuf", [128, 128], f32),
    "mk": ("sbuf", [128, 2048], bf), "xx": ("sbuf", [128, 2072], bf),
    "o0": ("sbuf", [128, 10 * P1 + 8], bf), "o1": ("sbuf", [128, 10, 122], bf), "o2": ("sbuf", [128, 11, 122], bf), "o3": ("sbuf", [128, 12, 122], bf),
    "mm": ("sbuf", [128, 48], f16), "pay": ("sbuf", [128, 32 * R], f16), "land": ("sbuf", [128, 32 * NR * R], f16),
    "neg": ("sbuf", [128, 128], bf), "far": ("sbuf", [128, 128], bf), "low": ("sbuf", [128, 48], f32),
    "sc": ("sbuf", [128, 48], f32), "tr": ("sbuf", [128, 36], f32), "rnd": ("sbuf", [128, 36], f32),
    "kk": ("sbuf", [128, 36 * R], f32),
    "fo": ("sbuf", [128, W], bf), "ded": ("sbuf", [128, W], bf),
    "cd": ("sbuf", [128, W], bf), "d1": ("sbuf", [128, W], bf),
    "pc": ("sbuf", [128, 2 * W], bf), "ne": ("sbuf", [128, 2 * W], bf),
    "ee": ("sbuf", [128, 136], bf),
    "ss": ("sbuf", [128, 132], f32), "nd": ("sbuf", [128, 132], f32),
    "zz": ("sbuf", [128, 128], f32),
    "y0": ("sbuf", [128, 2048], bf), "yw": ("sbuf", [128, WIN], bf),
    "v0": ("sbuf", [128, 2048], f32), "fw": ("sbuf", [128, WIN], f32),
    "ft": ("sbuf", [128, 128], f32), "fa": ("sbuf", [128, 128], f32), "fu": ("sbuf", [128, 128], f32),
    "fc": ("sbuf", [128, 128], f32),
    "mgs": ("sbuf", [128, 12], f32), "nk": ("sbuf", [128, 4], f32), "wa": ("sbuf", [128, 4], bf),
    "wb": ("sbuf", [128, 4], f32), "mt4": ("sbuf", [128, 8], f32), "fls": ("sbuf", [128, 4], f32),
    "p1": ("psum", [128, 512], f32), "p2": ("psum", [128, 512], f32), "p3": ("psum", [128, 512], f32),
    "pb": ("psum", [128, 512], f32), "e0": ("psum", [128, 512], f32), "e1": ("psum", [128, 512], f32),
    "e2": ("psum", [128, 512], f32), "e3": ("psum", [128, 512], f32),
}
PSUM = ("p1", "p2", "p3", "pb", "e0", "e1", "e2", "e3")
SEMAPHORES = (["cv", "ca", "cp", "cg", "dpos", "dst", "dle", "dve", "dft", "dfu", "dy", "dz", "dout", "dout2", "sent"]
              + ["ar%d_%d" % (t, s) for t in range(R) for s in range(NR)])


def rank_program(g, core, T, topo):
    rank = T.rank_of(core)
    if rank is None:
        return
    Q = {"v": g.vector, "a": g.scalar, "p": g.tensor, "g": g, "s": g.sync}
    CS = {"v": "cv", "a": "ca", "p": "cp", "g": "cg"}
    count = {k: 0 for k in SEMAPHORES}
    seen = {e: {} for e in Q}
    wrote, read = {}, {}

    def need(e, toks):
        top = {}
        for s, n in toks:
            if n > top.get(s, 0):
                top[s] = n
        for s, n in top.items():
            if e == "p" and s == "cp":
                continue
            if seen[e].get(s, 0) < n:
                Q[e].wait_ge(T.sem[s], n)
                seen[e][s] = n

    def order(e, r, w):
        toks = [wrote[k] for k in list(r) + list(w) if k in wrote]
        for k in w:
            toks += read.get(k, [])
        for k in r:
            if k in PSUM:
                toks += [x for x in read.get(k, []) if x[0] != CS.get(e)]
        need(e, toks)

    def note(tok, r, w):
        for k in r:
            read.setdefault(k, []).append(tok)
        for k in w:
            wrote[k] = tok
            read[k] = []

    def op(e, fn, r, w):
        order(e, r, w)
        s = CS[e]
        fn().then_inc(T.sem[s], 1)
        count[s] += 1
        note((s, count[s]), r, w)

    def dma(e, sem, out, in_, r, w):
        order(e, r, w)
        Q[e].dma_start(out, in_).then_inc(T.sem[sem], 16)
        count[sem] += 16
        note((sem, count[sem]), r, w)

    V, S, P = g.vector, g.scalar, g.tensor

    def ts(out, in0, s1, s2, o0, o1, r, w):
        if o1 is None:
            op("v", lambda: V.tensor_scalar(out, in0, s1, None, o0), r, w)
        else:
            op("v", lambda: V.tensor_scalar(out, in0, s1, s2, o0, o1), r, w)

    def tt(out, in0, in1, o, r, w):
        op("v", lambda: V.tensor_tensor(out, in0, in1, o), r, w)

    def cp(out, in_, r, w):
        op("v", lambda: V.tensor_copy(out, in_), r, w)

    def ms(out, c, w):
        op("v", lambda: V.memset(out, c), [], w)

    def scan(out, d0, d1, init, o0, o1, r, w):
        op("v", lambda: V.tensor_tensor_scan(out, d0, d1, init, o0, o1), r, w)

    def mm(out, l, rh, st, sp, r, w):
        op("p", lambda: P.matmul(out, l, rh, st, sp), r, w)

    def act(out, in_, bias, scale, r, w, fn=AF.Identity):
        op("a", lambda: S.activation(out, in_, fn, bias=bias, scale=scale), r, w)

    def io(out, pat, cm, w, base=0):
        op("g", lambda: g.iota(out, pat, base, cm, allow_small_or_imprecise_dtypes=True), [], w)

    def pick(out, in_, pat, cmp, base, cm, r, w, fill=0.0):
        op("g", lambda: g.affine_select(out, in_, pat, cmp, fill, base, cm), r, w)

    dma("s", "dpos", T.posi[:], T.pos[:], [], ["posi"])
    dma("a", "dst", T.stw[:], T.st[:], [], ["stw"])
    dma("s", "dle", T.lei[0:8, 0:1], T.le[:], [], ["lei"])
    dma("s", "dve", T.vew[:], T.ve[:], [], ["vew"])

    def slot_tables(t):
        np_, ns, _ = SLOT[t]
        u, k = t - 1, "%d" % t
        sel, sk = T.sel[:, 16 * u:16 * u + WID[t]], ["sel" + k]
        pat, neg, one = [[-ns, WID[t]]], [[ns, WID[t]]], [[0, 1]]
        scale = 128
        lc, old = T.lc[0:64, 32 * u:32 * u + 32], T.rows[0:64, u:u + 1]
        left, right = T.lc[0:64, 32 * u:32 * u + 16], T.lc[0:64, 32 * u + 16:32 * u + 32]
        ends = T.sel[:, 16 * u:16 * u + np_ + 1:np_]
        sels = [lambda: io(sel, [[0, WID[t]]], 0, sk, base=-1),
                lambda: pick(sel, sel, pat, A.is_ge, 0, 1, sk, sk, fill=1.0),
                lambda: pick(sel, sel, pat, A.is_ge, ns, 1, sk, sk),
                lambda: pick(sel, sel, neg, A.is_ge, ns - 1, -1, sk, sk),
                lambda: pick(ends, ends, [[0, 2]], A.is_ge, np_ * ns - 1, -1, sk, sk, fill=1.0)]
        io(T.aa[0:ns, 128 * u + np_ * ns:128 * u + np_ * ns + 1], one, 0, ["a1" + k], base=1)
        rest = [lambda: pick(T.aa[0:ns, 128 * u:128 * u + np_ * ns], T.oneb[0:ns, 0:np_ * ns], [[0, np_], [-1, ns]],
                             A.is_equal, 0, 1, ["oneb"], ["aa" + k]),
                lambda: io(lc, [[0, 32]], 0, ["lc" + k, "lr" + k], base=scale),
                lambda: io(old, one, 0, ["old" + k], base=scale),
                lambda: pick(left, left, [[0, 16]], A.is_ge, ns - 1, -1, ["lc" + k], ["lc" + k], fill=float(-scale)),
                lambda: pick(right, right, [[0, 16]], A.is_ge, -32, 1, ["lr" + k], ["lr" + k]),
                lambda: pick(left, left, [[0, 16]], A.is_ge, 2 * ns - 1, -1, ["lc" + k], ["lc" + k]),
                lambda: pick(T.rows[0:32, u:u + 1], T.rows[0:32, u:u + 1], one, A.is_ge, ns - 1, -1, ["old" + k], ["old" + k]),
                lambda: pick(lc, lc, [[0, 2], [1, 16]], A.is_equal, -(S0 + u), 0, ["lc" + k, "lr" + k], ["lc" + k])]
        for i, call in enumerate(rest):
            call()
            if i < len(sels):
                sels[i]()

    def slot_masks(t):
        np_, ns, _ = SLOT[t]
        u, k = t - 1, "%d" % t
        n8 = np_ * ns + 1
        mm(T.e0[0:n8, 0:3 * ns], T.aa[0:ns, 128 * u:128 * u + n8], T.aa[0:ns, 128 * u:128 * u + 3 * ns],
           True, True, ["aa" + k, "a1" + k], ["e0"])
        act(T.dm[0:n8, 48 * u:48 * u + 3 * ns], T.e0[0:n8, 0:3 * ns], 0.0, 1.0, ["e0"], ["dm" + k])

    op("g", lambda: g.iota(T.pin[:], [[-1, 16]], 128, 1), [], ["pin0"])
    io(T.oneb[:], [[0, 144]], 0, ["oneb"], base=1)
    io(T.pf[0:8, 0:1], [[0, 1]], 2048, ["goff"])
    pick(T.big[:], T.oneb[:], [[-16, 9], [1000, 16]], A.is_ge, -15000, 1, ["oneb"], ["big"])
    pick(T.big[:], T.big[:], [[16, 9], [0, 16]], A.is_ge, 15, -1, ["big"], ["big"])
    io(T.onef[:], [[0, 128]], 0, ["onef"], base=1)
    pick(T.g8[0:8, :], T.onef[0:8, :], [[-1, 8], [0, 16]], A.is_equal, 0, 1, ["onef"], ["g8"])
    io(T.jj[:], [[1, W]], 128, ["jj"], base=-8)
    pick(T.repf[0:32, :], T.onef[0:32, :], [[0, 4], [-1, 32]], A.is_equal, 0, 1, ["onef"], ["repf"])
    OH = {t: ["o%d_%d" % (t, x) for x in range(SLOT[t][0] + 1 if t else S0)] for t in range(R)}
    io(T.hs[0:32, :], [[-16, 16]], -1, ["hs"], base=BASE - 256)
    io(T.low[:], [[0, 48]], 0, ["low"], base=LOW)
    pick(T.hs[0:32, :], T.hs[0:32, :], [[-1, 16]], A.not_equal, 0, 1, ["hs"], ["hs"], fill=-1.0e9)
    pick(T.repb[0:32, :], T.oneb[0:32, 0:128], [[0, 4], [-1, 32]], A.is_equal, 0, 1, ["oneb"], ["repb"])
    for c in range(129, P1):
        io(T.o0[:, c:10 * P1:P1], [[0, 10]], 0, ["o0gap%d" % c])
    io(T.o0[:, 10 * P1:10 * P1 + 1], [[0, 1]], 0, ["o0pad"])
    for i in range(C0):
        pick(T.tri3[0:32, 128 * i:128 * i + 128], T.oneb[0:32, 0:128], [[0, 4], [1, 32]], A.is_equal, -i, -C0,
             ["oneb"], ["tri3_%d" % i])
    io(T.rows[0:64, 4:5], [[0, 1]], 0, ["ab4"], base=1)
    io(T.rows[0:64, 5:7], [[0, 2]], 0, ["ab5", "ab6"])
    io(T.n16[0:64, :], [[0, 2], [1, 16]], 0, ["n16", "n16r"], base=AOFF)
    for c, fill in ((4, -16), (5, 1), (6, AOFF + BOFF)):
        pick(T.rows[0:64, c:c + 1], T.rows[0:64, c:c + 1], [[0, 1]], A.is_ge, 31, -1, ["ab%d" % c], ["ab%d" % c],
             fill=float(fill))
    ts(T.pin[:], T.pin[:], 15, None, A.bitwise_and, None, ["pin0"], ["pin0"])
    ms(T.xx[:, 2056:2072], 0.0, ["xpad1"])
    ms(T.xx[:, 0:8], 15.0 / 16, ["xpad0"])
    ts(T.tm[:], T.pin[:], 0.0, None, A.is_equal, None, ["pin0"], ["tm"])
    ms(T.p1[:, 0:32], 0.0, ["p1"])

    ts(T.hiu[:], T.posi[:], -255.5, 1.0 / 512, A.add, A.mult, ["posi"], ["hiu"])
    ts(T.tmpi[:], T.posi[:], 511, None, A.bitwise_and, None, ["posi"], ["tmp1"])
    cuts = [0, 128, 448, 768, 1120, 1440, 1696, 1824, 1952, 2048]
    NC = len(cuts) - 1
    cp(T.mk[:, 0:cuts[1]], T.tm[:, 0:16].indirect(T.hiu[:, 0:cuts[1] // 16]), ["tm", "hiu"], ["mk0"])
    for i in range(1, NC):
        a, b = cuts[i], cuts[i + 1]
        op("a", lambda: S.activation(T.mk[:, a:b], T.tm[:, 0:16].indirect(T.hiu[:, a // 16:b // 16]), AF.Copy),
           ["tm", "hiu"], ["mk%d" % i])
    act(T.fc[:], T.mk[:, 0:128], 0.0, 0.0, ["mk0"], ["fc"], fn=AF.Silu)
    cp(T.lou[:], T.tmpi[:], ["tmp1"], ["lou"])
    ts(T.lef[0:8, 0:1], T.lei[0:8, 0:1], T.pf[0:8, 0:1], None, A.add, None, ["lei", "goff"], ["lef"])
    done_r = 0
    for i in range(NC):
        a, b = cuts[i], cuts[i + 1]
        tt(T.xx[:, 8 + a:8 + b], T.stw[:, 0:512].indirect(T.lou[:, a // 16:b // 16]), T.mk[:, a:b], A.mult,
           ["stw", "lou", "mk%d" % i], ["x%d" % i])
        if i == 3:
            mm(T.pb[:, 0:1], T.g8[0:8, :], T.lef[0:8, 0:1], True, True, ["g8", "lef"], ["pb"])
        while done_r < 16 and (i == NC - 1 or 128 * done_r + W - 8 <= b):
            r = done_r
            c = cuts[-2] + 8 - 128 * r if r == 15 else 0
            mm(T.e0[:, c:W], T.big[:, 15 - r:143 - r], T.xx[:, 128 * r + c:128 * r + W], r == 0, r == 15,
               ["big", "xpad0", "xpad1"] + ["x%d" % k for k in range(i + 1)], ["e0"])
            done_r += 1
        if i == NC - 2:
            mm(T.e0[:, 0:b + 8 - 128 * 15], T.big[:, 0:128], T.xx[:, 128 * 15:b + 8], False, False,
               ["big"] + ["x%d" % k for k in range(i + 1)], ["e0"])
    ts(T.inv[:], T.jj[:], T.pb[:, 0:1], 15.0, A.is_ge, A.mult, ["jj", "pb"], ["inv"])
    tt(T.fo[:], T.e0[:, 0:W], T.inv[:], A.max, ["e0", "inv"], ["fo"])

    cores = list(T.cores)
    chips = []
    for c in cores:
        if topo.chip(c) not in chips:
            chips.append(topo.chip(c))
    on = {ch: [c for c in cores if topo.chip(c) == ch] for ch in chips}

    def one_link(c, x):
        return topo.same_plane(topo.chip(c), topo.chip(x)) or topo.mates(topo.chip(c), topo.chip(x))

    def far_of(c):
        i = chips.index(topo.chip(c))
        m = on[topo.chip(c)].index(c)
        out = []
        for d in range(1, len(chips)):
            row = on[chips[(i + d) % len(chips)]]
            out += [row[(m + k) % len(row)] for k in range(len(row))]
        return sorted(out, key=lambda x: one_link(c, x))

    far = far_of(core)
    near = [c for c in on[topo.chip(core)] if c != core]
    far_eng = [e for e in topo.engines(core, far[0]) if all(e in topo.engines(core, c) for c in far)]
    near_eng = [e for e in topo.engines(core, near[0]) if e not in far_eng][0:4:2]
    senders = [(c, len(near_eng)) for c in near]
    senders += [(c, len(far_eng)) for c in sorted(far, key=lambda c: far_of(c).index(core) + 1.5 * (not one_link(c, core)))]

    def did(c):
        a = topo.addr(c)
        return DstId(rid=a[0], pnc=a[1])

    def vectors(rs):
        for r in rs:
            op("a", lambda: S.activation(T.y0[:, r:2048:16], T.vew[:, 0:8192].indirect(T.pou[:, 8 * r:8 * r + 8]),
                                         AF.Copy), ["vew", "pou"], ["y0_%d" % r])

    def sign_planes(t, off):
        planes, slots, steps = SLOT[t]
        for x in range(planes):
            act(T["o%d" % t][:, :, slots * x:slots * (x + 1)], T.fo[:, 8:8 + slots * steps], off - x - 0.5, 1.0,
                ["fo"], [OH[t][x]], fn=AF.Sign)

    def codes_out(banks):
        for b in banks:
            bank = "e%d" % b
            for q in range(4):
                r = 4 * b + q
                mm(T[bank][:, 128 * q:128 * q + 128], T.idn[:, r:r + 128], T.fo[:, 8:136], True, True,
                   ["idn", "fo"], [bank])
            if b < 3:
                for q in range(4):
                    r = 4 * b + q
                    act(T.v0[:, r:2048:16], T[bank][:, 128 * q:128 * q + 128], 32.0 + S0 + R - 2, 1.0, [bank], ["v0_%d" % r])

    FM, M1 = T.e1[:, 0:W], T.e1[:, 256:256 + W]
    AL = 128
    T16, R0 = T.e3, T.e2
    PCR = W
    fR = T.pf[:, 1:2]
    off = 0
    for t in range(R):
        NS = S0 + t
        last = t == R - 1
        wd = WID[t]
        pay = T.pay[:, 32 * t:32 * t + wd]
        if t == 0:
            act(T.nq[:, 0:129], T.fo[:, 7:136], 1.0 - NS, 1.0, ["fo"], ["nq"], fn=AF.Abs)
            act(T.o0[:, 0:129], T.fo[:, 7:136], 1.0, -1.0, ["fo"], [OH[0][0]], fn=AF.Relu)
            act(T.o0[:, P1 * (NS - 1):P1 * (NS - 1) + 129], T.nq[:, 0:129], 1.0, -1.0, ["nq"], [OH[0][NS - 1]], fn=AF.Relu)
            sign_planes(1, 0)
            for x in range(1, NS - 1):
                ts(T.o0[:, P1 * x:P1 * x + 129], T.fo[:, 7:136], float(x), None, A.is_equal, None, ["fo"], [OH[0][x]])
            step = P1 // C0
            per = -(-step // 4)
            for j in range(step):
                q = 32 * (j // per)
                mm(T.p1[q:q + wd, 0:wd], T.o0[:, j + 1:j + 2 + step * (wd - 1):step], T.o0[:, j:j + 1 + step * (wd - 1):step],
                   j % per == 0, j % per == per - 1 or j == step - 1, OH[0] + ["o0pad"], ["p1"])
            for i in range(C0):
                mm(T.e0[:, 128 * i:128 * i + 128], T.tri3[0:32, 128 * i:128 * i + 128], T.repb[0:32, :], True, True,
                   ["tri3_%d" % i, "repb"], ["e0"])
            act(T.rep[:, 0:128 * C0], T.e0[:, 0:128 * C0], 0.0, 256.0, ["e0"], ["rep"])
            ts(T16[:, 0:W], T.fo[:], -16.0, float(BASE), A.mult, A.add, ["fo"], ["e3"])
            ts(T.pb[:, AL:AL + W], T.inv[:], 0.0, None, A.is_equal, None, ["inv"], ["pb"])
            cp(T.pou[:], T.posi[:], ["posi"], ["pou"])
            ms(T.pc[:, 0:2 * W:2 * W - 1], 0.0, ["pcl", "pcr"])
            cp(pay, T.p1[:, 0:wd], ["p1"], ["pay0"])
            ms(T.cb[:], 0.0, ["cb0", "cb1", "cb2"])
            cp(fR, T.pin[:, 0:1], ["pin0"], ["pf"])
            ms(T.p2[:, 0:16], 0.0, ["p2"])
            vectors(range(0, 9))
        else:
            np_, ns, nc = SLOT[t]
            n8, nm = np_ * ns + 1, 3 * ns
            u = t - 1
            K, RK, KR = T.kk[:, 36 * u + 31:36 * u + 32], T.kk[:, 36 * u + 33:36 * u + 34], ["kk%d" % u]
            if t == 1:
                dma("s", "dy", T.fw[0:128:16, 0:2048], T.fc[:], ["fc"] + KR, ["fw"])
                dma("s", "dz", T.fw[0:128:16, 4096:WIN], T.fc[:], ["fc"], ["fwz"])
            for i, (a, b) in enumerate([(0, 4), (4, nc)]):
                ts(T.eb[:, :, 1 + a * ns:1 + b * ns], T.cb[:, :, 1 + a * ns:1 + b * ns], RK, K, A.add, A.is_equal,
                   ["cb0", "cb1", "cb2"] + KR, ["eb%d" % i])
                for k in range(a, b):
                    mm(T.p1[0:n8, 0:nm], T["o%d" % t][:, k, 0:n8], T.eb[:, :, 1 + k * ns:1 + (k + 1) * ns], k == 0, k == nc - 1,
                       OH[t] + ["eb%d" % i], ["p1"])
            ts(T.ne[:], T.pc[:], RK, K, A.add, A.not_equal, ["pcl", "pcr"] + KR, ["ne"])
            tt(M1, FM, T.ne[:, 0:W], A.mult, ["e1", "ne"], ["e1"])
            tt(T.mm[0:n8, 0:nm], T.p1[0:n8, 0:nm], T.dm[0:n8, 48 * u:48 * u + nm], A.mult, ["p1", "dm%d" % t], ["mm"])
            for lo, a, b in ((0, 0, 2 * ns), (32, 2 * ns, nm)):
                mm(T.p2[lo:lo + b - a, 0:wd], T.mm[0:n8, a:b], T.sel[0:n8, 16 * u:16 * u + wd], True, True,
                   ["mm", "sel%d" % t], ["p2"])
            tt(T.fo[:], M1, T.ne[:, W:2 * W], A.mult, ["e1", "ne"], ["fo"])
            off = NS - 1
            act(T.nk[:, u:u + 1], K, RK, -1.0, KR, ["nk%d" % u])
            act(T.mt4[:, 0:1], RK, 256.0, 1.0, KR, ["r256"])
            act(T.wa[:, u:u + 1], T.nk[:, u:u + 1], (BASE - 7.5) / 16 + AOFF, 1.0 / 16, ["nk%d" % u], ["a%d" % u])
            act(T.mt4[0:64, 1:2], T.nk[0:64, u:u + 1], T.rows[0:64, 6:7], T.rows[0:64, 5:6], ["nk%d" % u, "ab5", "ab6"], ["nkb"])
            act(T.mt4[0:64, 2:3], T.wa[0:64, u:u + 1], T.mt4[0:64, 1:2], T.rows[0:64, 4:5], ["nkb", "ab4", "a%d" % u], ["ab"])
            cp(pay, T.p2[:, 0:wd], ["p2"], ["pay%d" % t])
            tt(T.pb[:, AL:AL + W], T.pb[:, AL:AL + W], T.ne[:, 0:W], A.mult, ["pb", "ne"], ["pb"])
            ts(T.ht[0:32, :], T.p3[0:32, 0:16], T.kk[0:32, 36 * u + 31:36 * u + 32], T.mt4[0:32, 0:1], A.is_equal, A.mult,
               ["p3", "r256"] + KR, ["ht"])
            ts(T.ld[0:64, :], T.n16[0:64, :], T.mt4[0:64, 2:3], T.rows[0:64, u:u + 1], A.is_equal, A.mult,
               ["n16", "n16r", "old%d" % t, "ab"], ["ld"])
            act(T16[:, 0:W], T.fo[:], float(BASE - 17 * off), -16.0, ["fo"], ["e3"])
            act(T.wb[0:1, u:u + 1], T.wa[0:1, u:u + 1], T.nk[0:1, u:u + 1], -16.0, ["a%d" % u, "nk%d" % u], ["b%d" % u])
            if last:
                codes_out([0, 2, 1])
            else:
                act(T.ded[:], T.pb[:, AL:AL + W], 1.0, -1.0, ["pb"], ["ded"])
                act(FM, T.fo[:], float(off - NS), 1.0, ["fo"], ["e1"])
                sign_planes(t + 1, off)

        slot = T.land[:, 32 * (NR * t + rank):32 * (NR * t + rank) + wd]
        order("g", ["pay%d" % t], [])
        sem = T.sem["ar%d_%d" % (t, rank)]
        g.remote_dma_fused([
            RemoteDMATransfer(dst_ids=[did(c) for c in far], dma_engine_mask=sum(1 << e for e in far_eng),
                              remote_sem=sem, srcs=[pay], dsts=[slot for c in far]),
            RemoteDMATransfer(dst_ids=[did(c) for c in near], dma_engine_mask=sum(1 << e for e in near_eng),
                              remote_sem=sem, srcs=[pay], dsts=[slot for c in near]),
        ], local_sem=T.sem.sent)
        count["sent"] += len(far_eng) + len(near_eng)

        if not last:
            planes, slots, steps = SLOT[t + 1]
            io(T["o%d" % (t + 1)][:, :, planes * slots], [[0, steps]], 0, [OH[t + 1][planes]], base=1)
            slot_tables(t + 1)
        if t == 0:
            pick(T.n16[0:64, 0:16], T.n16[0:64, 0:16], [[0, 16]], A.is_ge, 31, -1, ["n16"], ["n16"])
            pick(T.n16[0:64, 16:32], T.n16[0:64, 16:32], [[0, 16]], A.is_ge, -32, 1, ["n16r"], ["n16r"])
            tt(T.pc[:, 1:W], T16[:, 0:W - 1], T.fo[:, 1:W], A.subtract, ["e3", "fo"], ["pcl"])
            tt(T.pc[:, W:2 * W - 1], T16[:, 0:W - 1], T.fo[:, 1:W], A.subtract, ["e3", "fo"], ["pcr"])
            ts(FM, T.fo[:], float(-NS), None, A.add, None, ["fo"], ["e1"])
            ms(T.p3[:, 16:48], -1.0e9, ["p3"])
            ms(T.tr[:, 32:34], -1.0e9, ["trpad"])
            ms(T.rnd[:, 0:32], 0.0, ["rnd0"])
            ms(T.rnd[:, 32:33], M31, ["rnd1"])
            ms(T.rnd[:, 33:34], -M31, ["rnd2"])
        else:
            if t == 1:
                pick(T.idn[:], T.oneb[:], [[-1, 144]], A.is_equal, 0, 1, ["oneb"], ["idn"])
            if t == 2:
                io(T.neg[:], [[0, 128]], 0, ["neg"], base=-1)
                io(T.ee[:, 128:136], [[0, 8]], 0, ["eepad"])
            if last:
                io(T.far[:], [[0, 128]], 0, ["far"], base=4096)
                pick(T.tri[:], T.onef[:], [[1, 128]], A.is_gt, 0, -1, ["onef"], ["tri"])
                pick(T.far[:], T.far[:], [[-1, 128]], A.is_equal, 0, 1, ["far"], ["far"])
                pick(T.gsel[:], T.onef[:, 0:8], [[-16, 8]], A.is_ge, 0, 1, ["onef"], ["gsel"])
                pick(T.tri[:], T.tri[:], [[-16, 8], [0, 16]], A.is_ge, 0, 1, ["tri"], ["tri"])
                pick(T.gsel[:], T.gsel[:], [[16, 8]], A.is_ge, 15, -1, ["gsel"], ["gsel"])
            tt(T.cd[:, 1:W], T16[:, 0:W - 1], T.fo[:, 1:W], A.subtract, ["e3", "fo"], ["cd"])
            tt(T.hs[0:32, :], T.p3[0:32, 0:16], T.ht[0:32, :], A.subtract, ["p3", "ht"], ["hs"])
            if last:
                codes_out([3])
            tt(T.d1[:, 1:W], T.pb[:, AL + 1:AL + W], T.cd[:, 1:W], A.mult, ["cd", "pb"], ["d1"])
            tt(T.lab[0:64, :], T.lc[0:64, 32 * u:32 * u + 32], T.ld[0:64, :], A.subtract, ["lc%d" % t, "ld"], ["lab"])
            if not last:
                scan(T.pc[:, 2 * W - 2:W - 1:-1], T.ded[:, W - 1:0:-1], T.d1[:, W - 1:0:-1], 0.0, A.mult, A.add,
                     ["ded", "d1"], ["pcr"])
                scan(T.pc[:, 1:W], T.ded[:, 1:W], T.d1[:, 1:W], 0.0, A.mult, A.add, ["ded", "d1"], ["pcl"])
        if not last:
            tt(T.cb[:, 0, 0:129], T.pb[:, AL + 8:AL + 137], T.pc[:, PCR + 8:PCR + 137], A.mult, ["pb", "pcr"], ["cb0"])
            tt(R0[:, 0:129], T.pb[:, AL + 8:AL + 137], T.pc[:, 7:136], A.mult, ["pb", "pcl"], ["e2"])
            tt(T.nq[:, 0:129], R0[:, 0:129], T.cb[:, 0, 0:129], A.is_equal, ["e2", "cb0"], ["nq"])
            tt(T.nn[:], R0[:, 0:128], T.cb[:, 0, 0:128], A.not_equal, ["e2", "cb0"], ["nn"])
            tt(T.cb[:, 1, 1:129], R0[:, 1:129], T.nq[:, 1:129], A.mult, ["e2", "nq"], ["cb1"])
            tt(T.cb[:, 2, 1:129], R0[:, 0:128], T.nn[:], A.mult, ["e2", "nn"], ["cb2"])
        if t == 0:
            io(T.nid[:, 0:128], [[1, 128]], 0, ["nid"])
            slot_masks(1)
            vectors(range(9, 13))
            ms(T.yw[:, 0:2048], 0.0, ["yw"])
        if t == 1:
            slot_masks(2)
            act(T.pf[:, 7:8], fR, 4096.0, -128.0, ["pf"], ["pf7"])
            act(T.pf[:, 8:9], fR, 4095.0 - 127, -128.0, ["pf"], ["pf8"])
            vectors(range(13, 14))
            act(T.tt[:], T.nid[:, 0:128], T.pf[:, 7:8], -1.0, ["nid", "pf7"], ["tt"])
        if t == 2:
            slot_masks(3)
            vectors(range(14, 16))
        if last:
            av = T.pb[:, AL + 8:AL + 136]
            scan(T.ss[:, 0:128], av, T.neg[:], T.tt[:, 0:1], A.add, A.add, ["pb", "neg", "tt"], ["ss"])
            tt(T.p2[:, 128:256], av, T.tt[:], A.mult, ["pb", "tt"], ["p2"])
            tt(T.zz[:], T.ss[:, 0:128], T.p2[:, 128:256], A.subtract, ["ss", "p2"], ["zz"])
            ts(T.nd[:, 128:129], T.p2[:, 255:256], -1.0, T.pf[:, 8:9], A.mult, A.add, ["p2", "pf8"], ["nd2"])
            tt(T.nd[:, 1:128], T.zz[:, 0:127], T.zz[:, 1:128], A.subtract, ["zz"], ["nd1"])
            ts(T.nd[:, 0:1], T.zz[:, 0:1], -1.0, None, A.mult, None, ["zz"], ["nd0"])
            for q in range(4):
                ts(T.v0[:, 12 + q:2048:16], T.e3[:, 128 * q:128 * q + 128], 32.0 + S0 + R - 2, None, A.add, None,
                   ["e3"], ["v0_%d" % (12 + q)])

        srcs = [(T.pay, 32 * t, None)]
        for c, n in senders:
            s = T.rank_of(c)
            srcs.append((T.land, 32 * (NR * t + s), ("ar%d_%d" % (t, s), n)))
        mm(T.p3[:, 0:16], T.repf[0:32, :], T.hs[0:32, :], True, False, ["repf", "hs"], ["p3"])
        for i, (src, c0, tok) in enumerate(srcs):
            end = i == len(srcs) - 1
            if tok:
                need("p", [tok])
            if t == 0:
                for k in range(C0):
                    mm(T.p3[:, 0:NS], T.rep[:, 128 * k:128 * k + 128], src[:, c0 + k:c0 + wd:C0], False, end and k == C0 - 1,
                       ["pay0", "rep"], ["p3"])
                continue
            for q in range(0, 128, 32):
                mm(T.p3[q:q + wd, 0:NS], src[0:32 + ns, c0:c0 + wd], T.lab[0:32 + ns, 16:16 + NS], False, False,
                   ["lab", "pay%d" % t], ["p3"])
                mm(T.p3[q:q + NS, 0:wd], T.lab[0:32 + ns, 0:NS], src[0:32 + ns, c0:c0 + wd], False, end, ["lab"], ["p3"])
        scan(T.sc[:], T.p3[:, 0:48], T.low[:], -1.0e9, A.max, A.max, ["p3", "low"], ["sc"])
        op("v", lambda: V.transpose(T.tr[:, 0:32], T.sc[:, 16:48]), ["sc"], ["tr"])
        scan(T.kk[:, 36 * t:36 * t + 34], T.tr[:, 0:34], T.rnd[:, 0:34], -1.0e9, A.max, A.add,
             ["tr", "trpad", "rnd0", "rnd1", "rnd2"], ["kk%d" % t])

    u = R - 1
    K, RK = T.kk[:, 36 * u + 31:36 * u + 32], T.kk[:, 36 * u + 33:36 * u + 34]
    ts(T.ee[:, 0:128], T.d1[:, 8:136], RK, K, A.add, A.is_equal, ["d1", "kk3"], ["ee"])
    scan(T.ss[:, 0:129], T.ee[:, 0:129], T.nd[:, 0:129], 0.0, A.add, A.add, ["ee", "eepad", "nd0", "nd1", "nd2"], ["ss"])
    mm(T.p2[:, 128:256], T.far[:], T.ee[:, 0:128], True, True, ["far", "ee"], ["p2"])
    mm(T.pb[:, 1:2], T.tri[:], T.ss[:, 128:129], True, True, ["tri", "ss"], ["pb"])
    tt(T.zz[:], T.p2[:, 128:256], T.ss[:, 0:128], A.subtract, ["p2", "ss"], ["zz"])
    ts(T.offu[:], T.zz[:], T.pb[:, 1:2], None, A.subtract, None, ["zz", "pb"], ["offu"])
    op("a", lambda: S.activation(T.fw[:, 0:WIN].indirect(T.offu[:, 0:128]), T.v0[:], AF.Silu),
       ["offu"] + ["v0_%d" % r for r in range(16)], ["fw", "fwz"])
    cp(T.yw[:, 0:WIN].indirect(T.offu[:, 0:128]), T.y0[:], ["offu"] + ["y0_%d" % r for r in range(16)], ["yw"])
    dma("s", "dft", T.ft[:], T.fw[0:128:16, 0:2048], ["fw"], ["ft"])
    dma("a", "dfu", T.fu[:], T.fw[0:128:16, 4096:WIN], ["fw"], ["fu"])
    dma("s", "dout", T.y[:], T.yw[:, 0:2048], ["yw"], [])

    KR = ["kk%d" % t for t in range(R)]
    mm(T.pb[0:8, 2:3], T.gsel[:], T.ss[:, 128:129], True, True, ["gsel", "ss"], ["pb"])
    act(T.nk[:, u:u + 1], K, RK, -1.0, KR, ["nk3"])
    act(T.fls[0:8, 0:1], T.pb[0:8, 2:3], 0.0, -1.0, ["pb"], ["fls"])
    act(T.wa[:, u:u + 1], T.nk[:, u:u + 1], (BASE - 7.5) / 16 + AOFF, 1.0 / 16, ["nk3"], ["a3"])
    act(T.mgs[0:1, 2:12:3], T.kk[0:1, 33:36 * R:36], 1.0, 1.0 / 256, KR, ["mg2"])
    dma("a", "dout2", T.fl[:], T.fls[0:8, 0:1], ["fls"], [])
    act(T.wb[0:1, u:u + 1], T.wa[0:1, u:u + 1], T.nk[0:1, u:u + 1], -16.0, ["a3", "nk3"], ["b3"])
    act(T.mgs[0:1, 0:12:3], T.wa[0:1, :], float(-AOFF), 1.0, ["a%d" % t for t in range(R)], ["mg0"])
    act(T.mgs[0:1, 1:12:3], T.wb[0:1, :], float(BOFF), 1.0, ["b%d" % t for t in range(R)], ["mg1"])
    dma("a", "dout2", T.mg[:], T.mgs[0:1, 0:12], ["mg0", "mg1", "mg2"], [])

    ts(T.fa[:], T.ft[:], M23, M23 + 32, A.add, A.subtract, ["ft"], ["fa"])
    ts(T.p2[:, 256:384], T.fu[:], -1.0, float(S0 + R - 1), A.add, A.min, ["fu"], ["p2"])
    tt(T.fc[:], T.p2[:, 256:384], T.fa[:], A.max, ["fa", "p2"], ["fc"])
    dma("s", "dout", T.fs[:], T.fc[:], ["fc"], [])

    need("s", [("dout", count["dout"])])
    need("a", [("dout2", count["dout2"]), ("ca", count["ca"])])
    need("v", [("cv", count["cv"]), ("cp", count["cp"])])
    need("g", [("sent", count["sent"]), ("cg", count["cg"])])
